import numpy as np
import ml_dtypes


def mxq(x, axis, fmt="e4m3"):
    dtype, down = {"e4m3": (ml_dtypes.float8_e4m3fn, 7), "e5m2": (ml_dtypes.float8_e5m2, 14)}[fmt]
    v = np.moveaxis(np.asarray(x, np.float32).astype(ml_dtypes.bfloat16).astype(np.float64), axis, -1)
    blocks = v.reshape(v.shape[:-1] + (-1, 32))
    amax = np.abs(blocks).max(-1, keepdims=True)
    byte = np.maximum(np.where(amax > 0, np.frexp(amax)[1] - 1 + 127, 0) - down, 1)
    scale = np.exp2(byte - 127.0)
    codes = (blocks / scale).astype(np.float32).astype(dtype).astype(np.float64)
    return np.moveaxis((codes * scale).reshape(v.shape), -1, axis)


WIDE = False


def mx_kscale(k):
    if not WIDE:
        return np.ones(k)
    levels = np.array([30, -30])
    if k % 512:
        return np.exp2(np.random.permutation(np.resize(levels, k // 32))).repeat(32)
    a = np.empty((k // 512, 16))
    for p in range(k // 512):
        a[p, :8] = np.random.permutation(np.resize(levels, 8))
        for g in range(8):
            far = levels[np.abs(levels - a[p, g]) >= 10]
            a[p, g + 8] = far[np.random.randint(len(far))]
    return np.exp2(a.ravel()).repeat(32)


def f64(x):
    return np.asarray(x).astype(np.float64)


E2M1 = np.array([0.0, 0.5, 1.0, 1.5, 2.0, 3.0, 4.0, 6.0, -0.0, -0.5, -1.0, -1.5, -2.0, -3.0, -4.0, -6.0])


def pack_weight(w, fmt):
    k, n = w.shape
    w = f64(np.asarray(w, np.float32).astype(ml_dtypes.bfloat16)).reshape(k // 32, 32, n)
    amax = np.abs(w).max(1)
    if fmt == "e4m3":
        byte = np.frexp(amax)[1] - 1 + 127 - 7
    else:
        mant, ex = np.frexp(amax / 6.0)
        byte = np.where(mant > 0.5, ex, ex - 1) + 127
    byte = np.clip(np.where(amax > 0, byte, 1), 1, 254)
    scaled = (w * np.exp2(127.0 - byte)[:, None, :]).reshape(k, n).astype(np.float32)
    by_word = np.ascontiguousarray(scaled.reshape(k // 512, 128, 4, n).transpose(0, 1, 3, 2))
    if fmt == "e4m3":
        words = by_word.astype(ml_dtypes.float8_e4m3fn).view(np.uint8)
    else:
        c = by_word.astype(ml_dtypes.float4_e2m1fn).view(np.uint8) & 0xF
        words = (c[..., 0::2] | (c[..., 1::2] << 4)).reshape(k // 512, 128, 2 * n)
    return np.ascontiguousarray(words), np.ascontiguousarray(byte.astype(np.uint8).reshape(k // 512, 16, n))


def unpack_weight(words, scales, fmt):
    g, _, n = scales.shape
    words = np.ascontiguousarray(words).reshape(g, 128, n, -1)
    if fmt == "e4m3":
        vals = words.view(ml_dtypes.float8_e4m3fn).astype(np.float64)
    else:
        nib = np.empty((g, 128, n, 4), np.uint8)
        nib[..., 0::2] = words & 0xF
        nib[..., 1::2] = words >> 4
        vals = E2M1[nib]
    vals = vals * np.repeat(np.exp2(scales.astype(np.float64) - 127.0), 8, axis=1)[..., None]
    return vals.transpose(0, 1, 3, 2).reshape(g * 512, n)


K, L, M, N = 1024, 512, 1024, 512


def setup_inputs():
    n = np.random.standard_normal
    s = mx_kscale(K)[:, None]
    u = mx_kscale(L)[:, None]
    p_am = pack_weight(n((K, M)) / s, "e4m3")
    p_bm = pack_weight(n((L, N)) / np.sqrt(L) / u, "e4m3")
    return {
        "g": (n((K, L)) / np.sqrt(K) * s * u.T).astype(np.float32),
        "am_words": p_am[0],
        "am_scales": p_am[1],
        "bm_words": p_bm[0],
        "bm_scales": p_bm[1],
        "mom": (n((M, N))).astype(np.float32),
    }


def reference(g, am_words, am_scales, bm_words, bm_scales, mom):
    g_ = mxq(f64(g), 0, "e5m2")
    am_ = unpack_weight(am_words, am_scales, "e4m3")
    h = g_.T @ am_
    h_ = mxq(h, 0, "e5m2")
    bm_ = unpack_weight(bm_words, bm_scales, "e4m3")
    y = h_.T @ bm_
    return 0.9 * f64(mom) + y

@@ -1,0 +1,146 @@
+from contextlib import ExitStack
+
+import concourse.mybir as mybir
+
+K, L, M, N = 1024, 512, 1024, 512
+FLOPS = 2 * K * L * M + 2 * L * M * N
+
+F32 = mybir.dt.float32
+BF16 = mybir.dt.bfloat16
+I32 = mybir.dt.int32
+U32 = mybir.dt.uint32
+U8 = mybir.dt.uint8
+E4M3 = mybir.dt.float8_e4m3fn_x4
+E5M2 = mybir.dt.float8_e5m2_x4
+ALU = mybir.AluOpType
+
+P = 128
+PACK = 4
+BANK = 512
+DECAY = 0.9
+
+
+def tile_mix_kfac_ema_kernel(tc, g, am_words, am_scales, bm_words, bm_scales, mom, out):
+    nc = tc.nc
+    am_rows = am_words.rearrange("a p m i -> p a (m i)").bitcast(I32)
+    bm_rows = bm_words.rearrange("a p n i -> p (a n i)").bitcast(I32)
+
+    with ExitStack() as ctx:
+        sb = ctx.enter_context(tc.tile_pool(name="sb", bufs=1))
+        ps = ctx.enter_context(tc.psum_pool(name="ps", bufs=1))
+        ctx.enter_context(tc.manual_schedule())
+
+        def alloc(name, shape, dtype):
+            return sb.tile(shape, dtype, name=name, align_bytes=64)
+
+        def bank(name, b):
+            return ps.tile([P, BANK], F32, name=name, tag="bank%d" % b)
+
+        am_plane = alloc("am_plane", [P, 2, M], U8)
+        bm_plane = alloc("bm_plane", [P, N], U8)
+        nc.vector.memset(am_plane[:].rearrange("p a m -> p (a m)").bitcast(I32), 0)
+        nc.vector.memset(bm_plane[:].bitcast(I32), 0)
+
+        g_raw = [alloc("g_raw%d" % a, [P, PACK, L], F32) for a in range(2)]
+        am_first = [alloc("am_first%d" % a, [P, BANK], U32) for a in range(2)]
+        am_second = alloc("am_second", [P, 2, BANK], U32)
+        bm_codes = alloc("bm_codes", [P, N], U32)
+        mom_sb = [alloc("mom%d" % u, [P, 2, N], F32) for u in range(4)]
+
+        def load_g(a):
+            nc.sync.dma_start(out=g_raw[a][:], in_=g[512 * a:512 * (a + 1), :].rearrange("(p j) l -> p j l", j=PACK))
+
+        load_g(0)
+        for q in range(4):
+            nc.sync.dma_start(out=am_plane[32 * q:32 * q + 4, :, :].bitcast(I32),
+                              in_=am_scales[:, 4 * q:4 * q + 4, :].rearrange("a r m -> r a m").bitcast(I32))
+        nc.sync.dma_start(out=am_first[0][:].bitcast(I32), in_=am_rows[:, 0, 0:BANK])
+        load_g(1)
+        nc.sync.dma_start(out=am_first[1][:].bitcast(I32), in_=am_rows[:, 1, 0:BANK])
+        nc.sync.dma_start(out=am_second[:].bitcast(I32), in_=am_rows[:, :, BANK:M])
+        for q in range(4):
+            nc.sync.dma_start(out=bm_plane[32 * q:32 * q + 4, :].bitcast(I32),
+                              in_=bm_scales[0, 4 * q:4 * q + 4, :].bitcast(I32))
+        nc.sync.dma_start(out=bm_codes[:].bitcast(I32), in_=bm_rows)
+        for u in range(4):
+            nc.sync.dma_start(out=mom_sb[u][:], in_=mom[2 * P * u:2 * P * (u + 1), :].rearrange("(v p) n -> p v n", p=P))
+
+        g_codes = {}
+        g_planes = {}
+
+        def quantise_g(a):
+            grouped = [alloc("g_grouped%d%d" % (a, w), [P, 2, P, PACK], BF16) for w in range(2)]
+            source = g_raw[a][:].rearrange("p j (c t) -> p c j t", t=PACK)
+            nc.vector.tensor_copy(out=grouped[0][:].rearrange("p t c j -> p c j t"), in_=source[:, :, :, 0:2])
+            nc.scalar.copy(out=grouped[1][:].rearrange("p t c j -> p c j t"), in_=source[:, :, :, 2:4])
+            for w in range(2):
+                codes = alloc("g_codes%d%d" % (a, w), [P, 2 * P], U32)
+                plane = alloc("g_plane%d%d" % (a, w), [P, 2 * P], U8)
+                nc.vector.quantize_mx(out=codes[:].bitcast(E5M2), scales=plane[:],
+                                      in_=grouped[w][:].rearrange("p t c j -> p (t c j)"))
+                for v in range(2):
+                    g_codes[a, 2 * w + v] = codes[:, P * v:P * (v + 1)]
+                    g_planes[a, 2 * w + v] = plane[:, P * v:P * (v + 1)]
+
+        def h_pass(acc, a, half, t):
+            moving = am_first[a][:] if half == 0 else am_second[:, a, :]
+            nc.tensor.matmul_mx(out=acc[:], lhsT=g_codes[a, t].bitcast(E5M2), lhsT_scale=g_planes[a, t],
+                                rhs=moving.bitcast(E4M3), rhs_scale=am_plane[:, a, BANK * half:BANK * (half + 1)],
+                                start=(a == 0), stop=(a == 1))
+
+        h_acc = [[bank("h%d%d" % (half, t), 4 * half + t) for t in range(PACK)] for half in range(2)]
+        h_rows = [alloc("h_rows%d" % half, [P, PACK, BANK], BF16) for half in range(2)]
+        h_grouped = [alloc("h_grouped%d" % u, [P, 2 * P, PACK], BF16) for u in range(4)]
+        h_codes = [alloc("h_codes%d" % u, [P, 2 * P], U32) for u in range(4)]
+        h_planes = [alloc("h_plane%d" % u, [P, 2 * P], U8) for u in range(4)]
+        y_acc = {}
+
+        def interleave_h(copy, u):
+            cols = slice(2 * P * (u % 2), 2 * P * (u % 2 + 1))
+            copy(out=h_grouped[u][:].rearrange("p (c i) t -> p c t i", i=4),
+                 in_=h_rows[u // 2][:, :, cols].rearrange("p t (c i) -> p c t i", i=4))
+
+        def quantise_h(u):
+            nc.vector.quantize_mx(out=h_codes[u][:].bitcast(E5M2), scales=h_planes[u][:],
+                                  in_=h_grouped[u][:].rearrange("p m t -> p (m t)"))
+            for v in range(2):
+                i = 2 * u + v
+                y_acc[i] = bank("y%d" % i, i)
+                nc.tensor.matmul_mx(out=y_acc[i][:], lhsT=h_codes[u][:, P * v:P * (v + 1)].bitcast(E5M2),
+                                    lhsT_scale=h_planes[u][:, P * v:P * (v + 1)],
+                                    rhs=bm_codes[:].bitcast(E4M3), rhs_scale=bm_plane[:], start=True, stop=True)
+
+        def finish(i):
+            result = alloc("result%d" % i, [P, N], F32)
+            nc.vector.scalar_tensor_tensor(out=result[:], in0=mom_sb[i // 2][:, i % 2, :], scalar=DECAY,
+                                           in1=y_acc[i][:], op0=ALU.mult, op1=ALU.add)
+            nc.sync.dma_start(out=out[P * i:P * (i + 1), :], in_=result[:])
+
+        quantise_g(0)
+        for t in range(PACK):
+            h_pass(h_acc[0][t], 0, 0, t)
+        quantise_g(1)
+        for t in range(PACK):
+            h_pass(h_acc[0][t], 1, 0, t)
+            copy = nc.scalar.copy if t % 2 == 0 else nc.vector.tensor_copy
+            copy(out=h_rows[0][:, t, :], in_=h_acc[0][t][:])
+        for t in range(PACK):
+            h_pass(h_acc[1][t], 0, 1, t)
+            h_pass(h_acc[1][t], 1, 1, t)
+            nc.scalar.copy(out=h_rows[1][:, t, :], in_=h_acc[1][t][:])
+        interleave_h(nc.vector.tensor_copy, 0)
+        interleave_h(nc.vector.tensor_copy, 1)
+        interleave_h(nc.scalar.copy, 2)
+        interleave_h(nc.scalar.copy, 3)
+        quantise_h(0)
+        quantise_h(1)
+        finish(0)
+        finish(1)
+        finish(2)
+        quantise_h(2)
+        finish(3)
+        finish(4)
+        quantise_h(3)
+        finish(5)
+        finish(6)
+        finish(7)

@@ -45,25 +45,29 @@ def tile_mix_kfac_ema_kernel(tc, g, am_words, am_scales, bm_words, bm_scales, mo
         am_first = [alloc("am_first%d" % a, [P, BANK], U32) for a in range(2)]
         am_second = alloc("am_second", [P, 2, BANK], U32)
         bm_codes = alloc("bm_codes", [P, N], U32)
-        mom_sb = [alloc("mom%d" % u, [P, 2, N], F32) for u in range(4)]
+        mom_first = [alloc("mom_first%d" % w, [P, 2, N], F32) for w in range(2)]
+        mom_second = alloc("mom_second", [P, 4, N], F32)
+        mom_rows = mom.rearrange("(h p u) n -> h p u n", h=2, u=4)
+        out_rows = out.rearrange("(h p u) n -> h p u n", h=2, u=4)
 
         def load_g(a):
             nc.sync.dma_start(out=g_raw[a][:], in_=g[512 * a:512 * (a + 1), :].rearrange("(p j) l -> p j l", j=PACK))
 
         load_g(0)
-        for q in range(4):
-            nc.sync.dma_start(out=am_plane[32 * q:32 * q + 4, :, :].bitcast(I32),
-                              in_=am_scales[:, 4 * q:4 * q + 4, :].rearrange("a r m -> r a m").bitcast(I32))
+        for r in range(4):
+            nc.sync.dma_start(out=am_plane[r:P:32, :, :].bitcast(I32),
+                              in_=am_scales.rearrange("a (q r) m -> r q a m", r=4)[r].bitcast(I32))
         nc.sync.dma_start(out=am_first[0][:].bitcast(I32), in_=am_rows[:, 0, 0:BANK])
         load_g(1)
         nc.sync.dma_start(out=am_first[1][:].bitcast(I32), in_=am_rows[:, 1, 0:BANK])
         nc.sync.dma_start(out=am_second[:].bitcast(I32), in_=am_rows[:, :, BANK:M])
-        for q in range(4):
-            nc.sync.dma_start(out=bm_plane[32 * q:32 * q + 4, :].bitcast(I32),
-                              in_=bm_scales[0, 4 * q:4 * q + 4, :].bitcast(I32))
+        for r in range(4):
+            nc.sync.dma_start(out=bm_plane[r:P:32, :].bitcast(I32),
+                              in_=bm_scales.rearrange("a (q r) n -> r q (a n)", r=4)[r].bitcast(I32))
         nc.sync.dma_start(out=bm_codes[:].bitcast(I32), in_=bm_rows)
-        for u in range(4):
-            nc.sync.dma_start(out=mom_sb[u][:], in_=mom[2 * P * u:2 * P * (u + 1), :].rearrange("(v p) n -> p v n", p=P))
+        for w in range(2):
+            nc.sync.dma_start(out=mom_first[w][:], in_=mom_rows[0, :, 2 * w:2 * w + 2, :])
+        nc.sync.dma_start(out=mom_second[:], in_=mom_rows[1])
 
         g_codes = {}
         g_planes = {}
@@ -94,6 +98,11 @@ def tile_mix_kfac_ema_kernel(tc, g, am_words, am_scales, bm_words, bm_scales, mo
         h_codes = [alloc("h_codes%d" % u, [P, 2 * P], U32) for u in range(4)]
         h_planes = [alloc("h_plane%d" % u, [P, 2 * P], U8) for u in range(4)]
         y_acc = {}
+        results = [alloc("result%d" % u, [P, 2, N], F32) for u in range(4)]
+
+        def round_h(copy, half, t):
+            copy(out=h_rows[half][:, t, :].rearrange("p (u c) -> p u c", u=4),
+                 in_=h_acc[half][t][:].rearrange("p (c u) -> p u c", u=4))
 
         def interleave_h(copy, u):
             cols = slice(2 * P * (u % 2), 2 * P * (u % 2 + 1))
@@ -111,10 +120,11 @@ def tile_mix_kfac_ema_kernel(tc, g, am_words, am_scales, bm_words, bm_scales, mo
                                     rhs=bm_codes[:].bitcast(E4M3), rhs_scale=bm_plane[:], start=True, stop=True)
 
         def finish(i):
-            result = alloc("result%d" % i, [P, N], F32)
-            nc.vector.scalar_tensor_tensor(out=result[:], in0=mom_sb[i // 2][:, i % 2, :], scalar=DECAY,
+            momentum = mom_first[i // 2][:, i % 2, :] if i < 4 else mom_second[:, i - 4, :]
+            nc.vector.scalar_tensor_tensor(out=results[i // 2][:, i % 2, :], in0=momentum, scalar=DECAY,
                                            in1=y_acc[i][:], op0=ALU.mult, op1=ALU.add)
-            nc.sync.dma_start(out=out[P * i:P * (i + 1), :], in_=result[:])
+            if i % 2 == 1:
+                nc.sync.dma_start(out=out_rows[i // 4, :, i % 4 - 1:i % 4 + 1, :], in_=results[i // 2][:])
 
         quantise_g(0)
         for t in range(PACK):
@@ -122,12 +132,11 @@ def tile_mix_kfac_ema_kernel(tc, g, am_words, am_scales, bm_words, bm_scales, mo
         quantise_g(1)
         for t in range(PACK):
             h_pass(h_acc[0][t], 1, 0, t)
-            copy = nc.scalar.copy if t % 2 == 0 else nc.vector.tensor_copy
-            copy(out=h_rows[0][:, t, :], in_=h_acc[0][t][:])
+            round_h(nc.scalar.copy if t % 2 == 0 else nc.vector.tensor_copy, 0, t)
         for t in range(PACK):
             h_pass(h_acc[1][t], 0, 1, t)
             h_pass(h_acc[1][t], 1, 1, t)
-            nc.scalar.copy(out=h_rows[1][:, t, :], in_=h_acc[1][t][:])
+            round_h(nc.scalar.copy, 1, t)
         interleave_h(nc.vector.tensor_copy, 0)
         interleave_h(nc.vector.tensor_copy, 1)
         interleave_h(nc.scalar.copy, 2)

@@ -18,6 +18,8 @@ P = 128
 PACK = 4
 BANK = 512
 DECAY = 0.9
+SPLITS = (80, 64)
+EARLY = 2
 
 
 def tile_mix_kfac_ema_kernel(tc, g, am_words, am_scales, bm_words, bm_scales, mom, out):
@@ -42,29 +44,32 @@ def tile_mix_kfac_ema_kernel(tc, g, am_words, am_scales, bm_words, bm_scales, mo
         nc.vector.memset(bm_plane[:].bitcast(I32), 0)
 
         g_raw = [alloc("g_raw%d" % a, [P, PACK, L], F32) for a in range(2)]
-        am_first = [alloc("am_first%d" % a, [P, BANK], U32) for a in range(2)]
-        am_second = alloc("am_second", [P, 2, BANK], U32)
+        am_codes = [[alloc("am_codes%d%d" % (a, half), [P, BANK], U32) for half in range(2)] for a in range(2)]
         bm_codes = alloc("bm_codes", [P, N], U32)
         mom_first = [alloc("mom_first%d" % w, [P, 2, N], F32) for w in range(2)]
         mom_second = alloc("mom_second", [P, 4, N], F32)
-        mom_rows = mom.rearrange("(h p u) n -> h p u n", h=2, u=4)
-        out_rows = out.rearrange("(h p u) n -> h p u n", h=2, u=4)
+        mom_rows = mom.rearrange("(h u p) n -> h p u n", h=2, u=4)
+        out_rows = out.rearrange("(h u p) n -> h p u n", h=2, u=4)
 
         def load_g(a):
             nc.sync.dma_start(out=g_raw[a][:], in_=g[512 * a:512 * (a + 1), :].rearrange("(p j) l -> p j l", j=PACK))
+
+        def load_am(a, half):
+            nc.sync.dma_start(out=am_codes[a][half][:].bitcast(I32), in_=am_rows[:, a, BANK * half:BANK * (half + 1)])
 
         load_g(0)
         for r in range(4):
             nc.sync.dma_start(out=am_plane[r:P:32, :, :].bitcast(I32),
                               in_=am_scales.rearrange("a (q r) m -> r q a m", r=4)[r].bitcast(I32))
-        nc.sync.dma_start(out=am_first[0][:].bitcast(I32), in_=am_rows[:, 0, 0:BANK])
+        load_am(0, 0)
         load_g(1)
-        nc.sync.dma_start(out=am_first[1][:].bitcast(I32), in_=am_rows[:, 1, 0:BANK])
-        nc.sync.dma_start(out=am_second[:].bitcast(I32), in_=am_rows[:, :, BANK:M])
+        load_am(0, 1)
+        load_am(1, 0)
+        load_am(1, 1)
+        nc.sync.dma_start(out=bm_codes[:].bitcast(I32), in_=bm_rows)
         for r in range(4):
             nc.sync.dma_start(out=bm_plane[r:P:32, :].bitcast(I32),
                               in_=bm_scales.rearrange("a (q r) n -> r q (a n)", r=4)[r].bitcast(I32))
-        nc.sync.dma_start(out=bm_codes[:].bitcast(I32), in_=bm_rows)
         for w in range(2):
             nc.sync.dma_start(out=mom_first[w][:], in_=mom_rows[0, :, 2 * w:2 * w + 2, :])
         nc.sync.dma_start(out=mom_second[:], in_=mom_rows[1])
@@ -75,8 +80,10 @@ def tile_mix_kfac_ema_kernel(tc, g, am_words, am_scales, bm_words, bm_scales, mo
         def quantise_g(a):
             grouped = [alloc("g_grouped%d%d" % (a, w), [P, 2, P, PACK], BF16) for w in range(2)]
             source = g_raw[a][:].rearrange("p j (c t) -> p c j t", t=PACK)
-            nc.vector.tensor_copy(out=grouped[0][:].rearrange("p t c j -> p c j t"), in_=source[:, :, :, 0:2])
-            nc.scalar.copy(out=grouped[1][:].rearrange("p t c j -> p c j t"), in_=source[:, :, :, 2:4])
+            for w, split in enumerate(SPLITS):
+                target = grouped[w][:].rearrange("p t c j -> p c j t")
+                nc.vector.tensor_copy(out=target[:, :split], in_=source[:, :split, :, 2 * w:2 * w + 2])
+                nc.scalar.copy(out=target[:, split:], in_=source[:, split:, :, 2 * w:2 * w + 2])
             for w in range(2):
                 codes = alloc("g_codes%d%d" % (a, w), [P, 2 * P], U32)
                 plane = alloc("g_plane%d%d" % (a, w), [P, 2 * P], U8)
@@ -87,9 +94,8 @@ def tile_mix_kfac_ema_kernel(tc, g, am_words, am_scales, bm_words, bm_scales, mo
                     g_planes[a, 2 * w + v] = plane[:, P * v:P * (v + 1)]
 
         def h_pass(acc, a, half, t):
-            moving = am_first[a][:] if half == 0 else am_second[:, a, :]
             nc.tensor.matmul_mx(out=acc[:], lhsT=g_codes[a, t].bitcast(E5M2), lhsT_scale=g_planes[a, t],
-                                rhs=moving.bitcast(E4M3), rhs_scale=am_plane[:, a, BANK * half:BANK * (half + 1)],
+                                rhs=am_codes[a][half][:].bitcast(E4M3), rhs_scale=am_plane[:, a, BANK * half:BANK * (half + 1)],
                                 start=(a == 0), stop=(a == 1))
 
         h_acc = [[bank("h%d%d" % (half, t), 4 * half + t) for t in range(PACK)] for half in range(2)]
@@ -100,9 +106,9 @@ def tile_mix_kfac_ema_kernel(tc, g, am_words, am_scales, bm_words, bm_scales, mo
         y_acc = {}
         results = [alloc("result%d" % u, [P, 2, N], F32) for u in range(4)]
 
-        def round_h(copy, half, t):
-            copy(out=h_rows[half][:, t, :].rearrange("p (u c) -> p u c", u=4),
-                 in_=h_acc[half][t][:].rearrange("p (c u) -> p u c", u=4))
+        def round_h(copy, half, t, tiles=slice(0, 4)):
+            copy(out=h_rows[half][:, t, :].rearrange("p (u c) -> p u c", u=4)[:, tiles],
+                 in_=h_acc[half][t][:].rearrange("p (u c) -> p u c", u=4)[:, tiles])
 
         def interleave_h(copy, u):
             cols = slice(2 * P * (u % 2), 2 * P * (u % 2 + 1))
@@ -112,6 +118,8 @@ def tile_mix_kfac_ema_kernel(tc, g, am_words, am_scales, bm_words, bm_scales, mo
         def quantise_h(u):
             nc.vector.quantize_mx(out=h_codes[u][:].bitcast(E5M2), scales=h_planes[u][:],
                                   in_=h_grouped[u][:].rearrange("p m t -> p (m t)"))
+
+        def y_passes(u):
             for v in range(2):
                 i = 2 * u + v
                 y_acc[i] = bank("y%d" % i, i)
@@ -119,37 +127,55 @@ def tile_mix_kfac_ema_kernel(tc, g, am_words, am_scales, bm_words, bm_scales, mo
                                     lhsT_scale=h_planes[u][:, P * v:P * (v + 1)],
                                     rhs=bm_codes[:].bitcast(E4M3), rhs_scale=bm_plane[:], start=True, stop=True)
 
-        def finish(i):
-            momentum = mom_first[i // 2][:, i % 2, :] if i < 4 else mom_second[:, i - 4, :]
-            nc.vector.scalar_tensor_tensor(out=results[i // 2][:, i % 2, :], in0=momentum, scalar=DECAY,
-                                           in1=y_acc[i][:], op0=ALU.mult, op1=ALU.add)
-            if i % 2 == 1:
-                nc.sync.dma_start(out=out_rows[i // 4, :, i % 4 - 1:i % 4 + 1, :], in_=results[i // 2][:])
+        def finish(i, cols=slice(0, N)):
+            momentum = mom_first[i // 2][:, i % 2, cols] if i < 4 else mom_second[:, i - 4, cols]
+            nc.vector.scalar_tensor_tensor(out=results[i // 2][:, i % 2, cols], in0=momentum, scalar=DECAY,
+                                           in1=y_acc[i][:, cols], op0=ALU.mult, op1=ALU.add)
+
+        def store(first, count, cols=slice(0, N)):
+            nc.sync.dma_start(out=out_rows[first // 4, :, first % 4:first % 4 + count, cols],
+                              in_=results[first // 2][:, first % 2:first % 2 + count, cols])
 
         quantise_g(0)
         for t in range(PACK):
             h_pass(h_acc[0][t], 0, 0, t)
         quantise_g(1)
+        for t in range(EARLY):
+            h_pass(h_acc[1][t], 0, 1, t)
         for t in range(PACK):
             h_pass(h_acc[0][t], 1, 0, t)
-            round_h(nc.scalar.copy if t % 2 == 0 else nc.vector.tensor_copy, 0, t)
+            if t < PACK - 1:
+                round_h(nc.scalar.copy if t % 2 == 0 else nc.vector.tensor_copy, 0, t)
+        round_h(nc.vector.tensor_copy, 0, PACK - 1, slice(0, 2))
+        round_h(nc.scalar.copy, 0, PACK - 1, slice(2, 4))
         for t in range(PACK):
-            h_pass(h_acc[1][t], 0, 1, t)
+            if t >= EARLY:
+                h_pass(h_acc[1][t], 0, 1, t)
             h_pass(h_acc[1][t], 1, 1, t)
             round_h(nc.scalar.copy, 1, t)
-        interleave_h(nc.vector.tensor_copy, 0)
-        interleave_h(nc.vector.tensor_copy, 1)
         interleave_h(nc.scalar.copy, 2)
         interleave_h(nc.scalar.copy, 3)
+
+        def finish_and_store(i, cols=slice(0, N)):
+            finish(i, cols)
+            store(i, 1, cols)
+
+        interleave_h(nc.vector.tensor_copy, 0)
         quantise_h(0)
+        y_passes(0)
+        interleave_h(nc.vector.tensor_copy, 1)
+        finish_and_store(0)
         quantise_h(1)
-        finish(0)
-        finish(1)
-        finish(2)
+        y_passes(1)
+        finish_and_store(1)
+        finish_and_store(2)
         quantise_h(2)
-        finish(3)
-        finish(4)
+        y_passes(2)
+        finish_and_store(3)
+        finish_and_store(4)
         quantise_h(3)
-        finish(5)
-        finish(6)
-        finish(7)
+        y_passes(3)
+        finish_and_store(5)
+        finish_and_store(6)
+        finish_and_store(7, slice(0, N // 2))
+        finish_and_store(7, slice(N // 2, N))

@@ -19,7 +19,6 @@ PACK = 4
 BANK = 512
 DECAY = 0.9
 SPLITS = (80, 64)
-EARLY = 2
 
 
 def tile_mix_kfac_ema_kernel(tc, g, am_words, am_scales, bm_words, bm_scales, mom, out):
@@ -38,38 +37,42 @@ def tile_mix_kfac_ema_kernel(tc, g, am_words, am_scales, bm_words, bm_scales, mo
         def bank(name, b):
             return ps.tile([P, BANK], F32, name=name, tag="bank%d" % b)
 
-        am_plane = alloc("am_plane", [P, 2, M], U8)
+        am_planes = [alloc("am_plane%d" % a, [P, M], U8) for a in range(2)]
         bm_plane = alloc("bm_plane", [P, N], U8)
-        nc.vector.memset(am_plane[:].rearrange("p a m -> p (a m)").bitcast(I32), 0)
-        nc.vector.memset(bm_plane[:].bitcast(I32), 0)
+        for plane in am_planes + [bm_plane]:
+            nc.vector.memset(plane[:].bitcast(I32), 0)
 
-        g_raw = [alloc("g_raw%d" % a, [P, PACK, L], F32) for a in range(2)]
+        g_raw = [[alloc("g_raw%d%d" % (a, b), [P, 2, L], F32) for b in range(2)] for a in range(2)]
         am_codes = [[alloc("am_codes%d%d" % (a, half), [P, BANK], U32) for half in range(2)] for a in range(2)]
         bm_codes = alloc("bm_codes", [P, N], U32)
         mom_first = [alloc("mom_first%d" % w, [P, 2, N], F32) for w in range(2)]
         mom_second = alloc("mom_second", [P, 4, N], F32)
-        mom_rows = mom.rearrange("(h u p) n -> h p u n", h=2, u=4)
-        out_rows = out.rearrange("(h u p) n -> h p u n", h=2, u=4)
+        mom_rows = mom.rearrange("(h p u) n -> h p u n", h=2, u=4)
+        out_rows = out.rearrange("(h p u) n -> h p u n", h=2, u=4)
 
         def load_g(a):
-            nc.sync.dma_start(out=g_raw[a][:], in_=g[512 * a:512 * (a + 1), :].rearrange("(p j) l -> p j l", j=PACK))
+            rows = g[512 * a:512 * (a + 1), :].rearrange("(p j) l -> p j l", j=PACK)
+            for b in range(2):
+                nc.sync.dma_start(out=g_raw[a][b][:], in_=rows[:, 2 * b:2 * b + 2, :])
 
         def load_am(a, half):
             nc.sync.dma_start(out=am_codes[a][half][:].bitcast(I32), in_=am_rows[:, a, BANK * half:BANK * (half + 1)])
 
+        def load_scales(plane, rows):
+            for r in range(4):
+                nc.sync.dma_start(out=plane[r:P:32, :].bitcast(I32),
+                                  in_=rows.rearrange("(q r) c -> r q c", r=4)[r].bitcast(I32))
+
         load_g(0)
-        for r in range(4):
-            nc.sync.dma_start(out=am_plane[r:P:32, :, :].bitcast(I32),
-                              in_=am_scales.rearrange("a (q r) m -> r q a m", r=4)[r].bitcast(I32))
+        load_scales(am_planes[0], am_scales[0])
         load_am(0, 0)
         load_g(1)
-        load_am(0, 1)
+        load_scales(am_planes[1], am_scales[1])
         load_am(1, 0)
+        load_am(0, 1)
         load_am(1, 1)
         nc.sync.dma_start(out=bm_codes[:].bitcast(I32), in_=bm_rows)
-        for r in range(4):
-            nc.sync.dma_start(out=bm_plane[r:P:32, :].bitcast(I32),
-                              in_=bm_scales.rearrange("a (q r) n -> r q (a n)", r=4)[r].bitcast(I32))
+        load_scales(bm_plane, bm_scales[0])
         for w in range(2):
             nc.sync.dma_start(out=mom_first[w][:], in_=mom_rows[0, :, 2 * w:2 * w + 2, :])
         nc.sync.dma_start(out=mom_second[:], in_=mom_rows[1])
@@ -79,11 +82,12 @@ def tile_mix_kfac_ema_kernel(tc, g, am_words, am_scales, bm_words, bm_scales, mo
 
         def quantise_g(a):
             grouped = [alloc("g_grouped%d%d" % (a, w), [P, 2, P, PACK], BF16) for w in range(2)]
-            source = g_raw[a][:].rearrange("p j (c t) -> p c j t", t=PACK)
-            for w, split in enumerate(SPLITS):
-                target = grouped[w][:].rearrange("p t c j -> p c j t")
-                nc.vector.tensor_copy(out=target[:, :split], in_=source[:, :split, :, 2 * w:2 * w + 2])
-                nc.scalar.copy(out=target[:, split:], in_=source[:, split:, :, 2 * w:2 * w + 2])
+            for b in range(2):
+                source = g_raw[a][b][:].rearrange("p j (c t) -> p c j t", t=PACK)
+                for w, split in enumerate(SPLITS):
+                    target = grouped[w][:].rearrange("p t c j -> p c j t")[:, :, 2 * b:2 * b + 2, :]
+                    nc.vector.tensor_copy(out=target[:, :split], in_=source[:, :split, :, 2 * w:2 * w + 2])
+                    nc.scalar.copy(out=target[:, split:], in_=source[:, split:, :, 2 * w:2 * w + 2])
             for w in range(2):
                 codes = alloc("g_codes%d%d" % (a, w), [P, 2 * P], U32)
                 plane = alloc("g_plane%d%d" % (a, w), [P, 2 * P], U8)
@@ -95,7 +99,7 @@ def tile_mix_kfac_ema_kernel(tc, g, am_words, am_scales, bm_words, bm_scales, mo
 
         def h_pass(acc, a, half, t):
             nc.tensor.matmul_mx(out=acc[:], lhsT=g_codes[a, t].bitcast(E5M2), lhsT_scale=g_planes[a, t],
-                                rhs=am_codes[a][half][:].bitcast(E4M3), rhs_scale=am_plane[:, a, BANK * half:BANK * (half + 1)],
+                                rhs=am_codes[a][half][:].bitcast(E4M3), rhs_scale=am_planes[a][:, BANK * half:BANK * (half + 1)],
                                 start=(a == 0), stop=(a == 1))
 
         h_acc = [[bank("h%d%d" % (half, t), 4 * half + t) for t in range(PACK)] for half in range(2)]
@@ -108,7 +112,7 @@ def tile_mix_kfac_ema_kernel(tc, g, am_words, am_scales, bm_words, bm_scales, mo
 
         def round_h(copy, half, t, tiles=slice(0, 4)):
             copy(out=h_rows[half][:, t, :].rearrange("p (u c) -> p u c", u=4)[:, tiles],
-                 in_=h_acc[half][t][:].rearrange("p (u c) -> p u c", u=4)[:, tiles])
+                 in_=h_acc[half][t][:].rearrange("p (c u) -> p u c", u=4)[:, tiles])
 
         def interleave_h(copy, u):
             cols = slice(2 * P * (u % 2), 2 * P * (u % 2 + 1))
@@ -140,8 +144,6 @@ def tile_mix_kfac_ema_kernel(tc, g, am_words, am_scales, bm_words, bm_scales, mo
         for t in range(PACK):
             h_pass(h_acc[0][t], 0, 0, t)
         quantise_g(1)
-        for t in range(EARLY):
-            h_pass(h_acc[1][t], 0, 1, t)
         for t in range(PACK):
             h_pass(h_acc[0][t], 1, 0, t)
             if t < PACK - 1:
@@ -149,8 +151,7 @@ def tile_mix_kfac_ema_kernel(tc, g, am_words, am_scales, bm_words, bm_scales, mo
         round_h(nc.vector.tensor_copy, 0, PACK - 1, slice(0, 2))
         round_h(nc.scalar.copy, 0, PACK - 1, slice(2, 4))
         for t in range(PACK):
-            if t >= EARLY:
-                h_pass(h_acc[1][t], 0, 1, t)
+            h_pass(h_acc[1][t], 0, 1, t)
             h_pass(h_acc[1][t], 1, 1, t)
             round_h(nc.scalar.copy, 1, t)
         interleave_h(nc.scalar.copy, 2)

@@ -18,7 +18,7 @@ P = 128
 PACK = 4
 BANK = 512
 DECAY = 0.9
-SPLITS = (80, 64)
+SPLITS = (84, 52)
 
 
 def tile_mix_kfac_ema_kernel(tc, g, am_words, am_scales, bm_words, bm_scales, mom, out):
@@ -37,57 +37,50 @@ def tile_mix_kfac_ema_kernel(tc, g, am_words, am_scales, bm_words, bm_scales, mo
         def bank(name, b):
             return ps.tile([P, BANK], F32, name=name, tag="bank%d" % b)
 
-        am_planes = [alloc("am_plane%d" % a, [P, M], U8) for a in range(2)]
+        am_plane = alloc("am_plane", [P, 2, M], U8)
         bm_plane = alloc("bm_plane", [P, N], U8)
-        for plane in am_planes + [bm_plane]:
-            nc.vector.memset(plane[:].bitcast(I32), 0)
+        nc.vector.memset(am_plane[:].rearrange("p a m -> p (a m)").bitcast(I32), 0)
+        nc.vector.memset(bm_plane[:].bitcast(I32), 0)
 
-        g_raw = [[alloc("g_raw%d%d" % (a, b), [P, 2, L], F32) for b in range(2)] for a in range(2)]
+        g_raw = [alloc("g_raw%d" % a, [P, PACK, L], F32) for a in range(2)]
         am_codes = [[alloc("am_codes%d%d" % (a, half), [P, BANK], U32) for half in range(2)] for a in range(2)]
         bm_codes = alloc("bm_codes", [P, N], U32)
-        mom_first = [alloc("mom_first%d" % w, [P, 2, N], F32) for w in range(2)]
-        mom_second = alloc("mom_second", [P, 4, N], F32)
+        momentum = [alloc("momentum%d" % w, [P, 2, N], F32) for w in range(4)]
         mom_rows = mom.rearrange("(h p u) n -> h p u n", h=2, u=4)
         out_rows = out.rearrange("(h p u) n -> h p u n", h=2, u=4)
 
         def load_g(a):
-            rows = g[512 * a:512 * (a + 1), :].rearrange("(p j) l -> p j l", j=PACK)
-            for b in range(2):
-                nc.sync.dma_start(out=g_raw[a][b][:], in_=rows[:, 2 * b:2 * b + 2, :])
+            nc.sync.dma_start(out=g_raw[a][:], in_=g[512 * a:512 * (a + 1), :].rearrange("(p j) l -> p j l", j=PACK))
 
         def load_am(a, half):
             nc.sync.dma_start(out=am_codes[a][half][:].bitcast(I32), in_=am_rows[:, a, BANK * half:BANK * (half + 1)])
 
-        def load_scales(plane, rows):
-            for r in range(4):
-                nc.sync.dma_start(out=plane[r:P:32, :].bitcast(I32),
-                                  in_=rows.rearrange("(q r) c -> r q c", r=4)[r].bitcast(I32))
-
         load_g(0)
-        load_scales(am_planes[0], am_scales[0])
+        for r in range(4):
+            nc.sync.dma_start(out=am_plane[r:P:32].bitcast(I32),
+                              in_=am_scales.rearrange("a (q r) c -> r q a c", r=4)[r].bitcast(I32))
         load_am(0, 0)
         load_g(1)
-        load_scales(am_planes[1], am_scales[1])
-        load_am(1, 0)
         load_am(0, 1)
+        load_am(1, 0)
         load_am(1, 1)
         nc.sync.dma_start(out=bm_codes[:].bitcast(I32), in_=bm_rows)
-        load_scales(bm_plane, bm_scales[0])
-        for w in range(2):
-            nc.sync.dma_start(out=mom_first[w][:], in_=mom_rows[0, :, 2 * w:2 * w + 2, :])
-        nc.sync.dma_start(out=mom_second[:], in_=mom_rows[1])
+        for r in range(4):
+            nc.sync.dma_start(out=bm_plane[r:P:32, :].bitcast(I32),
+                              in_=bm_scales[0].rearrange("(q r) c -> r q c", r=4)[r].bitcast(I32))
+        for w in range(4):
+            nc.sync.dma_start(out=momentum[w][:], in_=mom_rows[w // 2, :, 2 * (w % 2):2 * (w % 2) + 2, :])
 
         g_codes = {}
         g_planes = {}
 
         def quantise_g(a):
             grouped = [alloc("g_grouped%d%d" % (a, w), [P, 2, P, PACK], BF16) for w in range(2)]
-            for b in range(2):
-                source = g_raw[a][b][:].rearrange("p j (c t) -> p c j t", t=PACK)
-                for w, split in enumerate(SPLITS):
-                    target = grouped[w][:].rearrange("p t c j -> p c j t")[:, :, 2 * b:2 * b + 2, :]
-                    nc.vector.tensor_copy(out=target[:, :split], in_=source[:, :split, :, 2 * w:2 * w + 2])
-                    nc.scalar.copy(out=target[:, split:], in_=source[:, split:, :, 2 * w:2 * w + 2])
+            source = g_raw[a][:].rearrange("p j (c t) -> p c j t", t=PACK)
+            for w, split in enumerate(SPLITS):
+                target = grouped[w][:].rearrange("p t c j -> p c j t")
+                nc.vector.tensor_copy(out=target[:, :split], in_=source[:, :split, :, 2 * w:2 * w + 2])
+                nc.scalar.copy(out=target[:, split:], in_=source[:, split:, :, 2 * w:2 * w + 2])
             for w in range(2):
                 codes = alloc("g_codes%d%d" % (a, w), [P, 2 * P], U32)
                 plane = alloc("g_plane%d%d" % (a, w), [P, 2 * P], U8)
@@ -97,86 +90,89 @@ def tile_mix_kfac_ema_kernel(tc, g, am_words, am_scales, bm_words, bm_scales, mo
                     g_codes[a, 2 * w + v] = codes[:, P * v:P * (v + 1)]
                     g_planes[a, 2 * w + v] = plane[:, P * v:P * (v + 1)]
 
-        def h_pass(acc, a, half, t):
-            nc.tensor.matmul_mx(out=acc[:], lhsT=g_codes[a, t].bitcast(E5M2), lhsT_scale=g_planes[a, t],
-                                rhs=am_codes[a][half][:].bitcast(E4M3), rhs_scale=am_planes[a][:, BANK * half:BANK * (half + 1)],
+        h_acc = [[bank("h%d%d" % (half, t), 4 * half + t) for t in range(PACK)] for half in range(2)]
+
+        def h_pass(a, half, t):
+            nc.tensor.matmul_mx(out=h_acc[half][t][:], lhsT=g_codes[a, t].bitcast(E5M2), lhsT_scale=g_planes[a, t],
+                                rhs=am_codes[a][half][:].bitcast(E4M3),
+                                rhs_scale=am_plane[:, a, BANK * half:BANK * (half + 1)],
                                 start=(a == 0), stop=(a == 1))
 
-        h_acc = [[bank("h%d%d" % (half, t), 4 * half + t) for t in range(PACK)] for half in range(2)]
-        h_rows = [alloc("h_rows%d" % half, [P, PACK, BANK], BF16) for half in range(2)]
-        h_grouped = [alloc("h_grouped%d" % u, [P, 2 * P, PACK], BF16) for u in range(4)]
-        h_codes = [alloc("h_codes%d" % u, [P, 2 * P], U32) for u in range(4)]
-        h_planes = [alloc("h_plane%d" % u, [P, 2 * P], U8) for u in range(4)]
+        h_rows = [alloc("h_rows%d" % half, [P, 4, PACK, P], BF16) for half in range(2)]
+        h_grouped = [alloc("h_grouped%d" % i, [P, P, PACK], BF16) for i in range(8)]
+        h_codes = [alloc("h_codes%d" % i, [P, P], U32) for i in range(8)]
+        h_planes = [alloc("h_plane%d" % i, [P, P], U8) for i in range(8)]
         y_acc = {}
-        results = [alloc("result%d" % u, [P, 2, N], F32) for u in range(4)]
+        results = [alloc("result%d" % w, [P, 2, N], F32) for w in range(4)]
 
         def round_h(copy, half, t, tiles=slice(0, 4)):
-            copy(out=h_rows[half][:, t, :].rearrange("p (u c) -> p u c", u=4)[:, tiles],
+            copy(out=h_rows[half][:, tiles, t, :],
                  in_=h_acc[half][t][:].rearrange("p (c u) -> p u c", u=4)[:, tiles])
 
-        def interleave_h(copy, u):
-            cols = slice(2 * P * (u % 2), 2 * P * (u % 2 + 1))
-            copy(out=h_grouped[u][:].rearrange("p (c i) t -> p c t i", i=4),
-                 in_=h_rows[u // 2][:, :, cols].rearrange("p t (c i) -> p c t i", i=4))
+        def interleave_h(copy, i):
+            copy(out=h_grouped[i][:].rearrange("p (c e) t -> p c t e", e=4),
+                 in_=h_rows[i // 4][:, i % 4].rearrange("p t (c e) -> p c t e", e=4))
 
-        def quantise_h(u):
-            nc.vector.quantize_mx(out=h_codes[u][:].bitcast(E5M2), scales=h_planes[u][:],
-                                  in_=h_grouped[u][:].rearrange("p m t -> p (m t)"))
+        def quantise_h(i):
+            nc.vector.quantize_mx(out=h_codes[i][:].bitcast(E5M2), scales=h_planes[i][:],
+                                  in_=h_grouped[i][:].rearrange("p m t -> p (m t)"))
 
-        def y_passes(u):
-            for v in range(2):
-                i = 2 * u + v
-                y_acc[i] = bank("y%d" % i, i)
-                nc.tensor.matmul_mx(out=y_acc[i][:], lhsT=h_codes[u][:, P * v:P * (v + 1)].bitcast(E5M2),
-                                    lhsT_scale=h_planes[u][:, P * v:P * (v + 1)],
-                                    rhs=bm_codes[:].bitcast(E4M3), rhs_scale=bm_plane[:], start=True, stop=True)
+        def y_pass(i):
+            y_acc[i] = bank("y%d" % i, i)
+            nc.tensor.matmul_mx(out=y_acc[i][:], lhsT=h_codes[i][:].bitcast(E5M2), lhsT_scale=h_planes[i][:],
+                                rhs=bm_codes[:].bitcast(E4M3), rhs_scale=bm_plane[:], start=True, stop=True)
 
-        def finish(i, cols=slice(0, N)):
-            momentum = mom_first[i // 2][:, i % 2, cols] if i < 4 else mom_second[:, i - 4, cols]
-            nc.vector.scalar_tensor_tensor(out=results[i // 2][:, i % 2, cols], in0=momentum, scalar=DECAY,
-                                           in1=y_acc[i][:, cols], op0=ALU.mult, op1=ALU.add)
+        def finish(i):
+            nc.vector.scalar_tensor_tensor(out=results[i // 2][:, i % 2, :], in0=momentum[i // 2][:, i % 2, :], scalar=DECAY,
+                                           in1=y_acc[i][:], op0=ALU.mult, op1=ALU.add)
 
-        def store(first, count, cols=slice(0, N)):
-            nc.sync.dma_start(out=out_rows[first // 4, :, first % 4:first % 4 + count, cols],
-                              in_=results[first // 2][:, first % 2:first % 2 + count, cols])
+        def store(first, count):
+            nc.sync.dma_start(out=out_rows[first // 4, :, first % 4:first % 4 + count, :],
+                              in_=results[first // 2][:, first % 2:first % 2 + count, :])
 
         quantise_g(0)
         for t in range(PACK):
-            h_pass(h_acc[0][t], 0, 0, t)
+            h_pass(0, 0, t)
         quantise_g(1)
+        for t in range(2):
+            h_pass(0, 1, t)
         for t in range(PACK):
-            h_pass(h_acc[0][t], 1, 0, t)
-            if t < PACK - 1:
-                round_h(nc.scalar.copy if t % 2 == 0 else nc.vector.tensor_copy, 0, t)
-        round_h(nc.vector.tensor_copy, 0, PACK - 1, slice(0, 2))
-        round_h(nc.scalar.copy, 0, PACK - 1, slice(2, 4))
+            h_pass(1, 0, t)
+        round_h(nc.vector.tensor_copy, 0, 0)
+        round_h(nc.scalar.copy, 0, 1)
+        for tiles in (slice(0, 2), slice(2, 4)):
+            round_h(nc.vector.tensor_copy, 0, 2, tiles)
+            round_h(nc.scalar.copy, 0, 3, tiles)
         for t in range(PACK):
-            h_pass(h_acc[1][t], 0, 1, t)
-            h_pass(h_acc[1][t], 1, 1, t)
+            if t >= 2:
+                h_pass(0, 1, t)
+            h_pass(1, 1, t)
             round_h(nc.scalar.copy, 1, t)
-        interleave_h(nc.scalar.copy, 2)
-        interleave_h(nc.scalar.copy, 3)
+        for i in range(4, 8):
+            interleave_h(nc.scalar.copy, i)
 
-        def finish_and_store(i, cols=slice(0, N)):
-            finish(i, cols)
-            store(i, 1, cols)
+        def quantise_and_multiply(i):
+            quantise_h(i)
+            y_pass(i)
 
         interleave_h(nc.vector.tensor_copy, 0)
-        quantise_h(0)
-        y_passes(0)
-        interleave_h(nc.vector.tensor_copy, 1)
-        finish_and_store(0)
-        quantise_h(1)
-        y_passes(1)
-        finish_and_store(1)
-        finish_and_store(2)
-        quantise_h(2)
-        y_passes(2)
-        finish_and_store(3)
-        finish_and_store(4)
-        quantise_h(3)
-        y_passes(3)
-        finish_and_store(5)
-        finish_and_store(6)
-        finish_and_store(7, slice(0, N // 2))
-        finish_and_store(7, slice(N // 2, N))
+        for i in range(3):
+            interleave_h(nc.vector.tensor_copy, i + 1)
+            quantise_and_multiply(i)
+        finish(0)
+        quantise_and_multiply(3)
+        finish(1)
+        store(0, 2)
+        finish(2)
+        quantise_and_multiply(4)
+        finish(3)
+        store(2, 2)
+        quantise_and_multiply(5)
+        finish(4)
+        quantise_and_multiply(6)
+        quantise_and_multiply(7)
+        finish(5)
+        store(4, 2)
+        for i in (6, 7):
+            finish(i)
+            store(i, 1)

@@ -122,13 +122,17 @@ def tile_mix_kfac_ema_kernel(tc, g, am_words, am_scales, bm_words, bm_scales, mo
             nc.tensor.matmul_mx(out=y_acc[i][:], lhsT=h_codes[i][:].bitcast(E5M2), lhsT_scale=h_planes[i][:],
                                 rhs=bm_codes[:].bitcast(E4M3), rhs_scale=bm_plane[:], start=True, stop=True)
 
-        def finish(i):
-            nc.vector.scalar_tensor_tensor(out=results[i // 2][:, i % 2, :], in0=momentum[i // 2][:, i % 2, :], scalar=DECAY,
-                                           in1=y_acc[i][:], op0=ALU.mult, op1=ALU.add)
+        def finish(i, cols=slice(0, N)):
+            nc.vector.scalar_tensor_tensor(out=results[i // 2][:, i % 2, cols], in0=momentum[i // 2][:, i % 2, cols],
+                                           scalar=DECAY, in1=y_acc[i][:, cols], op0=ALU.mult, op1=ALU.add)
 
-        def store(first, count):
-            nc.sync.dma_start(out=out_rows[first // 4, :, first % 4:first % 4 + count, :],
-                              in_=results[first // 2][:, first % 2:first % 2 + count, :])
+        def store(first, count, cols=slice(0, N)):
+            nc.sync.dma_start(out=out_rows[first // 4, :, first % 4:first % 4 + count, cols],
+                              in_=results[first // 2][:, first % 2:first % 2 + count, cols])
+
+        def finish_and_store(i, cols=slice(0, N)):
+            finish(i, cols)
+            store(i, 1, cols)
 
         quantise_g(0)
         for t in range(PACK):
@@ -163,16 +167,14 @@ def tile_mix_kfac_ema_kernel(tc, g, am_words, am_scales, bm_words, bm_scales, mo
         quantise_and_multiply(3)
         finish(1)
         store(0, 2)
-        finish(2)
+        finish_and_store(2)
         quantise_and_multiply(4)
-        finish(3)
-        store(2, 2)
+        finish_and_store(3)
         quantise_and_multiply(5)
-        finish(4)
+        finish_and_store(4)
         quantise_and_multiply(6)
         quantise_and_multiply(7)
-        finish(5)
-        store(4, 2)
-        for i in (6, 7):
-            finish(i)
-            store(i, 1)
+        finish_and_store(5)
+        finish_and_store(6)
+        finish_and_store(7, slice(0, N // 2))
+        finish_and_store(7, slice(N // 2, N))

@@ -43,33 +43,33 @@ def tile_mix_kfac_ema_kernel(tc, g, am_words, am_scales, bm_words, bm_scales, mo
         nc.vector.memset(bm_plane[:].bitcast(I32), 0)
 
         g_raw = [alloc("g_raw%d" % a, [P, PACK, L], F32) for a in range(2)]
-        am_codes = [[alloc("am_codes%d%d" % (a, half), [P, BANK], U32) for half in range(2)] for a in range(2)]
+        am_codes = [alloc("am_codes%d" % a, [P, M], U32) for a in range(2)]
         bm_codes = alloc("bm_codes", [P, N], U32)
-        momentum = [alloc("momentum%d" % w, [P, 2, N], F32) for w in range(4)]
+        mom_first = alloc("mom_first", [P, 4, N], F32)
+        mom_second = [alloc("mom_second%d" % w, [P, 2, N], F32) for w in range(2)]
         mom_rows = mom.rearrange("(h p u) n -> h p u n", h=2, u=4)
         out_rows = out.rearrange("(h p u) n -> h p u n", h=2, u=4)
 
         def load_g(a):
             nc.sync.dma_start(out=g_raw[a][:], in_=g[512 * a:512 * (a + 1), :].rearrange("(p j) l -> p j l", j=PACK))
 
-        def load_am(a, half):
-            nc.sync.dma_start(out=am_codes[a][half][:].bitcast(I32), in_=am_rows[:, a, BANK * half:BANK * (half + 1)])
+        def load_am(a):
+            nc.sync.dma_start(out=am_codes[a][:].bitcast(I32), in_=am_rows[:, a, :])
 
         load_g(0)
         for r in range(4):
             nc.sync.dma_start(out=am_plane[r:P:32].bitcast(I32),
                               in_=am_scales.rearrange("a (q r) c -> r q a c", r=4)[r].bitcast(I32))
-        load_am(0, 0)
+        load_am(0)
         load_g(1)
-        load_am(0, 1)
-        load_am(1, 0)
-        load_am(1, 1)
+        load_am(1)
         nc.sync.dma_start(out=bm_codes[:].bitcast(I32), in_=bm_rows)
         for r in range(4):
             nc.sync.dma_start(out=bm_plane[r:P:32, :].bitcast(I32),
                               in_=bm_scales[0].rearrange("(q r) c -> r q c", r=4)[r].bitcast(I32))
-        for w in range(4):
-            nc.sync.dma_start(out=momentum[w][:], in_=mom_rows[w // 2, :, 2 * (w % 2):2 * (w % 2) + 2, :])
+        nc.sync.dma_start(out=mom_first[:], in_=mom_rows[0])
+        for w in range(2):
+            nc.sync.dma_start(out=mom_second[w][:], in_=mom_rows[1, :, 2 * w:2 * w + 2, :])
 
         g_codes = {}
         g_planes = {}
@@ -94,7 +94,7 @@ def tile_mix_kfac_ema_kernel(tc, g, am_words, am_scales, bm_words, bm_scales, mo
 
         def h_pass(a, half, t):
             nc.tensor.matmul_mx(out=h_acc[half][t][:], lhsT=g_codes[a, t].bitcast(E5M2), lhsT_scale=g_planes[a, t],
-                                rhs=am_codes[a][half][:].bitcast(E4M3),
+                                rhs=am_codes[a][:, BANK * half:BANK * (half + 1)].bitcast(E4M3),
                                 rhs_scale=am_plane[:, a, BANK * half:BANK * (half + 1)],
                                 start=(a == 0), stop=(a == 1))
 
@@ -123,7 +123,8 @@ def tile_mix_kfac_ema_kernel(tc, g, am_words, am_scales, bm_words, bm_scales, mo
                                 rhs=bm_codes[:].bitcast(E4M3), rhs_scale=bm_plane[:], start=True, stop=True)
 
         def finish(i, cols=slice(0, N)):
-            nc.vector.scalar_tensor_tensor(out=results[i // 2][:, i % 2, cols], in0=momentum[i // 2][:, i % 2, cols],
+            momentum = mom_first[:, i, cols] if i < 4 else mom_second[i // 2 - 2][:, i % 2, cols]
+            nc.vector.scalar_tensor_tensor(out=results[i // 2][:, i % 2, cols], in0=momentum,
                                            scalar=DECAY, in1=y_acc[i][:, cols], op0=ALU.mult, op1=ALU.add)
 
         def store(first, count, cols=slice(0, N)):
@@ -134,19 +135,23 @@ def tile_mix_kfac_ema_kernel(tc, g, am_words, am_scales, bm_words, bm_scales, mo
             finish(i, cols)
             store(i, 1, cols)
 
+        def quantise_and_multiply(i):
+            quantise_h(i)
+            y_pass(i)
+
         quantise_g(0)
         for t in range(PACK):
             h_pass(0, 0, t)
-        quantise_g(1)
         for t in range(2):
             h_pass(0, 1, t)
+        quantise_g(1)
         for t in range(PACK):
             h_pass(1, 0, t)
         round_h(nc.vector.tensor_copy, 0, 0)
         round_h(nc.scalar.copy, 0, 1)
-        for tiles in (slice(0, 2), slice(2, 4)):
-            round_h(nc.vector.tensor_copy, 0, 2, tiles)
-            round_h(nc.scalar.copy, 0, 3, tiles)
+        round_h(nc.vector.tensor_copy, 0, 2, slice(0, 2))
+        round_h(nc.scalar.copy, 0, 3, slice(0, 1))
+        round_h(nc.scalar.copy, 0, 3, slice(1, 4))
         for t in range(PACK):
             if t >= 2:
                 h_pass(0, 1, t)
@@ -155,26 +160,25 @@ def tile_mix_kfac_ema_kernel(tc, g, am_words, am_scales, bm_words, bm_scales, mo
         for i in range(4, 8):
             interleave_h(nc.scalar.copy, i)
 
-        def quantise_and_multiply(i):
-            quantise_h(i)
-            y_pass(i)
-
         interleave_h(nc.vector.tensor_copy, 0)
-        for i in range(3):
-            interleave_h(nc.vector.tensor_copy, i + 1)
-            quantise_and_multiply(i)
+        round_h(nc.vector.tensor_copy, 0, 2, slice(2, 4))
+        quantise_and_multiply(0)
+        interleave_h(nc.vector.tensor_copy, 1)
+        interleave_h(nc.vector.tensor_copy, 2)
+        quantise_and_multiply(1)
+        interleave_h(nc.vector.tensor_copy, 3)
+        quantise_and_multiply(2)
         finish(0)
         quantise_and_multiply(3)
         finish(1)
         store(0, 2)
-        finish_and_store(2)
+        finish(2)
         quantise_and_multiply(4)
-        finish_and_store(3)
+        finish(3)
+        store(2, 2)
         quantise_and_multiply(5)
         finish_and_store(4)
         quantise_and_multiply(6)
         quantise_and_multiply(7)
-        finish_and_store(5)
-        finish_and_store(6)
-        finish_and_store(7, slice(0, N // 2))
-        finish_and_store(7, slice(N // 2, N))
+        for i in (5, 6, 7):
+            finish_and_store(i)

@@ -43,7 +43,8 @@ def tile_mix_kfac_ema_kernel(tc, g, am_words, am_scales, bm_words, bm_scales, mo
         nc.vector.memset(bm_plane[:].bitcast(I32), 0)
 
         g_raw = [alloc("g_raw%d" % a, [P, PACK, L], F32) for a in range(2)]
-        am_codes = [alloc("am_codes%d" % a, [P, M], U32) for a in range(2)]
+        am_first = [alloc("am_first%d" % a, [P, BANK], U32) for a in range(2)]
+        am_second = alloc("am_second", [P, 2, BANK], U32)
         bm_codes = alloc("bm_codes", [P, N], U32)
         mom_first = alloc("mom_first", [P, 4, N], F32)
         mom_second = [alloc("mom_second%d" % w, [P, 2, N], F32) for w in range(2)]
@@ -53,16 +54,17 @@ def tile_mix_kfac_ema_kernel(tc, g, am_words, am_scales, bm_words, bm_scales, mo
         def load_g(a):
             nc.sync.dma_start(out=g_raw[a][:], in_=g[512 * a:512 * (a + 1), :].rearrange("(p j) l -> p j l", j=PACK))
 
-        def load_am(a):
-            nc.sync.dma_start(out=am_codes[a][:].bitcast(I32), in_=am_rows[:, a, :])
+        def load_am_first(a):
+            nc.sync.dma_start(out=am_first[a][:].bitcast(I32), in_=am_rows[:, a, :BANK])
 
         load_g(0)
         for r in range(4):
             nc.sync.dma_start(out=am_plane[r:P:32].bitcast(I32),
                               in_=am_scales.rearrange("a (q r) c -> r q a c", r=4)[r].bitcast(I32))
-        load_am(0)
+        load_am_first(0)
         load_g(1)
-        load_am(1)
+        load_am_first(1)
+        nc.sync.dma_start(out=am_second[:].bitcast(I32), in_=am_rows[:, :, BANK:])
         nc.sync.dma_start(out=bm_codes[:].bitcast(I32), in_=bm_rows)
         for r in range(4):
             nc.sync.dma_start(out=bm_plane[r:P:32, :].bitcast(I32),
@@ -93,8 +95,9 @@ def tile_mix_kfac_ema_kernel(tc, g, am_words, am_scales, bm_words, bm_scales, mo
         h_acc = [[bank("h%d%d" % (half, t), 4 * half + t) for t in range(PACK)] for half in range(2)]
 
         def h_pass(a, half, t):
+            codes = am_first[a][:] if half == 0 else am_second[:, a, :]
             nc.tensor.matmul_mx(out=h_acc[half][t][:], lhsT=g_codes[a, t].bitcast(E5M2), lhsT_scale=g_planes[a, t],
-                                rhs=am_codes[a][:, BANK * half:BANK * (half + 1)].bitcast(E4M3),
+                                rhs=codes.bitcast(E4M3),
                                 rhs_scale=am_plane[:, a, BANK * half:BANK * (half + 1)],
                                 start=(a == 0), stop=(a == 1))
 
@@ -139,35 +142,33 @@ def tile_mix_kfac_ema_kernel(tc, g, am_words, am_scales, bm_words, bm_scales, mo
             quantise_h(i)
             y_pass(i)
 
+        def second_half(t):
+            h_pass(0, 1, t)
+            h_pass(1, 1, t)
+            round_h(nc.scalar.copy, 1, t)
+
         quantise_g(0)
         for t in range(PACK):
             h_pass(0, 0, t)
-        for t in range(2):
-            h_pass(0, 1, t)
         quantise_g(1)
         for t in range(PACK):
             h_pass(1, 0, t)
         round_h(nc.vector.tensor_copy, 0, 0)
         round_h(nc.scalar.copy, 0, 1)
-        round_h(nc.vector.tensor_copy, 0, 2, slice(0, 2))
-        round_h(nc.scalar.copy, 0, 3, slice(0, 1))
-        round_h(nc.scalar.copy, 0, 3, slice(1, 4))
-        for t in range(PACK):
-            if t >= 2:
-                h_pass(0, 1, t)
-            h_pass(1, 1, t)
-            round_h(nc.scalar.copy, 1, t)
+        for tiles in (slice(0, 2), slice(2, 4)):
+            round_h(nc.vector.tensor_copy, 0, 2, tiles)
+            round_h(nc.scalar.copy, 0, 3, tiles)
+        for t in range(PACK - 1):
+            second_half(t)
+        interleave_h(nc.vector.tensor_copy, 0)
+        interleave_h(nc.vector.tensor_copy, 1)
+        quantise_and_multiply(0)
+        second_half(PACK - 1)
         for i in range(4, 8):
             interleave_h(nc.scalar.copy, i)
-
-        interleave_h(nc.vector.tensor_copy, 0)
-        round_h(nc.vector.tensor_copy, 0, 2, slice(2, 4))
-        quantise_and_multiply(0)
-        interleave_h(nc.vector.tensor_copy, 1)
-        interleave_h(nc.vector.tensor_copy, 2)
-        quantise_and_multiply(1)
-        interleave_h(nc.vector.tensor_copy, 3)
-        quantise_and_multiply(2)
+        for i in (1, 2):
+            interleave_h(nc.vector.tensor_copy, i + 1)
+            quantise_and_multiply(i)
         finish(0)
         quantise_and_multiply(3)
         finish(1)

@@ -1,6 +1,7 @@
 from contextlib import ExitStack
 
 import concourse.mybir as mybir
+from concourse.masks import make_identity
 
 K, L, M, N = 1024, 512, 1024, 512
 FLOPS = 2 * K * L * M + 2 * L * M * N
@@ -43,38 +44,46 @@ def tile_mix_kfac_ema_kernel(tc, g, am_words, am_scales, bm_words, bm_scales, mo
         nc.vector.memset(bm_plane[:].bitcast(I32), 0)
 
         g_raw = [alloc("g_raw%d" % a, [P, PACK, L], F32) for a in range(2)]
-        am_first = [alloc("am_first%d" % a, [P, BANK], U32) for a in range(2)]
-        am_second = alloc("am_second", [P, 2, BANK], U32)
+        am_moving = [alloc("am_moving%d" % a, [P, BANK], U32) for a in range(2)]
+        am_third = [alloc("am_third%d" % a, [P, 2 * P], U32) for a in range(2)]
+        am_fourth = alloc("am_fourth", [P, 2, 2 * P], U32)
         bm_codes = alloc("bm_codes", [P, N], U32)
-        mom_first = alloc("mom_first", [P, 4, N], F32)
-        mom_second = [alloc("mom_second%d" % w, [P, 2, N], F32) for w in range(2)]
-        mom_rows = mom.rearrange("(h p u) n -> h p u n", h=2, u=4)
-        out_rows = out.rearrange("(h p u) n -> h p u n", h=2, u=4)
+        momentum = [alloc("momentum%d" % i, [P, N], F32) for i in range(8)]
+        identity = alloc("identity", [P, P], F32)
+        make_identity(nc, identity[:])
 
         def load_g(a):
             nc.sync.dma_start(out=g_raw[a][:], in_=g[512 * a:512 * (a + 1), :].rearrange("(p j) l -> p j l", j=PACK))
 
-        def load_am_first(a):
-            nc.sync.dma_start(out=am_first[a][:].bitcast(I32), in_=am_rows[:, a, :BANK])
+        def load_am(tile, a, first, count):
+            nc.sync.dma_start(out=tile[:].bitcast(I32), in_=am_rows[:, a, first:first + count])
+
+        def load_momentum(i):
+            nc.sync.dma_start(out=momentum[i][:], in_=mom[P * i:P * (i + 1), :])
 
         load_g(0)
         for r in range(4):
             nc.sync.dma_start(out=am_plane[r:P:32].bitcast(I32),
                               in_=am_scales.rearrange("a (q r) c -> r q a c", r=4)[r].bitcast(I32))
-        load_am_first(0)
+        load_am(am_moving[0], 0, 0, BANK)
         load_g(1)
-        load_am_first(1)
-        nc.sync.dma_start(out=am_second[:].bitcast(I32), in_=am_rows[:, :, BANK:])
+        load_am(am_third[0], 0, BANK, 2 * P)
+        load_am(am_moving[1], 1, 0, BANK)
+        load_am(am_third[1], 1, BANK, 2 * P)
+        load_am(am_fourth, slice(0, 2), BANK + 2 * P, 2 * P)
         nc.sync.dma_start(out=bm_codes[:].bitcast(I32), in_=bm_rows)
+        load_momentum(0)
         for r in range(4):
             nc.sync.dma_start(out=bm_plane[r:P:32, :].bitcast(I32),
                               in_=bm_scales[0].rearrange("(q r) c -> r q c", r=4)[r].bitcast(I32))
-        nc.sync.dma_start(out=mom_first[:], in_=mom_rows[0])
-        for w in range(2):
-            nc.sync.dma_start(out=mom_second[w][:], in_=mom_rows[1, :, 2 * w:2 * w + 2, :])
+        for i in range(1, 8):
+            load_momentum(i)
 
-        g_codes = {}
-        g_planes = {}
+        g_codes = [alloc("g_codes%d" % a, [P, L], U32) for a in range(2)]
+        g_planes = [alloc("g_plane%d" % a, [P, L], U8) for a in range(2)]
+
+        def columns(j):
+            return slice(P * j, P * (j + 1))
 
         def quantise_g(a):
             grouped = [alloc("g_grouped%d%d" % (a, w), [P, 2, P, PACK], BF16) for w in range(2)]
@@ -83,38 +92,53 @@ def tile_mix_kfac_ema_kernel(tc, g, am_words, am_scales, bm_words, bm_scales, mo
                 target = grouped[w][:].rearrange("p t c j -> p c j t")
                 nc.vector.tensor_copy(out=target[:, :split], in_=source[:, :split, :, 2 * w:2 * w + 2])
                 nc.scalar.copy(out=target[:, split:], in_=source[:, split:, :, 2 * w:2 * w + 2])
-            for w in range(2):
-                codes = alloc("g_codes%d%d" % (a, w), [P, 2 * P], U32)
-                plane = alloc("g_plane%d%d" % (a, w), [P, 2 * P], U8)
-                nc.vector.quantize_mx(out=codes[:].bitcast(E5M2), scales=plane[:],
-                                      in_=grouped[w][:].rearrange("p t c j -> p (t c j)"))
-                for v in range(2):
-                    g_codes[a, 2 * w + v] = codes[:, P * v:P * (v + 1)]
-                    g_planes[a, 2 * w + v] = plane[:, P * v:P * (v + 1)]
+            for t in range(PACK):
+                nc.vector.quantize_mx(out=g_codes[a][:, columns(t)].bitcast(E5M2), scales=g_planes[a][:, columns(t)],
+                                      in_=grouped[t // 2][:, t % 2].rearrange("p c j -> p (c j)"))
 
-        h_acc = [[bank("h%d%d" % (half, t), 4 * half + t) for t in range(PACK)] for half in range(2)]
+        h_acc = [bank("h%d" % t, t) for t in range(PACK)]
+        ht_acc = {i: bank("ht%d" % i, i) for i in range(4, 8)}
 
-        def h_pass(a, half, t):
-            codes = am_first[a][:] if half == 0 else am_second[:, a, :]
-            nc.tensor.matmul_mx(out=h_acc[half][t][:], lhsT=g_codes[a, t].bitcast(E5M2), lhsT_scale=g_planes[a, t],
-                                rhs=codes.bitcast(E4M3),
-                                rhs_scale=am_plane[:, a, BANK * half:BANK * (half + 1)],
+        def h_pass(a, t):
+            nc.tensor.matmul_mx(out=h_acc[t][:], lhsT=g_codes[a][:, columns(t)].bitcast(E5M2),
+                                lhsT_scale=g_planes[a][:, columns(t)],
+                                rhs=am_moving[a][:].bitcast(E4M3), rhs_scale=am_plane[:, a, :BANK],
                                 start=(a == 0), stop=(a == 1))
 
-        h_rows = [alloc("h_rows%d" % half, [P, 4, PACK, P], BF16) for half in range(2)]
+        def ht_pass(a, i):
+            codes = am_third[a][:, columns(i - 4)] if i < 6 else am_fourth[:, a, columns(i - 6)]
+            nc.tensor.matmul_mx(out=ht_acc[i][:], lhsT=codes.bitcast(E4M3), lhsT_scale=am_plane[:, a, columns(i)],
+                                rhs=g_codes[a][:].bitcast(E5M2), rhs_scale=g_planes[a][:],
+                                start=(a == 0), stop=(a == 1))
+
+        h_rows = alloc("h_rows", [P, 4, PACK, P], BF16)
+        ht_pairs = {i: alloc("ht_pairs%d" % i, [P, 2, P, 2], BF16) for i in range(4, 8)}
         h_grouped = [alloc("h_grouped%d" % i, [P, P, PACK], BF16) for i in range(8)]
         h_codes = [alloc("h_codes%d" % i, [P, P], U32) for i in range(8)]
         h_planes = [alloc("h_plane%d" % i, [P, P], U8) for i in range(8)]
+        turned = {}
         y_acc = {}
-        results = [alloc("result%d" % w, [P, 2, N], F32) for w in range(4)]
+        results = [alloc("result%d" % i, [P, N], F32) for i in range(8)]
 
-        def round_h(copy, half, t, tiles=slice(0, 4)):
-            copy(out=h_rows[half][:, tiles, t, :],
-                 in_=h_acc[half][t][:].rearrange("p (c u) -> p u c", u=4)[:, tiles])
+        def round_h(copy, t, tiles=slice(0, 4)):
+            copy(out=h_rows[:, tiles, t, :], in_=h_acc[t][:].rearrange("p (u c) -> p u c", u=4)[:, tiles])
 
         def interleave_h(copy, i):
             copy(out=h_grouped[i][:].rearrange("p (c e) t -> p c t e", e=4),
-                 in_=h_rows[i // 4][:, i % 4].rearrange("p t (c e) -> p c t e", e=4))
+                 in_=h_rows[:, i].rearrange("p t (c e) -> p c t e", e=4))
+
+        def round_ht(i):
+            nc.scalar.copy(out=ht_pairs[i][:], in_=ht_acc[i][:].rearrange("p (v e c) -> p v c e", v=2, e=2))
+
+        def turn_ht(i):
+            turned[i] = ps.tile([P, 2, P], F32, name="turned%d" % i, tag="bank%d" % i)
+            words = ht_pairs[i][:].rearrange("p v c e -> p (v c e)").bitcast(F32)
+            for v in range(2):
+                nc.tensor.transpose(turned[i][:, v, :], words[:, columns(v)], identity[:])
+
+        def gather_words(i):
+            nc.scalar.copy(out=h_grouped[i][:].rearrange("p m t -> p (m t)").bitcast(F32).rearrange("p (m v) -> p m v", v=2),
+                           in_=turned[i][:].rearrange("p v m -> p m v"))
 
         def quantise_h(i):
             nc.vector.quantize_mx(out=h_codes[i][:].bitcast(E5M2), scales=h_planes[i][:],
@@ -125,61 +149,55 @@ def tile_mix_kfac_ema_kernel(tc, g, am_words, am_scales, bm_words, bm_scales, mo
             nc.tensor.matmul_mx(out=y_acc[i][:], lhsT=h_codes[i][:].bitcast(E5M2), lhsT_scale=h_planes[i][:],
                                 rhs=bm_codes[:].bitcast(E4M3), rhs_scale=bm_plane[:], start=True, stop=True)
 
-        def finish(i, cols=slice(0, N)):
-            momentum = mom_first[:, i, cols] if i < 4 else mom_second[i // 2 - 2][:, i % 2, cols]
-            nc.vector.scalar_tensor_tensor(out=results[i // 2][:, i % 2, cols], in0=momentum,
-                                           scalar=DECAY, in1=y_acc[i][:, cols], op0=ALU.mult, op1=ALU.add)
+        def finish_and_store(i):
+            nc.vector.scalar_tensor_tensor(out=results[i][:], in0=momentum[i][:], scalar=DECAY, in1=y_acc[i][:],
+                                           op0=ALU.mult, op1=ALU.add)
+            nc.sync.dma_start(out=out[P * i:P * (i + 1), :], in_=results[i][:])
 
-        def store(first, count, cols=slice(0, N)):
-            nc.sync.dma_start(out=out_rows[first // 4, :, first % 4:first % 4 + count, cols],
-                              in_=results[first // 2][:, first % 2:first % 2 + count, cols])
+        def ht_tile(i):
+            ht_pass(0, i)
+            ht_pass(1, i)
 
-        def finish_and_store(i, cols=slice(0, N)):
-            finish(i, cols)
-            store(i, 1, cols)
-
-        def quantise_and_multiply(i):
+        def multiply(i):
             quantise_h(i)
             y_pass(i)
 
-        def second_half(t):
-            h_pass(0, 1, t)
-            h_pass(1, 1, t)
-            round_h(nc.scalar.copy, 1, t)
-
         quantise_g(0)
         for t in range(PACK):
-            h_pass(0, 0, t)
+            h_pass(0, t)
         quantise_g(1)
+        for i in (4, 5):
+            ht_pass(0, i)
         for t in range(PACK):
-            h_pass(1, 0, t)
-        round_h(nc.vector.tensor_copy, 0, 0)
-        round_h(nc.scalar.copy, 0, 1)
-        for tiles in (slice(0, 2), slice(2, 4)):
-            round_h(nc.vector.tensor_copy, 0, 2, tiles)
-            round_h(nc.scalar.copy, 0, 3, tiles)
-        for t in range(PACK - 1):
-            second_half(t)
-        interleave_h(nc.vector.tensor_copy, 0)
-        interleave_h(nc.vector.tensor_copy, 1)
-        quantise_and_multiply(0)
-        second_half(PACK - 1)
+            h_pass(1, t)
+        for i in (4, 5):
+            ht_pass(1, i)
+        for i in (6, 7):
+            ht_tile(i)
+        round_h(nc.vector.tensor_copy, 0)
+        round_h(nc.scalar.copy, 1)
+        round_h(nc.vector.tensor_copy, 2, slice(0, 2))
+        round_h(nc.vector.tensor_copy, 2, slice(2, 4))
+        round_h(nc.scalar.copy, 3, slice(0, 1))
+        round_h(nc.scalar.copy, 3, slice(1, 4))
         for i in range(4, 8):
-            interleave_h(nc.scalar.copy, i)
-        for i in (1, 2):
+            round_ht(i)
+        interleave_h(nc.vector.tensor_copy, 0)
+        for i in range(3):
             interleave_h(nc.vector.tensor_copy, i + 1)
-            quantise_and_multiply(i)
-        finish(0)
-        quantise_and_multiply(3)
-        finish(1)
-        store(0, 2)
-        finish(2)
-        quantise_and_multiply(4)
-        finish(3)
-        store(2, 2)
-        quantise_and_multiply(5)
-        finish_and_store(4)
-        quantise_and_multiply(6)
-        quantise_and_multiply(7)
+            quantise_h(i)
+            if i == 2:
+                turn_ht(4)
+                turn_ht(5)
+            y_pass(i)
+        finish_and_store(0)
+        multiply(3)
+        turn_ht(6)
+        turn_ht(7)
+        for i in range(4, 8):
+            gather_words(i)
+        for i in range(4, 8):
+            finish_and_store(i - 3)
+            multiply(i)
         for i in (5, 6, 7):
             finish_and_store(i)

@@ -45,10 +45,16 @@ def tile_mix_kfac_ema_kernel(tc, g, am_words, am_scales, bm_words, bm_scales, mo
 
         g_raw = [alloc("g_raw%d" % a, [P, PACK, L], F32) for a in range(2)]
         am_moving = [alloc("am_moving%d" % a, [P, BANK], U32) for a in range(2)]
-        am_third = [alloc("am_third%d" % a, [P, 2 * P], U32) for a in range(2)]
-        am_fourth = alloc("am_fourth", [P, 2, 2 * P], U32)
+        am_third = alloc("am_third", [P, 2 * P], U32)
+        am_fourth = alloc("am_fourth", [P, 2 * P], U32)
+        am_late = alloc("am_late", [P, BANK], U32)
         bm_codes = alloc("bm_codes", [P, N], U32)
-        momentum = [alloc("momentum%d" % i, [P, N], F32) for i in range(8)]
+        mom_first = [alloc("mom_first%d" % q, [P, 2, N], F32) for q in range(2)]
+        mom_second = alloc("mom_second", [P, 2, 2 * N], F32)
+        momentum = [mom_first[i // 2][:, i % 2] for i in range(4)]
+        momentum.extend(mom_second[:, i // 2, N * (i % 2):N * (i % 2 + 1)] for i in range(4))
+        out_rows = [out[:BANK].rearrange("(p u) n -> p u n", u=4)[:, u] for u in range(4)]
+        out_rows.extend(out[BANK:].rearrange("(q p u) n -> p q u n", q=2, u=2)[:, i // 2, i % 2] for i in range(4))
         identity = alloc("identity", [P, P], F32)
         make_identity(nc, identity[:])
 
@@ -58,26 +64,23 @@ def tile_mix_kfac_ema_kernel(tc, g, am_words, am_scales, bm_words, bm_scales, mo
         def load_am(tile, a, first, count):
             nc.sync.dma_start(out=tile[:].bitcast(I32), in_=am_rows[:, a, first:first + count])
 
-        def load_momentum(i):
-            nc.sync.dma_start(out=momentum[i][:], in_=mom[P * i:P * (i + 1), :])
-
         load_g(0)
         for r in range(4):
             nc.sync.dma_start(out=am_plane[r:P:32].bitcast(I32),
                               in_=am_scales.rearrange("a (q r) c -> r q a c", r=4)[r].bitcast(I32))
         load_am(am_moving[0], 0, 0, BANK)
         load_g(1)
-        load_am(am_third[0], 0, BANK, 2 * P)
+        load_am(am_third, 0, BANK, 2 * P)
         load_am(am_moving[1], 1, 0, BANK)
-        load_am(am_third[1], 1, BANK, 2 * P)
-        load_am(am_fourth, slice(0, 2), BANK + 2 * P, 2 * P)
-        nc.sync.dma_start(out=bm_codes[:].bitcast(I32), in_=bm_rows)
-        load_momentum(0)
         for r in range(4):
             nc.sync.dma_start(out=bm_plane[r:P:32, :].bitcast(I32),
                               in_=bm_scales[0].rearrange("(q r) c -> r q c", r=4)[r].bitcast(I32))
-        for i in range(1, 8):
-            load_momentum(i)
+        load_am(am_late, 1, BANK, BANK)
+        load_am(am_fourth, 0, BANK + 2 * P, 2 * P)
+        nc.sync.dma_start(out=bm_codes[:].bitcast(I32), in_=bm_rows)
+        for q in range(2):
+            nc.sync.dma_start(out=mom_first[q][:], in_=mom[:BANK].rearrange("(p u) n -> p u n", u=4)[:, 2 * q:2 * q + 2])
+        nc.sync.dma_start(out=mom_second[:], in_=mom[BANK:].rearrange("(q p u) n -> p q (u n)", q=2, u=2))
 
         g_codes = [alloc("g_codes%d" % a, [P, L], U32) for a in range(2)]
         g_planes = [alloc("g_plane%d" % a, [P, L], U8) for a in range(2)]
@@ -106,7 +109,10 @@ def tile_mix_kfac_ema_kernel(tc, g, am_words, am_scales, bm_words, bm_scales, mo
                                 start=(a == 0), stop=(a == 1))
 
         def ht_pass(a, i):
-            codes = am_third[a][:, columns(i - 4)] if i < 6 else am_fourth[:, a, columns(i - 6)]
+            if a == 1:
+                codes = am_late[:, columns(i - 4)]
+            else:
+                codes = am_third[:, columns(i - 4)] if i < 6 else am_fourth[:, columns(i - 6)]
             nc.tensor.matmul_mx(out=ht_acc[i][:], lhsT=codes.bitcast(E4M3), lhsT_scale=am_plane[:, a, columns(i)],
                                 rhs=g_codes[a][:].bitcast(E5M2), rhs_scale=g_planes[a][:],
                                 start=(a == 0), stop=(a == 1))
@@ -121,7 +127,7 @@ def tile_mix_kfac_ema_kernel(tc, g, am_words, am_scales, bm_words, bm_scales, mo
         results = [alloc("result%d" % i, [P, N], F32) for i in range(8)]
 
         def round_h(copy, t, tiles=slice(0, 4)):
-            copy(out=h_rows[:, tiles, t, :], in_=h_acc[t][:].rearrange("p (u c) -> p u c", u=4)[:, tiles])
+            copy(out=h_rows[:, tiles, t, :], in_=h_acc[t][:].rearrange("p (c u) -> p u c", u=4)[:, tiles])
 
         def interleave_h(copy, i):
             copy(out=h_grouped[i][:].rearrange("p (c e) t -> p c t e", e=4),
@@ -130,29 +136,31 @@ def tile_mix_kfac_ema_kernel(tc, g, am_words, am_scales, bm_words, bm_scales, mo
         def round_ht(i):
             nc.scalar.copy(out=ht_pairs[i][:], in_=ht_acc[i][:].rearrange("p (v e c) -> p v c e", v=2, e=2))
 
-        def turn_ht(i):
-            turned[i] = ps.tile([P, 2, P], F32, name="turned%d" % i, tag="bank%d" % i)
-            words = ht_pairs[i][:].rearrange("p v c e -> p (v c e)").bitcast(F32)
-            for v in range(2):
-                nc.tensor.transpose(turned[i][:, v, :], words[:, columns(v)], identity[:])
+        def turn_pair(first):
+            turned[first] = ps.tile([P, 2, 2, P], F32, name="turned%d" % first, tag="bank%d" % first)
+            for i in range(2):
+                words = ht_pairs[first + i][:].rearrange("p v c e -> p (v c e)").bitcast(F32)
+                for v in range(2):
+                    nc.tensor.transpose(turned[first][:, i, v, :], words[:, columns(v)], identity[:])
 
         def gather_words(i):
-            nc.scalar.copy(out=h_grouped[i][:].rearrange("p m t -> p (m t)").bitcast(F32).rearrange("p (m v) -> p m v", v=2),
-                           in_=turned[i][:].rearrange("p v m -> p m v"))
+            words = h_grouped[i][:].rearrange("p m t -> p (m t)").bitcast(F32)
+            nc.scalar.copy(out=words.rearrange("p (i c v) -> p i c v", i=2, v=2),
+                           in_=turned[i - i % 2][:].rearrange("p i v (c u) -> p u i c v", u=2)[:, i % 2])
 
         def quantise_h(i):
             nc.vector.quantize_mx(out=h_codes[i][:].bitcast(E5M2), scales=h_planes[i][:],
                                   in_=h_grouped[i][:].rearrange("p m t -> p (m t)"))
 
         def y_pass(i):
-            y_acc[i] = bank("y%d" % i, i)
+            y_acc[i] = bank("y%d" % i, i if i < 4 else i ^ 1)
             nc.tensor.matmul_mx(out=y_acc[i][:], lhsT=h_codes[i][:].bitcast(E5M2), lhsT_scale=h_planes[i][:],
                                 rhs=bm_codes[:].bitcast(E4M3), rhs_scale=bm_plane[:], start=True, stop=True)
 
         def finish_and_store(i):
-            nc.vector.scalar_tensor_tensor(out=results[i][:], in0=momentum[i][:], scalar=DECAY, in1=y_acc[i][:],
+            nc.vector.scalar_tensor_tensor(out=results[i][:], in0=momentum[i], scalar=DECAY, in1=y_acc[i][:],
                                            op0=ALU.mult, op1=ALU.add)
-            nc.sync.dma_start(out=out[P * i:P * (i + 1), :], in_=results[i][:])
+            nc.sync.dma_start(out=out_rows[i], in_=results[i][:])
 
         def ht_tile(i):
             ht_pass(0, i)
@@ -187,13 +195,11 @@ def tile_mix_kfac_ema_kernel(tc, g, am_words, am_scales, bm_words, bm_scales, mo
             interleave_h(nc.vector.tensor_copy, i + 1)
             quantise_h(i)
             if i == 2:
-                turn_ht(4)
-                turn_ht(5)
+                turn_pair(4)
             y_pass(i)
         finish_and_store(0)
         multiply(3)
-        turn_ht(6)
-        turn_ht(7)
+        turn_pair(6)
         for i in range(4, 8):
             gather_words(i)
         for i in range(4, 8):

@@ -19,7 +19,8 @@ P = 128
 PACK = 4
 BANK = 512
 DECAY = 0.9
-SPLITS = (84, 52)
+SPLITS = (96, 72)
+AM_LOADS = ((0, 0, 512), (0, 512, 256), (1, 0, 512), (1, 512, 512), (0, 768, 256))
 
 
 def tile_mix_kfac_ema_kernel(tc, g, am_words, am_scales, bm_words, bm_scales, mom, out):
@@ -38,49 +39,49 @@ def tile_mix_kfac_ema_kernel(tc, g, am_words, am_scales, bm_words, bm_scales, mo
         def bank(name, b):
             return ps.tile([P, BANK], F32, name=name, tag="bank%d" % b)
 
-        am_plane = alloc("am_plane", [P, 2, M], U8)
+        am_planes = [alloc("am_plane%d" % a, [P, M], U8) for a in range(2)]
         bm_plane = alloc("bm_plane", [P, N], U8)
-        nc.vector.memset(am_plane[:].rearrange("p a m -> p (a m)").bitcast(I32), 0)
-        nc.vector.memset(bm_plane[:].bitcast(I32), 0)
+        for plane in am_planes + [bm_plane]:
+            nc.vector.memset(plane[:].bitcast(I32), 0)
 
         g_raw = [alloc("g_raw%d" % a, [P, PACK, L], F32) for a in range(2)]
-        am_moving = [alloc("am_moving%d" % a, [P, BANK], U32) for a in range(2)]
-        am_third = alloc("am_third", [P, 2 * P], U32)
-        am_fourth = alloc("am_fourth", [P, 2 * P], U32)
-        am_late = alloc("am_late", [P, BANK], U32)
+        am_parts = [alloc("am_part%d" % q, [P, count], U32) for q, (a, first, count) in enumerate(AM_LOADS)]
         bm_codes = alloc("bm_codes", [P, N], U32)
-        mom_first = [alloc("mom_first%d" % q, [P, 2, N], F32) for q in range(2)]
-        mom_second = alloc("mom_second", [P, 2, 2 * N], F32)
-        momentum = [mom_first[i // 2][:, i % 2] for i in range(4)]
-        momentum.extend(mom_second[:, i // 2, N * (i % 2):N * (i % 2 + 1)] for i in range(4))
-        out_rows = [out[:BANK].rearrange("(p u) n -> p u n", u=4)[:, u] for u in range(4)]
-        out_rows.extend(out[BANK:].rearrange("(q p u) n -> p q u n", q=2, u=2)[:, i // 2, i % 2] for i in range(4))
+        momentum = [alloc("momentum%d" % pair, [P, 2, N], F32) for pair in range(4)]
+        results = [alloc("result%d" % i, [P, N], F32) for i in range(8)]
+        mom_rows = mom.rearrange("(q p u) n -> p q u n", p=P, u=2)
+        out_rows = out.rearrange("(q p u) n -> p q u n", p=P, u=2)
         identity = alloc("identity", [P, P], F32)
         make_identity(nc, identity[:])
 
         def load_g(a):
             nc.sync.dma_start(out=g_raw[a][:], in_=g[512 * a:512 * (a + 1), :].rearrange("(p j) l -> p j l", j=PACK))
 
-        def load_am(tile, a, first, count):
-            nc.sync.dma_start(out=tile[:].bitcast(I32), in_=am_rows[:, a, first:first + count])
+        def load_am(q):
+            a, first, count = AM_LOADS[q]
+            nc.sync.dma_start(out=am_parts[q][:].bitcast(I32), in_=am_rows[:, a, first:first + count])
+
+        def load_scales(plane, scales):
+            for r in range(4):
+                nc.sync.dma_start(out=plane[r:P:32, :].bitcast(I32),
+                                  in_=scales.rearrange("(q r) c -> r q c", r=4)[r].bitcast(I32))
+
+        def am_columns(a, first, count):
+            q = [a == b and start <= first < start + width for b, start, width in AM_LOADS].index(True)
+            return am_parts[q][:, first - AM_LOADS[q][1]:first - AM_LOADS[q][1] + count].bitcast(E4M3)
 
         load_g(0)
-        for r in range(4):
-            nc.sync.dma_start(out=am_plane[r:P:32].bitcast(I32),
-                              in_=am_scales.rearrange("a (q r) c -> r q a c", r=4)[r].bitcast(I32))
-        load_am(am_moving[0], 0, 0, BANK)
+        load_scales(am_planes[0], am_scales[0])
+        load_am(0)
         load_g(1)
-        load_am(am_third, 0, BANK, 2 * P)
-        load_am(am_moving[1], 1, 0, BANK)
-        for r in range(4):
-            nc.sync.dma_start(out=bm_plane[r:P:32, :].bitcast(I32),
-                              in_=bm_scales[0].rearrange("(q r) c -> r q c", r=4)[r].bitcast(I32))
-        load_am(am_late, 1, BANK, BANK)
-        load_am(am_fourth, 0, BANK + 2 * P, 2 * P)
+        load_am(1)
+        load_scales(am_planes[1], am_scales[1])
+        for q in (2, 3, 4):
+            load_am(q)
         nc.sync.dma_start(out=bm_codes[:].bitcast(I32), in_=bm_rows)
-        for q in range(2):
-            nc.sync.dma_start(out=mom_first[q][:], in_=mom[:BANK].rearrange("(p u) n -> p u n", u=4)[:, 2 * q:2 * q + 2])
-        nc.sync.dma_start(out=mom_second[:], in_=mom[BANK:].rearrange("(q p u) n -> p q (u n)", q=2, u=2))
+        load_scales(bm_plane, bm_scales[0])
+        for pair in range(4):
+            nc.sync.dma_start(out=momentum[pair][:], in_=mom_rows[:, pair])
 
         g_codes = [alloc("g_codes%d" % a, [P, L], U32) for a in range(2)]
         g_planes = [alloc("g_plane%d" % a, [P, L], U8) for a in range(2)]
@@ -105,15 +106,11 @@ def tile_mix_kfac_ema_kernel(tc, g, am_words, am_scales, bm_words, bm_scales, mo
         def h_pass(a, t):
             nc.tensor.matmul_mx(out=h_acc[t][:], lhsT=g_codes[a][:, columns(t)].bitcast(E5M2),
                                 lhsT_scale=g_planes[a][:, columns(t)],
-                                rhs=am_moving[a][:].bitcast(E4M3), rhs_scale=am_plane[:, a, :BANK],
+                                rhs=am_columns(a, 0, BANK), rhs_scale=am_planes[a][:, :BANK],
                                 start=(a == 0), stop=(a == 1))
 
         def ht_pass(a, i):
-            if a == 1:
-                codes = am_late[:, columns(i - 4)]
-            else:
-                codes = am_third[:, columns(i - 4)] if i < 6 else am_fourth[:, columns(i - 6)]
-            nc.tensor.matmul_mx(out=ht_acc[i][:], lhsT=codes.bitcast(E4M3), lhsT_scale=am_plane[:, a, columns(i)],
+            nc.tensor.matmul_mx(out=ht_acc[i][:], lhsT=am_columns(a, P * i, P), lhsT_scale=am_planes[a][:, columns(i)],
                                 rhs=g_codes[a][:].bitcast(E5M2), rhs_scale=g_planes[a][:],
                                 start=(a == 0), stop=(a == 1))
 
@@ -124,10 +121,10 @@ def tile_mix_kfac_ema_kernel(tc, g, am_words, am_scales, bm_words, bm_scales, mo
         h_planes = [alloc("h_plane%d" % i, [P, P], U8) for i in range(8)]
         turned = {}
         y_acc = {}
-        results = [alloc("result%d" % i, [P, N], F32) for i in range(8)]
 
-        def round_h(copy, t, tiles=slice(0, 4)):
-            copy(out=h_rows[:, tiles, t, :], in_=h_acc[t][:].rearrange("p (c u) -> p u c", u=4)[:, tiles])
+        def round_h(copy, t, pairs=slice(0, 2), tiles=slice(0, 2)):
+            copy(out=h_rows[:].rearrange("p (q u) t c -> p q u t c", u=2)[:, pairs, tiles, t, :],
+                 in_=h_acc[t][:].rearrange("p (q c u) -> p q u c", q=2, u=2)[:, pairs, tiles])
 
         def interleave_h(copy, i):
             copy(out=h_grouped[i][:].rearrange("p (c e) t -> p c t e", e=4),
@@ -158,9 +155,9 @@ def tile_mix_kfac_ema_kernel(tc, g, am_words, am_scales, bm_words, bm_scales, mo
                                 rhs=bm_codes[:].bitcast(E4M3), rhs_scale=bm_plane[:], start=True, stop=True)
 
         def finish_and_store(i):
-            nc.vector.scalar_tensor_tensor(out=results[i][:], in0=momentum[i], scalar=DECAY, in1=y_acc[i][:],
-                                           op0=ALU.mult, op1=ALU.add)
-            nc.sync.dma_start(out=out_rows[i], in_=results[i][:])
+            nc.vector.scalar_tensor_tensor(out=results[i][:], in0=momentum[i // 2][:, i % 2], scalar=DECAY,
+                                           in1=y_acc[i][:], op0=ALU.mult, op1=ALU.add)
+            nc.sync.dma_start(out=out_rows[:, i // 2, i % 2], in_=results[i][:])
 
         def ht_tile(i):
             ht_pass(0, i)
@@ -184,25 +181,22 @@ def tile_mix_kfac_ema_kernel(tc, g, am_words, am_scales, bm_words, bm_scales, mo
             ht_tile(i)
         round_h(nc.vector.tensor_copy, 0)
         round_h(nc.scalar.copy, 1)
-        round_h(nc.vector.tensor_copy, 2, slice(0, 2))
-        round_h(nc.vector.tensor_copy, 2, slice(2, 4))
-        round_h(nc.scalar.copy, 3, slice(0, 1))
-        round_h(nc.scalar.copy, 3, slice(1, 4))
+        round_h(nc.vector.tensor_copy, 2, slice(0, 1))
+        round_h(nc.vector.tensor_copy, 2, slice(1, 2))
+        round_h(nc.scalar.copy, 3, slice(0, 1), slice(0, 1))
+        round_h(nc.scalar.copy, 3, slice(0, 1), slice(1, 2))
+        round_h(nc.scalar.copy, 3, slice(1, 2))
         for i in range(4, 8):
             round_ht(i)
         interleave_h(nc.vector.tensor_copy, 0)
         for i in range(3):
             interleave_h(nc.vector.tensor_copy, i + 1)
-            quantise_h(i)
-            if i == 2:
-                turn_pair(4)
-            y_pass(i)
-        finish_and_store(0)
-        multiply(3)
-        turn_pair(6)
+            multiply(i)
+            if i % 2 == 0:
+                turn_pair(4 + i)
         for i in range(4, 8):
             gather_words(i)
-        for i in range(4, 8):
+        for i in range(3, 8):
             finish_and_store(i - 3)
             multiply(i)
         for i in (5, 6, 7):

@@ -1,7 +1,6 @@
 from contextlib import ExitStack
 
 import concourse.mybir as mybir
-from concourse.masks import make_identity
 
 K, L, M, N = 1024, 512, 1024, 512
 FLOPS = 2 * K * L * M + 2 * L * M * N
@@ -17,10 +16,9 @@ ALU = mybir.AluOpType
 
 P = 128
 PACK = 4
-BANK = 512
 DECAY = 0.9
-SPLITS = (96, 72)
-AM_LOADS = ((0, 0, 512), (0, 512, 256), (1, 0, 512), (1, 512, 512), (0, 768, 256))
+SPLITS = ((88, 88), (104, 48))
+EARLY = 5
 
 
 def tile_mix_kfac_ema_kernel(tc, g, am_words, am_scales, bm_words, bm_scales, mom, out):
@@ -36,52 +34,48 @@ def tile_mix_kfac_ema_kernel(tc, g, am_words, am_scales, bm_words, bm_scales, mo
         def alloc(name, shape, dtype):
             return sb.tile(shape, dtype, name=name, align_bytes=64)
 
-        def bank(name, b):
-            return ps.tile([P, BANK], F32, name=name, tag="bank%d" % b)
-
         am_planes = [alloc("am_plane%d" % a, [P, M], U8) for a in range(2)]
         bm_plane = alloc("bm_plane", [P, N], U8)
         for plane in am_planes + [bm_plane]:
             nc.vector.memset(plane[:].bitcast(I32), 0)
 
         g_raw = [alloc("g_raw%d" % a, [P, PACK, L], F32) for a in range(2)]
-        am_parts = [alloc("am_part%d" % q, [P, count], U32) for q, (a, first, count) in enumerate(AM_LOADS)]
+        am_early = [alloc("am_early%d" % a, [P, EARLY * P], U32) for a in range(2)]
+        am_late = alloc("am_late", [P, 2, M - EARLY * P], U32)
         bm_codes = alloc("bm_codes", [P, N], U32)
-        momentum = [alloc("momentum%d" % pair, [P, 2, N], F32) for pair in range(4)]
-        results = [alloc("result%d" % i, [P, N], F32) for i in range(8)]
+        momentum = [alloc("momentum%d" % q, [P, 2, N], F32) for q in range(4)]
+        results = [alloc("result%d" % q, [P, 2, N], F32) for q in range(4)]
         mom_rows = mom.rearrange("(q p u) n -> p q u n", p=P, u=2)
         out_rows = out.rearrange("(q p u) n -> p q u n", p=P, u=2)
-        identity = alloc("identity", [P, P], F32)
-        make_identity(nc, identity[:])
 
         def load_g(a):
             nc.sync.dma_start(out=g_raw[a][:], in_=g[512 * a:512 * (a + 1), :].rearrange("(p j) l -> p j l", j=PACK))
 
-        def load_am(q):
-            a, first, count = AM_LOADS[q]
-            nc.sync.dma_start(out=am_parts[q][:].bitcast(I32), in_=am_rows[:, a, first:first + count])
+        def load_am_early(a):
+            nc.sync.dma_start(out=am_early[a][:].bitcast(I32), in_=am_rows[:, a, :EARLY * P])
+
+        def am_columns(a, i):
+            if i < EARLY:
+                return am_early[a][:, P * i:P * (i + 1)].bitcast(E4M3)
+            return am_late[:, a, P * (i - EARLY):P * (i - EARLY + 1)].bitcast(E4M3)
 
         def load_scales(plane, scales):
             for r in range(4):
                 nc.sync.dma_start(out=plane[r:P:32, :].bitcast(I32),
                                   in_=scales.rearrange("(q r) c -> r q c", r=4)[r].bitcast(I32))
 
-        def am_columns(a, first, count):
-            q = [a == b and start <= first < start + width for b, start, width in AM_LOADS].index(True)
-            return am_parts[q][:, first - AM_LOADS[q][1]:first - AM_LOADS[q][1] + count].bitcast(E4M3)
+        def load_mom(q):
+            nc.sync.dma_start(out=momentum[q][:], in_=mom_rows[:, q])
 
-        load_g(0)
-        load_scales(am_planes[0], am_scales[0])
-        load_am(0)
-        load_g(1)
-        load_am(1)
-        load_scales(am_planes[1], am_scales[1])
-        for q in (2, 3, 4):
-            load_am(q)
+        for a in range(2):
+            load_g(a)
+            load_scales(am_planes[a], am_scales[a])
+            load_am_early(a)
         nc.sync.dma_start(out=bm_codes[:].bitcast(I32), in_=bm_rows)
+        nc.sync.dma_start(out=am_late[:].bitcast(I32), in_=am_rows[:, :, EARLY * P:])
         load_scales(bm_plane, bm_scales[0])
-        for pair in range(4):
-            nc.sync.dma_start(out=momentum[pair][:], in_=mom_rows[:, pair])
+        for q in range(4):
+            load_mom(q)
 
         g_codes = [alloc("g_codes%d" % a, [P, L], U32) for a in range(2)]
         g_planes = [alloc("g_plane%d" % a, [P, L], U8) for a in range(2)]
@@ -89,115 +83,103 @@ def tile_mix_kfac_ema_kernel(tc, g, am_words, am_scales, bm_words, bm_scales, mo
         def columns(j):
             return slice(P * j, P * (j + 1))
 
-        def quantise_g(a):
-            grouped = [alloc("g_grouped%d%d" % (a, w), [P, 2, P, PACK], BF16) for w in range(2)]
+        g_grouped = [[alloc("g_grouped%d%d" % (a, w), [P, 2, P, PACK], BF16) for w in range(2)] for a in range(2)]
+
+        def round_g(a, w):
+            split = SPLITS[a][w]
             source = g_raw[a][:].rearrange("p j (c t) -> p c j t", t=PACK)
-            for w, split in enumerate(SPLITS):
-                target = grouped[w][:].rearrange("p t c j -> p c j t")
-                nc.vector.tensor_copy(out=target[:, :split], in_=source[:, :split, :, 2 * w:2 * w + 2])
-                nc.scalar.copy(out=target[:, split:], in_=source[:, split:, :, 2 * w:2 * w + 2])
-            for t in range(PACK):
-                nc.vector.quantize_mx(out=g_codes[a][:, columns(t)].bitcast(E5M2), scales=g_planes[a][:, columns(t)],
-                                      in_=grouped[t // 2][:, t % 2].rearrange("p c j -> p (c j)"))
+            target = g_grouped[a][w][:].rearrange("p t c j -> p c j t")
+            nc.vector.tensor_copy(out=target[:, :split], in_=source[:, :split, :, 2 * w:2 * w + 2])
+            nc.scalar.copy(out=target[:, split:], in_=source[:, split:, :, 2 * w:2 * w + 2])
 
-        h_acc = [bank("h%d" % t, t) for t in range(PACK)]
-        ht_acc = {i: bank("ht%d" % i, i) for i in range(4, 8)}
+        def quantise_g(a, t):
+            nc.vector.quantize_mx(out=g_codes[a][:, columns(t)].bitcast(E5M2), scales=g_planes[a][:, columns(t)],
+                                  in_=g_grouped[a][t // 2][:, t % 2].rearrange("p c j -> p (c j)"))
 
-        def h_pass(a, t):
-            nc.tensor.matmul_mx(out=h_acc[t][:], lhsT=g_codes[a][:, columns(t)].bitcast(E5M2),
+        h_acc = [ps.tile([P, PACK, P], F32, name="h%d" % i, tag="bank%d" % i) for i in range(8)]
+
+        def h_pass(a, i, t):
+            nc.tensor.matmul_mx(out=h_acc[i][:, t, :], lhsT=g_codes[a][:, columns(t)].bitcast(E5M2),
                                 lhsT_scale=g_planes[a][:, columns(t)],
-                                rhs=am_columns(a, 0, BANK), rhs_scale=am_planes[a][:, :BANK],
-                                start=(a == 0), stop=(a == 1))
+                                rhs=am_columns(a, i),
+                                rhs_scale=am_planes[a][:, columns(i)],
+                                start=(a == 0 and t == 0), stop=(a == 1 and t == PACK - 1))
 
-        def ht_pass(a, i):
-            nc.tensor.matmul_mx(out=ht_acc[i][:], lhsT=am_columns(a, P * i, P), lhsT_scale=am_planes[a][:, columns(i)],
-                                rhs=g_codes[a][:].bitcast(E5M2), rhs_scale=g_planes[a][:],
-                                start=(a == 0), stop=(a == 1))
+        def h_passes(a, banks):
+            for t in range(PACK):
+                for i in banks:
+                    h_pass(a, i, t)
 
-        h_rows = alloc("h_rows", [P, 4, PACK, P], BF16)
-        ht_pairs = {i: alloc("ht_pairs%d" % i, [P, 2, P, 2], BF16) for i in range(4, 8)}
-        h_grouped = [alloc("h_grouped%d" % i, [P, P, PACK], BF16) for i in range(8)]
+        h_grouped = [alloc("h_grouped%d" % q, [P, 2, P, PACK], BF16) for q in range(4)]
         h_codes = [alloc("h_codes%d" % i, [P, P], U32) for i in range(8)]
         h_planes = [alloc("h_plane%d" % i, [P, P], U8) for i in range(8)]
-        turned = {}
         y_acc = {}
 
-        def round_h(copy, t, pairs=slice(0, 2), tiles=slice(0, 2)):
-            copy(out=h_rows[:].rearrange("p (q u) t c -> p q u t c", u=2)[:, pairs, tiles, t, :],
-                 in_=h_acc[t][:].rearrange("p (q c u) -> p q u c", q=2, u=2)[:, pairs, tiles])
-
-        def interleave_h(copy, i):
-            copy(out=h_grouped[i][:].rearrange("p (c e) t -> p c t e", e=4),
-                 in_=h_rows[:, i].rearrange("p t (c e) -> p c t e", e=4))
-
-        def round_ht(i):
-            nc.scalar.copy(out=ht_pairs[i][:], in_=ht_acc[i][:].rearrange("p (v e c) -> p v c e", v=2, e=2))
-
-        def turn_pair(first):
-            turned[first] = ps.tile([P, 2, 2, P], F32, name="turned%d" % first, tag="bank%d" % first)
-            for i in range(2):
-                words = ht_pairs[first + i][:].rearrange("p v c e -> p (v c e)").bitcast(F32)
-                for v in range(2):
-                    nc.tensor.transpose(turned[first][:, i, v, :], words[:, columns(v)], identity[:])
-
-        def gather_words(i):
-            words = h_grouped[i][:].rearrange("p m t -> p (m t)").bitcast(F32)
-            nc.scalar.copy(out=words.rearrange("p (i c v) -> p i c v", i=2, v=2),
-                           in_=turned[i - i % 2][:].rearrange("p i v (c u) -> p u i c v", u=2)[:, i % 2])
+        def round_h(copy, i, tiles=slice(0, 2)):
+            copy(out=h_grouped[i // 2][:, tiles, 64 * (i % 2):64 * (i % 2 + 1), :],
+                 in_=h_acc[i][:].rearrange("p t (c u) -> p u c t", u=2)[:, tiles])
 
         def quantise_h(i):
             nc.vector.quantize_mx(out=h_codes[i][:].bitcast(E5M2), scales=h_planes[i][:],
-                                  in_=h_grouped[i][:].rearrange("p m t -> p (m t)"))
+                                  in_=h_grouped[i // 2][:, i % 2].rearrange("p m t -> p (m t)"))
 
         def y_pass(i):
-            y_acc[i] = bank("y%d" % i, i if i < 4 else i ^ 1)
+            y_acc[i] = ps.tile([P, N], F32, name="y%d" % i, tag="bank%d" % i)
             nc.tensor.matmul_mx(out=y_acc[i][:], lhsT=h_codes[i][:].bitcast(E5M2), lhsT_scale=h_planes[i][:],
                                 rhs=bm_codes[:].bitcast(E4M3), rhs_scale=bm_plane[:], start=True, stop=True)
 
-        def finish_and_store(i):
-            nc.vector.scalar_tensor_tensor(out=results[i][:], in0=momentum[i // 2][:, i % 2], scalar=DECAY,
+        def finish(i):
+            nc.vector.scalar_tensor_tensor(out=results[i // 2][:, i % 2], in0=momentum[i // 2][:, i % 2], scalar=DECAY,
                                            in1=y_acc[i][:], op0=ALU.mult, op1=ALU.add)
-            nc.sync.dma_start(out=out_rows[:, i // 2, i % 2], in_=results[i][:])
+            if i >= 4:
+                nc.sync.dma_start(out=out_rows[:, i // 2, i % 2], in_=results[i // 2][:, i % 2])
+            elif i % 2 == 1:
+                nc.sync.dma_start(out=out_rows[:, i // 2], in_=results[i // 2][:])
 
-        def ht_tile(i):
-            ht_pass(0, i)
-            ht_pass(1, i)
+        def complete_h(copy, i):
+            h_passes(1, (i,))
+            round_h(copy, i)
 
-        def multiply(i):
-            quantise_h(i)
-            y_pass(i)
+        def multiply_pair(q):
+            for i in (2 * q, 2 * q + 1):
+                quantise_h(i)
+                y_pass(i)
 
-        quantise_g(0)
+        for w in range(2):
+            round_g(0, w)
+            quantise_g(0, 2 * w)
+            quantise_g(0, 2 * w + 1)
+        h_passes(0, range(EARLY))
+        for w in range(2):
+            round_g(1, w)
         for t in range(PACK):
-            h_pass(0, t)
-        quantise_g(1)
-        for i in (4, 5):
-            ht_pass(0, i)
-        for t in range(PACK):
-            h_pass(1, t)
-        for i in (4, 5):
-            ht_pass(1, i)
-        for i in (6, 7):
-            ht_tile(i)
-        round_h(nc.vector.tensor_copy, 0)
-        round_h(nc.scalar.copy, 1)
-        round_h(nc.vector.tensor_copy, 2, slice(0, 1))
-        round_h(nc.vector.tensor_copy, 2, slice(1, 2))
-        round_h(nc.scalar.copy, 3, slice(0, 1), slice(0, 1))
-        round_h(nc.scalar.copy, 3, slice(0, 1), slice(1, 2))
-        round_h(nc.scalar.copy, 3, slice(1, 2))
-        for i in range(4, 8):
-            round_ht(i)
-        interleave_h(nc.vector.tensor_copy, 0)
+            quantise_g(1, t)
+        h_passes(1, (0, 1))
+        for u in range(2):
+            round_h(nc.vector.tensor_copy, 0, slice(u, u + 1))
+            round_h(nc.scalar.copy, 1, slice(u, u + 1))
+        for i in (2, 3):
+            h_passes(1, (i,))
+        for u in range(2):
+            for i in (2, 3):
+                round_h(nc.scalar.copy, i, slice(u, u + 1))
+        complete_h(nc.scalar.copy, 4)
+        h_passes(0, (5,))
         for i in range(3):
-            interleave_h(nc.vector.tensor_copy, i + 1)
-            multiply(i)
-            if i % 2 == 0:
-                turn_pair(4 + i)
-        for i in range(4, 8):
-            gather_words(i)
-        for i in range(3, 8):
-            finish_and_store(i - 3)
-            multiply(i)
-        for i in (5, 6, 7):
-            finish_and_store(i)
+            quantise_h(i)
+        y_pass(0)
+        y_pass(1)
+        finish(0)
+        quantise_h(3)
+        complete_h(nc.scalar.copy, 5)
+        for i in (6, 7):
+            y_pass(i - 4)
+            h_passes(0, (i,))
+            complete_h(nc.scalar.copy, i)
+        finish(1)
+        for q in (1, 2):
+            finish(2 * q)
+            multiply_pair(q + 1)
+            finish(2 * q + 1)
+        finish(6)
+        finish(7)

@@ -17,7 +17,7 @@ ALU = mybir.AluOpType
 P = 128
 PACK = 4
 DECAY = 0.9
-SPLITS = ((88, 88), (104, 48))
+SPLITS = ((88, 88), (96, 72))
 EARLY = 5
 
 
@@ -115,9 +115,9 @@ def tile_mix_kfac_ema_kernel(tc, g, am_words, am_scales, bm_words, bm_scales, mo
         h_planes = [alloc("h_plane%d" % i, [P, P], U8) for i in range(8)]
         y_acc = {}
 
-        def round_h(copy, i, tiles=slice(0, 2)):
-            copy(out=h_grouped[i // 2][:, tiles, 64 * (i % 2):64 * (i % 2 + 1), :],
-                 in_=h_acc[i][:].rearrange("p t (c u) -> p u c t", u=2)[:, tiles])
+        def round_h(copy, i):
+            copy(out=h_grouped[i // 2][:, :, 64 * (i % 2):64 * (i % 2 + 1), :].rearrange("p u c t -> p c t u"),
+                 in_=h_acc[i][:].rearrange("p t (c u) -> p c t u", u=2))
 
         def quantise_h(i):
             nc.vector.quantize_mx(out=h_codes[i][:].bitcast(E5M2), scales=h_planes[i][:],
@@ -155,27 +155,22 @@ def tile_mix_kfac_ema_kernel(tc, g, am_words, am_scales, bm_words, bm_scales, mo
         for t in range(PACK):
             quantise_g(1, t)
         h_passes(1, (0, 1))
-        for u in range(2):
-            round_h(nc.vector.tensor_copy, 0, slice(u, u + 1))
-            round_h(nc.scalar.copy, 1, slice(u, u + 1))
-        for i in (2, 3):
-            h_passes(1, (i,))
-        for u in range(2):
-            for i in (2, 3):
-                round_h(nc.scalar.copy, i, slice(u, u + 1))
-        complete_h(nc.scalar.copy, 4)
-        h_passes(0, (5,))
-        for i in range(3):
-            quantise_h(i)
-        y_pass(0)
-        y_pass(1)
-        finish(0)
-        quantise_h(3)
-        complete_h(nc.scalar.copy, 5)
-        for i in (6, 7):
-            y_pass(i - 4)
-            h_passes(0, (i,))
+        round_h(nc.vector.tensor_copy, 0)
+        round_h(nc.scalar.copy, 1)
+        for i in range(2, EARLY):
             complete_h(nc.scalar.copy, i)
+        h_passes(0, (5,))
+        multiply_pair(0)
+        complete_h(nc.scalar.copy, 5)
+        h_passes(0, (6,))
+        complete_h(nc.scalar.copy, 6)
+        finish(0)
+        quantise_h(2)
+        quantise_h(3)
+        y_pass(2)
+        h_passes(0, (7,))
+        complete_h(nc.scalar.copy, 7)
+        y_pass(3)
         finish(1)
         for q in (1, 2):
             finish(2 * q)

@@ -116,8 +116,8 @@ def tile_mix_kfac_ema_kernel(tc, g, am_words, am_scales, bm_words, bm_scales, mo
         y_acc = {}
 
         def round_h(copy, i):
-            copy(out=h_grouped[i // 2][:, :, 64 * (i % 2):64 * (i % 2 + 1), :].rearrange("p u c t -> p c t u"),
-                 in_=h_acc[i][:].rearrange("p t (c u) -> p c t u", u=2))
+            copy(out=h_grouped[i // 2][:, :, 64 * (i % 2):64 * (i % 2 + 1), :].rearrange("p u c t -> p c u t"),
+                 in_=h_acc[i][:].rearrange("p t (c u) -> p c u t", u=2))
 
         def quantise_h(i):
             nc.vector.quantize_mx(out=h_codes[i][:].bitcast(E5M2), scales=h_planes[i][:],

@@ -18,7 +18,7 @@ P = 128
 PACK = 4
 DECAY = 0.9
 SPLITS = ((88, 88), (96, 72))
-EARLY = 5
+AM_LOADS = ((0, 0, 512), (1, 0, 512), (0, 512, 256), (1, 512, 512), (0, 768, 256))
 
 
 def tile_mix_kfac_ema_kernel(tc, g, am_words, am_scales, bm_words, bm_scales, mom, out):
@@ -40,8 +40,7 @@ def tile_mix_kfac_ema_kernel(tc, g, am_words, am_scales, bm_words, bm_scales, mo
             nc.vector.memset(plane[:].bitcast(I32), 0)
 
         g_raw = [alloc("g_raw%d" % a, [P, PACK, L], F32) for a in range(2)]
-        am_early = [alloc("am_early%d" % a, [P, EARLY * P], U32) for a in range(2)]
-        am_late = alloc("am_late", [P, 2, M - EARLY * P], U32)
+        am_parts = [alloc("am_part%d" % n, [P, count], U32) for n, (a, first, count) in enumerate(AM_LOADS)]
         bm_codes = alloc("bm_codes", [P, N], U32)
         momentum = [alloc("momentum%d" % q, [P, 2, N], F32) for q in range(4)]
         results = [alloc("result%d" % q, [P, 2, N], F32) for q in range(4)]
@@ -51,13 +50,14 @@ def tile_mix_kfac_ema_kernel(tc, g, am_words, am_scales, bm_words, bm_scales, mo
         def load_g(a):
             nc.sync.dma_start(out=g_raw[a][:], in_=g[512 * a:512 * (a + 1), :].rearrange("(p j) l -> p j l", j=PACK))
 
-        def load_am_early(a):
-            nc.sync.dma_start(out=am_early[a][:].bitcast(I32), in_=am_rows[:, a, :EARLY * P])
+        def load_am(n):
+            a, first, count = AM_LOADS[n]
+            nc.sync.dma_start(out=am_parts[n][:].bitcast(I32), in_=am_rows[:, a, first:first + count])
 
         def am_columns(a, i):
-            if i < EARLY:
-                return am_early[a][:, P * i:P * (i + 1)].bitcast(E4M3)
-            return am_late[:, a, P * (i - EARLY):P * (i - EARLY + 1)].bitcast(E4M3)
+            n = [a == b and first <= P * i < first + count for b, first, count in AM_LOADS].index(True)
+            offset = P * i - AM_LOADS[n][1]
+            return am_parts[n][:, offset:offset + P].bitcast(E4M3)
 
         def load_scales(plane, scales):
             for r in range(4):
@@ -70,11 +70,14 @@ def tile_mix_kfac_ema_kernel(tc, g, am_words, am_scales, bm_words, bm_scales, mo
         for a in range(2):
             load_g(a)
             load_scales(am_planes[a], am_scales[a])
-            load_am_early(a)
+            load_am(a)
         nc.sync.dma_start(out=bm_codes[:].bitcast(I32), in_=bm_rows)
-        nc.sync.dma_start(out=am_late[:].bitcast(I32), in_=am_rows[:, :, EARLY * P:])
+        for n in (2, 3):
+            load_am(n)
         load_scales(bm_plane, bm_scales[0])
-        for q in range(4):
+        load_mom(0)
+        load_am(4)
+        for q in range(1, 4):
             load_mom(q)
 
         g_codes = [alloc("g_codes%d" % a, [P, L], U32) for a in range(2)]
@@ -131,10 +134,7 @@ def tile_mix_kfac_ema_kernel(tc, g, am_words, am_scales, bm_words, bm_scales, mo
         def finish(i):
             nc.vector.scalar_tensor_tensor(out=results[i // 2][:, i % 2], in0=momentum[i // 2][:, i % 2], scalar=DECAY,
                                            in1=y_acc[i][:], op0=ALU.mult, op1=ALU.add)
-            if i >= 4:
-                nc.sync.dma_start(out=out_rows[:, i // 2, i % 2], in_=results[i // 2][:, i % 2])
-            elif i % 2 == 1:
-                nc.sync.dma_start(out=out_rows[:, i // 2], in_=results[i // 2][:])
+            nc.sync.dma_start(out=out_rows[:, i // 2, i % 2], in_=results[i // 2][:, i % 2])
 
         def complete_h(copy, i):
             h_passes(1, (i,))
@@ -149,7 +149,7 @@ def tile_mix_kfac_ema_kernel(tc, g, am_words, am_scales, bm_words, bm_scales, mo
             round_g(0, w)
             quantise_g(0, 2 * w)
             quantise_g(0, 2 * w + 1)
-        h_passes(0, range(EARLY))
+        h_passes(0, range(4))
         for w in range(2):
             round_g(1, w)
         for t in range(PACK):
@@ -157,20 +157,22 @@ def tile_mix_kfac_ema_kernel(tc, g, am_words, am_scales, bm_words, bm_scales, mo
         h_passes(1, (0, 1))
         round_h(nc.vector.tensor_copy, 0)
         round_h(nc.scalar.copy, 1)
-        for i in range(2, EARLY):
+        for i in (2, 3):
             complete_h(nc.scalar.copy, i)
-        h_passes(0, (5,))
+        h_passes(0, (4,))
+        complete_h(nc.scalar.copy, 4)
         multiply_pair(0)
+        h_passes(0, (5,))
         complete_h(nc.scalar.copy, 5)
         h_passes(0, (6,))
-        complete_h(nc.scalar.copy, 6)
         finish(0)
         quantise_h(2)
         quantise_h(3)
         y_pass(2)
+        complete_h(nc.scalar.copy, 6)
+        y_pass(3)
         h_passes(0, (7,))
         complete_h(nc.scalar.copy, 7)
-        y_pass(3)
         finish(1)
         for q in (1, 2):
             finish(2 * q)

@@ -67,14 +67,16 @@ def tile_mix_kfac_ema_kernel(tc, g, am_words, am_scales, bm_words, bm_scales, mo
         def load_mom(q):
             nc.sync.dma_start(out=momentum[q][:], in_=mom_rows[:, q])
 
-        for a in range(2):
-            load_g(a)
-            load_scales(am_planes[a], am_scales[a])
-            load_am(a)
+        load_g(0)
+        load_scales(am_planes[0], am_scales[0])
+        load_am(0)
+        load_g(1)
+        load_am(2)
+        load_scales(am_planes[1], am_scales[1])
+        load_am(1)
         nc.sync.dma_start(out=bm_codes[:].bitcast(I32), in_=bm_rows)
-        for n in (2, 3):
-            load_am(n)
         load_scales(bm_plane, bm_scales[0])
+        load_am(3)
         load_mom(0)
         load_am(4)
         for q in range(1, 4):
@@ -154,24 +156,18 @@ def tile_mix_kfac_ema_kernel(tc, g, am_words, am_scales, bm_words, bm_scales, mo
             round_g(1, w)
         for t in range(PACK):
             quantise_g(1, t)
+        h_passes(0, (4, 5))
         h_passes(1, (0, 1))
         round_h(nc.vector.tensor_copy, 0)
         round_h(nc.scalar.copy, 1)
-        for i in (2, 3):
+        for i in range(2, 6):
             complete_h(nc.scalar.copy, i)
-        h_passes(0, (4,))
-        complete_h(nc.scalar.copy, 4)
         multiply_pair(0)
-        h_passes(0, (5,))
-        complete_h(nc.scalar.copy, 5)
         h_passes(0, (6,))
-        finish(0)
-        quantise_h(2)
-        quantise_h(3)
-        y_pass(2)
         complete_h(nc.scalar.copy, 6)
-        y_pass(3)
         h_passes(0, (7,))
+        finish(0)
+        multiply_pair(1)
         complete_h(nc.scalar.copy, 7)
         finish(1)
         for q in (1, 2):

@@ -16,9 +16,10 @@ ALU = mybir.AluOpType
 
 P = 128
 PACK = 4
+PAIR = 2 * P
 DECAY = 0.9
-SPLITS = ((88, 88), (96, 72))
-AM_LOADS = ((0, 0, 512), (1, 0, 512), (0, 512, 256), (1, 512, 512), (0, 768, 256))
+SPLITS = (96, 72)
+AM_LOADS = ((0, 0, 512), (1, 0, 512), (0, 512, 512), (1, 512, 512))
 
 
 def tile_mix_kfac_ema_kernel(tc, g, am_words, am_scales, bm_words, bm_scales, mom, out):
@@ -54,10 +55,10 @@ def tile_mix_kfac_ema_kernel(tc, g, am_words, am_scales, bm_words, bm_scales, mo
             a, first, count = AM_LOADS[n]
             nc.sync.dma_start(out=am_parts[n][:].bitcast(I32), in_=am_rows[:, a, first:first + count])
 
-        def am_columns(a, i):
-            n = [a == b and first <= P * i < first + count for b, first, count in AM_LOADS].index(True)
-            offset = P * i - AM_LOADS[n][1]
-            return am_parts[n][:, offset:offset + P].bitcast(E4M3)
+        def am_columns(a, q):
+            n = [a == b and first <= PAIR * q < first + count for b, first, count in AM_LOADS].index(True)
+            offset = PAIR * q - AM_LOADS[n][1]
+            return am_parts[n][:, offset:offset + PAIR].bitcast(E4M3)
 
         def load_scales(plane, scales):
             for r in range(4):
@@ -67,18 +68,16 @@ def tile_mix_kfac_ema_kernel(tc, g, am_words, am_scales, bm_words, bm_scales, mo
         def load_mom(q):
             nc.sync.dma_start(out=momentum[q][:], in_=mom_rows[:, q])
 
-        load_g(0)
-        load_scales(am_planes[0], am_scales[0])
-        load_am(0)
-        load_g(1)
-        load_am(2)
-        load_scales(am_planes[1], am_scales[1])
-        load_am(1)
+        for a in range(2):
+            load_g(a)
+            load_scales(am_planes[a], am_scales[a])
+            load_am(a)
         nc.sync.dma_start(out=bm_codes[:].bitcast(I32), in_=bm_rows)
+        for n in (2, 3):
+            load_am(n)
         load_scales(bm_plane, bm_scales[0])
-        load_am(3)
-        load_mom(0)
-        load_am(4)
+        for u in range(2):
+            nc.sync.dma_start(out=momentum[0][:, u], in_=mom_rows[:, 0, u])
         for q in range(1, 4):
             load_mom(q)
 
@@ -91,7 +90,7 @@ def tile_mix_kfac_ema_kernel(tc, g, am_words, am_scales, bm_words, bm_scales, mo
         g_grouped = [[alloc("g_grouped%d%d" % (a, w), [P, 2, P, PACK], BF16) for w in range(2)] for a in range(2)]
 
         def round_g(a, w):
-            split = SPLITS[a][w]
+            split = SPLITS[w]
             source = g_raw[a][:].rearrange("p j (c t) -> p c j t", t=PACK)
             target = g_grouped[a][w][:].rearrange("p t c j -> p c j t")
             nc.vector.tensor_copy(out=target[:, :split], in_=source[:, :split, :, 2 * w:2 * w + 2])
@@ -101,35 +100,31 @@ def tile_mix_kfac_ema_kernel(tc, g, am_words, am_scales, bm_words, bm_scales, mo
             nc.vector.quantize_mx(out=g_codes[a][:, columns(t)].bitcast(E5M2), scales=g_planes[a][:, columns(t)],
                                   in_=g_grouped[a][t // 2][:, t % 2].rearrange("p c j -> p (c j)"))
 
-        h_acc = [ps.tile([P, PACK, P], F32, name="h%d" % i, tag="bank%d" % i) for i in range(8)]
+        h_acc = [ps.tile([P, 2, PAIR], F32, name="h%d" % i, tag="bank%d" % i) for i in range(8)]
 
-        def h_pass(a, i, t):
-            nc.tensor.matmul_mx(out=h_acc[i][:, t, :], lhsT=g_codes[a][:, columns(t)].bitcast(E5M2),
-                                lhsT_scale=g_planes[a][:, columns(t)],
-                                rhs=am_columns(a, i),
-                                rhs_scale=am_planes[a][:, columns(i)],
-                                start=(a == 0 and t == 0), stop=(a == 1 and t == PACK - 1))
+        def h_passes(a, pairs, slots=range(PACK)):
+            for t in slots:
+                for q in pairs:
+                    nc.tensor.matmul_mx(out=h_acc[2 * q + t // 2][:, t % 2, :], lhsT=g_codes[a][:, columns(t)].bitcast(E5M2),
+                                        lhsT_scale=g_planes[a][:, columns(t)],
+                                        rhs=am_columns(a, q), rhs_scale=am_planes[a][:, PAIR * q:PAIR * (q + 1)],
+                                        start=(a == 0 and t % 2 == 0), stop=(a == 1 and t % 2 == 1))
 
-        def h_passes(a, banks):
-            for t in range(PACK):
-                for i in banks:
-                    h_pass(a, i, t)
-
-        h_grouped = [alloc("h_grouped%d" % q, [P, 2, P, PACK], BF16) for q in range(4)]
+        h_grouped = [alloc("h_grouped%d" % i, [P, P, PACK], BF16) for i in range(8)]
         h_codes = [alloc("h_codes%d" % i, [P, P], U32) for i in range(8)]
         h_planes = [alloc("h_plane%d" % i, [P, P], U8) for i in range(8)]
         y_acc = {}
 
-        def round_h(copy, i):
-            copy(out=h_grouped[i // 2][:, :, 64 * (i % 2):64 * (i % 2 + 1), :].rearrange("p u c t -> p c u t"),
-                 in_=h_acc[i][:].rearrange("p t (c u) -> p c u t", u=2))
+        def round_h(copy, i, w):
+            copy(out=h_grouped[i][:, :, 2 * w:2 * w + 2],
+                 in_=h_acc[i - i % 2 + w][:].rearrange("p t (c u) -> p u c t", u=2)[:, i % 2])
 
         def quantise_h(i):
             nc.vector.quantize_mx(out=h_codes[i][:].bitcast(E5M2), scales=h_planes[i][:],
-                                  in_=h_grouped[i // 2][:, i % 2].rearrange("p m t -> p (m t)"))
+                                  in_=h_grouped[i][:].rearrange("p m t -> p (m t)"))
 
         def y_pass(i):
-            y_acc[i] = ps.tile([P, N], F32, name="y%d" % i, tag="bank%d" % i)
+            y_acc[i] = ps.tile([P, N], F32, name="y%d" % i, tag="bank%d" % (i - 2 if i in (4, 6) else i))
             nc.tensor.matmul_mx(out=y_acc[i][:], lhsT=h_codes[i][:].bitcast(E5M2), lhsT_scale=h_planes[i][:],
                                 rhs=bm_codes[:].bitcast(E4M3), rhs_scale=bm_plane[:], start=True, stop=True)
 
@@ -138,41 +133,40 @@ def tile_mix_kfac_ema_kernel(tc, g, am_words, am_scales, bm_words, bm_scales, mo
                                            in1=y_acc[i][:], op0=ALU.mult, op1=ALU.add)
             nc.sync.dma_start(out=out_rows[:, i // 2, i % 2], in_=results[i // 2][:, i % 2])
 
-        def complete_h(copy, i):
-            h_passes(1, (i,))
-            round_h(copy, i)
-
-        def multiply_pair(q):
+        def round_pair(q):
             for i in (2 * q, 2 * q + 1):
-                quantise_h(i)
-                y_pass(i)
+                round_h(nc.scalar.copy, i, 0)
+                round_h(nc.vector.tensor_copy if q == 0 else nc.scalar.copy, i, 1)
 
-        for w in range(2):
-            round_g(0, w)
-            quantise_g(0, 2 * w)
-            quantise_g(0, 2 * w + 1)
-        h_passes(0, range(4))
-        for w in range(2):
-            round_g(1, w)
-        for t in range(PACK):
-            quantise_g(1, t)
-        h_passes(0, (4, 5))
-        h_passes(1, (0, 1))
-        round_h(nc.vector.tensor_copy, 0)
-        round_h(nc.scalar.copy, 1)
-        for i in range(2, 6):
-            complete_h(nc.scalar.copy, i)
-        multiply_pair(0)
-        h_passes(0, (6,))
-        complete_h(nc.scalar.copy, 6)
-        h_passes(0, (7,))
+        def multiply(i):
+            quantise_h(i)
+            y_pass(i)
+
+        for a in range(2):
+            for w in range(2):
+                round_g(a, w)
+            for t in range(PACK):
+                quantise_g(a, t)
+            if a == 0:
+                h_passes(0, (0, 1))
+        for q in range(2):
+            h_passes(1, (q,))
+            round_pair(q)
+        h_passes(0, (2,))
+        h_passes(1, (2,), (0, 1))
+        multiply(0)
+        multiply(1)
+        h_passes(1, (2,), (2, 3))
+        round_pair(2)
+        multiply(2)
+        h_passes(0, (3,))
+        h_passes(1, (3,), (0, 1))
         finish(0)
-        multiply_pair(1)
-        complete_h(nc.scalar.copy, 7)
         finish(1)
-        for q in (1, 2):
-            finish(2 * q)
-            multiply_pair(q + 1)
-            finish(2 * q + 1)
-        finish(6)
-        finish(7)
+        multiply(3)
+        h_passes(1, (3,), (2, 3))
+        round_pair(3)
+        for i in range(2, 8):
+            finish(i)
+            if i + 2 < 8:
+                multiply(i + 2)

@@ -19,7 +19,7 @@ PACK = 4
 PAIR = 2 * P
 DECAY = 0.9
 SPLITS = (96, 72)
-AM_LOADS = ((0, 0, 512), (1, 0, 512), (0, 512, 512), (1, 512, 512))
+AM_LOADS = ((0, 0, 512), (0, 512, 256), (1, 0, 512), (1, 512, 512), (0, 768, 256))
 
 
 def tile_mix_kfac_ema_kernel(tc, g, am_words, am_scales, bm_words, bm_scales, mom, out):
@@ -68,16 +68,18 @@ def tile_mix_kfac_ema_kernel(tc, g, am_words, am_scales, bm_words, bm_scales, mo
         def load_mom(q):
             nc.sync.dma_start(out=momentum[q][:], in_=mom_rows[:, q])
 
-        for a in range(2):
-            load_g(a)
-            load_scales(am_planes[a], am_scales[a])
-            load_am(a)
+        load_g(0)
+        load_scales(am_planes[0], am_scales[0])
+        load_am(0)
+        load_g(1)
+        load_am(1)
+        load_scales(am_planes[1], am_scales[1])
+        load_am(2)
+        load_am(3)
         nc.sync.dma_start(out=bm_codes[:].bitcast(I32), in_=bm_rows)
-        for n in (2, 3):
-            load_am(n)
         load_scales(bm_plane, bm_scales[0])
-        for u in range(2):
-            nc.sync.dma_start(out=momentum[0][:, u], in_=mom_rows[:, 0, u])
+        load_mom(0)
+        load_am(4)
         for q in range(1, 4):
             load_mom(q)
 
@@ -110,21 +112,21 @@ def tile_mix_kfac_ema_kernel(tc, g, am_words, am_scales, bm_words, bm_scales, mo
                                         rhs=am_columns(a, q), rhs_scale=am_planes[a][:, PAIR * q:PAIR * (q + 1)],
                                         start=(a == 0 and t % 2 == 0), stop=(a == 1 and t % 2 == 1))
 
-        h_grouped = [alloc("h_grouped%d" % i, [P, P, PACK], BF16) for i in range(8)]
+        h_grouped = [alloc("h_grouped%d" % q, [P, 2, P, PACK], BF16) for q in range(4)]
         h_codes = [alloc("h_codes%d" % i, [P, P], U32) for i in range(8)]
         h_planes = [alloc("h_plane%d" % i, [P, P], U8) for i in range(8)]
         y_acc = {}
 
-        def round_h(copy, i, w):
-            copy(out=h_grouped[i][:, :, 2 * w:2 * w + 2],
-                 in_=h_acc[i - i % 2 + w][:].rearrange("p t (c u) -> p u c t", u=2)[:, i % 2])
+        def round_h(copy, q, w, tiles=slice(0, 2), part=slice(0, P)):
+            copy(out=h_grouped[q][:, tiles, part, 2 * w:2 * w + 2].rearrange("p u c t -> p c u t"),
+                 in_=h_acc[2 * q + w][:].rearrange("p t (c u) -> p c u t", u=2)[:, part, tiles])
 
         def quantise_h(i):
             nc.vector.quantize_mx(out=h_codes[i][:].bitcast(E5M2), scales=h_planes[i][:],
-                                  in_=h_grouped[i][:].rearrange("p m t -> p (m t)"))
+                                  in_=h_grouped[i // 2][:, i % 2].rearrange("p m t -> p (m t)"))
 
         def y_pass(i):
-            y_acc[i] = ps.tile([P, N], F32, name="y%d" % i, tag="bank%d" % (i - 2 if i in (4, 6) else i))
+            y_acc[i] = ps.tile([P, N], F32, name="y%d" % i, tag="bank%d" % i)
             nc.tensor.matmul_mx(out=y_acc[i][:], lhsT=h_codes[i][:].bitcast(E5M2), lhsT_scale=h_planes[i][:],
                                 rhs=bm_codes[:].bitcast(E4M3), rhs_scale=bm_plane[:], start=True, stop=True)
 
@@ -132,11 +134,6 @@ def tile_mix_kfac_ema_kernel(tc, g, am_words, am_scales, bm_words, bm_scales, mo
             nc.vector.scalar_tensor_tensor(out=results[i // 2][:, i % 2], in0=momentum[i // 2][:, i % 2], scalar=DECAY,
                                            in1=y_acc[i][:], op0=ALU.mult, op1=ALU.add)
             nc.sync.dma_start(out=out_rows[:, i // 2, i % 2], in_=results[i // 2][:, i % 2])
-
-        def round_pair(q):
-            for i in (2 * q, 2 * q + 1):
-                round_h(nc.scalar.copy, i, 0)
-                round_h(nc.vector.tensor_copy if q == 0 else nc.scalar.copy, i, 1)
 
         def multiply(i):
             quantise_h(i)
@@ -147,26 +144,33 @@ def tile_mix_kfac_ema_kernel(tc, g, am_words, am_scales, bm_words, bm_scales, mo
                 round_g(a, w)
             for t in range(PACK):
                 quantise_g(a, t)
-            if a == 0:
-                h_passes(0, (0, 1))
-        for q in range(2):
-            h_passes(1, (q,))
-            round_pair(q)
-        h_passes(0, (2,))
-        h_passes(1, (2,), (0, 1))
+            h_passes(0, (0, 1) if a == 0 else (2,))
+        h_passes(1, (0,))
+        for u in range(2):
+            round_h(nc.scalar.copy, 0, 0, slice(u, u + 1))
+            round_h(nc.vector.tensor_copy, 0, 1, slice(u, u + 1))
+        h_passes(1, (1,))
+        round_h(nc.scalar.copy, 1, 1, part=slice(0, P // 2))
+        round_h(nc.scalar.copy, 1, 0)
+        h_passes(1, (2,))
+        for w in range(2):
+            round_h(nc.scalar.copy, 2, w)
         multiply(0)
         multiply(1)
-        h_passes(1, (2,), (2, 3))
-        round_pair(2)
-        multiply(2)
+        round_h(nc.vector.tensor_copy, 1, 1, part=slice(P // 2, P))
         h_passes(0, (3,))
         h_passes(1, (3,), (0, 1))
         finish(0)
-        finish(1)
-        multiply(3)
+        multiply(2)
         h_passes(1, (3,), (2, 3))
-        round_pair(3)
-        for i in range(2, 8):
-            finish(i)
-            if i + 2 < 8:
-                multiply(i + 2)
+        multiply(3)
+        for w in range(2):
+            round_h(nc.scalar.copy, 3, w)
+        finish(1)
+        for q in (1, 2):
+            finish(2 * q)
+            multiply(2 * q + 2)
+            multiply(2 * q + 3)
+            finish(2 * q + 1)
+        finish(6)
+        finish(7)

@@ -78,9 +78,8 @@ def tile_mix_kfac_ema_kernel(tc, g, am_words, am_scales, bm_words, bm_scales, mo
         load_am(3)
         nc.sync.dma_start(out=bm_codes[:].bitcast(I32), in_=bm_rows)
         load_scales(bm_plane, bm_scales[0])
-        load_mom(0)
         load_am(4)
-        for q in range(1, 4):
+        for q in range(4):
             load_mom(q)
 
         g_codes = [alloc("g_codes%d" % a, [P, L], U32) for a in range(2)]
@@ -117,9 +116,9 @@ def tile_mix_kfac_ema_kernel(tc, g, am_words, am_scales, bm_words, bm_scales, mo
         h_planes = [alloc("h_plane%d" % i, [P, P], U8) for i in range(8)]
         y_acc = {}
 
-        def round_h(copy, q, w, tiles=slice(0, 2), part=slice(0, P)):
-            copy(out=h_grouped[q][:, tiles, part, 2 * w:2 * w + 2].rearrange("p u c t -> p c u t"),
-                 in_=h_acc[2 * q + w][:].rearrange("p t (c u) -> p c u t", u=2)[:, part, tiles])
+        def round_h(copy, q, w, tiles=slice(0, 2)):
+            copy(out=h_grouped[q][:, tiles, :, 2 * w:2 * w + 2].rearrange("p u c t -> p c u t"),
+                 in_=h_acc[2 * q + w][:].rearrange("p t (c u) -> p c u t", u=2)[:, :, tiles])
 
         def quantise_h(i):
             nc.vector.quantize_mx(out=h_codes[i][:].bitcast(E5M2), scales=h_planes[i][:],
@@ -150,27 +149,27 @@ def tile_mix_kfac_ema_kernel(tc, g, am_words, am_scales, bm_words, bm_scales, mo
             round_h(nc.scalar.copy, 0, 0, slice(u, u + 1))
             round_h(nc.vector.tensor_copy, 0, 1, slice(u, u + 1))
         h_passes(1, (1,))
-        round_h(nc.scalar.copy, 1, 1, part=slice(0, P // 2))
         round_h(nc.scalar.copy, 1, 0)
         h_passes(1, (2,))
         for w in range(2):
             round_h(nc.scalar.copy, 2, w)
+        h_passes(0, (3,), (0, 1))
         multiply(0)
         multiply(1)
-        round_h(nc.vector.tensor_copy, 1, 1, part=slice(P // 2, P))
-        h_passes(0, (3,))
+        round_h(nc.vector.tensor_copy, 1, 1)
         h_passes(1, (3,), (0, 1))
-        finish(0)
-        multiply(2)
-        h_passes(1, (3,), (2, 3))
-        multiply(3)
+        for a in range(2):
+            h_passes(a, (3,), (2, 3))
         for w in range(2):
             round_h(nc.scalar.copy, 3, w)
+        finish(0)
+        multiply(2)
+        multiply(3)
         finish(1)
-        for q in (1, 2):
-            finish(2 * q)
-            multiply(2 * q + 2)
-            multiply(2 * q + 3)
-            finish(2 * q + 1)
+        for q in (2, 3):
+            multiply(2 * q)
+            multiply(2 * q + 1)
+            finish(2 * q - 2)
+            finish(2 * q - 1)
         finish(6)
         finish(7)

@@ -19,6 +19,7 @@ PACK = 4
 PAIR = 2 * P
 DECAY = 0.9
 SPLITS = (96, 72)
+ROW_PAIR_SPLITS = ((84, 84), (72, 80))
 AM_LOADS = ((0, 0, 512), (0, 512, 256), (1, 0, 512), (1, 512, 512), (0, 768, 256))
 
 
@@ -40,7 +41,8 @@ def tile_mix_kfac_ema_kernel(tc, g, am_words, am_scales, bm_words, bm_scales, mo
         for plane in am_planes + [bm_plane]:
             nc.vector.memset(plane[:].bitcast(I32), 0)
 
-        g_raw = [alloc("g_raw%d" % a, [P, PACK, L], F32) for a in range(2)]
+        g_first = alloc("g_first", [P, PACK, L], F32)
+        g_second = [alloc("g_second%d" % v, [P, 2, L], F32) for v in range(2)]
         am_parts = [alloc("am_part%d" % n, [P, count], U32) for n, (a, first, count) in enumerate(AM_LOADS)]
         bm_codes = alloc("bm_codes", [P, N], U32)
         momentum = [alloc("momentum%d" % q, [P, 2, N], F32) for q in range(4)]
@@ -48,8 +50,7 @@ def tile_mix_kfac_ema_kernel(tc, g, am_words, am_scales, bm_words, bm_scales, mo
         mom_rows = mom.rearrange("(q p u) n -> p q u n", p=P, u=2)
         out_rows = out.rearrange("(q p u) n -> p q u n", p=P, u=2)
 
-        def load_g(a):
-            nc.sync.dma_start(out=g_raw[a][:], in_=g[512 * a:512 * (a + 1), :].rearrange("(p j) l -> p j l", j=PACK))
+        g_rows = g.rearrange("(a p j) l -> a p j l", a=2, j=PACK)
 
         def load_am(n):
             a, first, count = AM_LOADS[n]
@@ -68,10 +69,11 @@ def tile_mix_kfac_ema_kernel(tc, g, am_words, am_scales, bm_words, bm_scales, mo
         def load_mom(q):
             nc.sync.dma_start(out=momentum[q][:], in_=mom_rows[:, q])
 
-        load_g(0)
+        nc.sync.dma_start(out=g_first[:], in_=g_rows[0])
         load_scales(am_planes[0], am_scales[0])
         load_am(0)
-        load_g(1)
+        for v in range(2):
+            nc.sync.dma_start(out=g_second[v][:], in_=g_rows[1][:, 2 * v:2 * v + 2])
         load_am(1)
         load_scales(am_planes[1], am_scales[1])
         load_am(2)
@@ -90,12 +92,12 @@ def tile_mix_kfac_ema_kernel(tc, g, am_words, am_scales, bm_words, bm_scales, mo
 
         g_grouped = [[alloc("g_grouped%d%d" % (a, w), [P, 2, P, PACK], BF16) for w in range(2)] for a in range(2)]
 
-        def round_g(a, w):
-            split = SPLITS[w]
-            source = g_raw[a][:].rearrange("p j (c t) -> p c j t", t=PACK)
-            target = g_grouped[a][w][:].rearrange("p t c j -> p c j t")
-            nc.vector.tensor_copy(out=target[:, :split], in_=source[:, :split, :, 2 * w:2 * w + 2])
-            nc.scalar.copy(out=target[:, split:], in_=source[:, split:, :, 2 * w:2 * w + 2])
+        def round_g(a, raw, rows, splits):
+            source = raw[:].rearrange("p j (c t) -> p c j t", t=PACK)
+            for w, split in enumerate(splits):
+                target = g_grouped[a][w][:, :, :, rows].rearrange("p t c j -> p c j t")
+                nc.vector.tensor_copy(out=target[:, :split], in_=source[:, :split, :, 2 * w:2 * w + 2])
+                nc.scalar.copy(out=target[:, split:], in_=source[:, split:, :, 2 * w:2 * w + 2])
 
         def quantise_g(a, t):
             nc.vector.quantize_mx(out=g_codes[a][:, columns(t)].bitcast(E5M2), scales=g_planes[a][:, columns(t)],
@@ -132,30 +134,38 @@ def tile_mix_kfac_ema_kernel(tc, g, am_words, am_scales, bm_words, bm_scales, mo
         def finish(i):
             nc.vector.scalar_tensor_tensor(out=results[i // 2][:, i % 2], in0=momentum[i // 2][:, i % 2], scalar=DECAY,
                                            in1=y_acc[i][:], op0=ALU.mult, op1=ALU.add)
-            nc.sync.dma_start(out=out_rows[:, i // 2, i % 2], in_=results[i // 2][:, i % 2])
+            if i == 1:
+                nc.sync.dma_start(out=out_rows[:, 0], in_=results[0][:])
+            elif i > 1:
+                nc.sync.dma_start(out=out_rows[:, i // 2, i % 2], in_=results[i // 2][:, i % 2])
 
         def multiply(i):
             quantise_h(i)
             y_pass(i)
 
-        for a in range(2):
-            for w in range(2):
-                round_g(a, w)
-            for t in range(PACK):
-                quantise_g(a, t)
-            h_passes(0, (0, 1) if a == 0 else (2,))
+        round_g(0, g_first, slice(0, PACK), SPLITS)
+        for t in range(PACK):
+            quantise_g(0, t)
+        h_passes(0, (0, 1))
+        for v in range(2):
+            round_g(1, g_second[v], slice(2 * v, 2 * v + 2), ROW_PAIR_SPLITS[v])
+        for t in range(PACK):
+            quantise_g(1, t)
+        h_passes(0, (2,), (0, 1))
         h_passes(1, (0,))
         for u in range(2):
             round_h(nc.scalar.copy, 0, 0, slice(u, u + 1))
             round_h(nc.vector.tensor_copy, 0, 1, slice(u, u + 1))
         h_passes(1, (1,))
         round_h(nc.scalar.copy, 1, 0)
-        h_passes(1, (2,))
+        h_passes(1, (2,), (0, 1))
+        h_passes(0, (2,), (2, 3))
+        h_passes(1, (2,), (2, 3))
         for w in range(2):
             round_h(nc.scalar.copy, 2, w)
-        h_passes(0, (3,), (0, 1))
         multiply(0)
         multiply(1)
+        h_passes(0, (3,), (0, 1))
         round_h(nc.vector.tensor_copy, 1, 1)
         h_passes(1, (3,), (0, 1))
         for a in range(2):

@@ -18,9 +18,9 @@ P = 128
 PACK = 4
 PAIR = 2 * P
 DECAY = 0.9
-SPLITS = (96, 72)
-ROW_PAIR_SPLITS = ((84, 84), (72, 80))
-AM_LOADS = ((0, 0, 512), (0, 512, 256), (1, 0, 512), (1, 512, 512), (0, 768, 256))
+SPLITS = (92, 92)
+ROW_PAIR_SPLITS = ((84, 84), (84, 84))
+AM_LOADS = ((0, 0, 512), (0, 512, 256), (1, 0, 256), (1, 256, 768), (0, 768, 256))
 
 
 def tile_mix_kfac_ema_kernel(tc, g, am_words, am_scales, bm_words, bm_scales, mom, out):
@@ -92,12 +92,15 @@ def tile_mix_kfac_ema_kernel(tc, g, am_words, am_scales, bm_words, bm_scales, mo
 
         g_grouped = [[alloc("g_grouped%d%d" % (a, w), [P, 2, P, PACK], BF16) for w in range(2)] for a in range(2)]
 
-        def round_g(a, raw, rows, splits):
+        def round_half(a, raw, rows, w, split):
             source = raw[:].rearrange("p j (c t) -> p c j t", t=PACK)
+            target = g_grouped[a][w][:, :, :, rows].rearrange("p t c j -> p c j t")
+            nc.vector.tensor_copy(out=target[:, :split], in_=source[:, :split, :, 2 * w:2 * w + 2])
+            nc.scalar.copy(out=target[:, split:], in_=source[:, split:, :, 2 * w:2 * w + 2])
+
+        def round_g(a, raw, rows, splits):
             for w, split in enumerate(splits):
-                target = g_grouped[a][w][:, :, :, rows].rearrange("p t c j -> p c j t")
-                nc.vector.tensor_copy(out=target[:, :split], in_=source[:, :split, :, 2 * w:2 * w + 2])
-                nc.scalar.copy(out=target[:, split:], in_=source[:, split:, :, 2 * w:2 * w + 2])
+                round_half(a, raw, rows, w, split)
 
         def quantise_g(a, t):
             nc.vector.quantize_mx(out=g_codes[a][:, columns(t)].bitcast(E5M2), scales=g_planes[a][:, columns(t)],
@@ -143,9 +146,10 @@ def tile_mix_kfac_ema_kernel(tc, g, am_words, am_scales, bm_words, bm_scales, mo
             quantise_h(i)
             y_pass(i)
 
-        round_g(0, g_first, slice(0, PACK), SPLITS)
-        for t in range(PACK):
-            quantise_g(0, t)
+        for w in range(2):
+            round_half(0, g_first, slice(0, PACK), w, SPLITS[w])
+            quantise_g(0, 2 * w)
+            quantise_g(0, 2 * w + 1)
         h_passes(0, (0, 1))
         for v in range(2):
             round_g(1, g_second[v], slice(2 * v, 2 * v + 2), ROW_PAIR_SPLITS[v])
@@ -156,11 +160,10 @@ def tile_mix_kfac_ema_kernel(tc, g, am_words, am_scales, bm_words, bm_scales, mo
         for u in range(2):
             round_h(nc.scalar.copy, 0, 0, slice(u, u + 1))
             round_h(nc.vector.tensor_copy, 0, 1, slice(u, u + 1))
+        h_passes(0, (2,), (2, 3))
         h_passes(1, (1,))
         round_h(nc.scalar.copy, 1, 0)
-        h_passes(1, (2,), (0, 1))
-        h_passes(0, (2,), (2, 3))
-        h_passes(1, (2,), (2, 3))
+        h_passes(1, (2,))
         for w in range(2):
             round_h(nc.scalar.copy, 2, w)
         multiply(0)

@@ -18,15 +18,22 @@ P = 128
 PACK = 4
 PAIR = 2 * P
 DECAY = 0.9
-SPLITS = (92, 92)
-ROW_PAIR_SPLITS = ((84, 84), (84, 84))
-AM_LOADS = ((0, 0, 512), (0, 512, 256), (1, 0, 256), (1, 256, 768), (0, 768, 256))
+WHOLE_SPLIT = 88
+ROW_PAIR_SPLIT = 84
+NARROW_BANKS = 4
+NATURAL = (0, 1)
+AM_LOADS = ((0, 0, 512), (1, 0, 512), (0, 512, 512), (1, 512, 512))
 
 
 def tile_mix_kfac_ema_kernel(tc, g, am_words, am_scales, bm_words, bm_scales, mom, out):
     nc = tc.nc
     am_rows = am_words.rearrange("a p m i -> p a (m i)").bitcast(I32)
     bm_rows = bm_words.rearrange("a p n i -> p (a n i)").bitcast(I32)
+    g_rows = g.rearrange("(a p j) l -> a p j l", a=2, j=PACK)
+
+    def pair_rows(matrix, q):
+        rows = matrix[PAIR * q:PAIR * (q + 1)]
+        return rows.rearrange("(u p) n -> p u n" if q in NATURAL else "(p u) n -> p u n", u=2)
 
     with ExitStack() as ctx:
         sb = ctx.enter_context(tc.tile_pool(name="sb", bufs=1))
@@ -46,84 +53,86 @@ def tile_mix_kfac_ema_kernel(tc, g, am_words, am_scales, bm_words, bm_scales, mo
         am_parts = [alloc("am_part%d" % n, [P, count], U32) for n, (a, first, count) in enumerate(AM_LOADS)]
         bm_codes = alloc("bm_codes", [P, N], U32)
         momentum = [alloc("momentum%d" % q, [P, 2, N], F32) for q in range(4)]
-        results = [alloc("result%d" % q, [P, 2, N], F32) for q in range(4)]
-        mom_rows = mom.rearrange("(q p u) n -> p q u n", p=P, u=2)
-        out_rows = out.rearrange("(q p u) n -> p q u n", p=P, u=2)
-
-        g_rows = g.rearrange("(a p j) l -> a p j l", a=2, j=PACK)
+        results = [alloc("result%d" % i, [P, N], F32) for i in range(8)]
 
         def load_am(n):
             a, first, count = AM_LOADS[n]
             nc.sync.dma_start(out=am_parts[n][:].bitcast(I32), in_=am_rows[:, a, first:first + count])
-
-        def am_columns(a, q):
-            n = [a == b and first <= PAIR * q < first + count for b, first, count in AM_LOADS].index(True)
-            offset = PAIR * q - AM_LOADS[n][1]
-            return am_parts[n][:, offset:offset + PAIR].bitcast(E4M3)
 
         def load_scales(plane, scales):
             for r in range(4):
                 nc.sync.dma_start(out=plane[r:P:32, :].bitcast(I32),
                                   in_=scales.rearrange("(q r) c -> r q c", r=4)[r].bitcast(I32))
 
-        def load_mom(q):
-            nc.sync.dma_start(out=momentum[q][:], in_=mom_rows[:, q])
-
         nc.sync.dma_start(out=g_first[:], in_=g_rows[0])
         load_scales(am_planes[0], am_scales[0])
         load_am(0)
         for v in range(2):
             nc.sync.dma_start(out=g_second[v][:], in_=g_rows[1][:, 2 * v:2 * v + 2])
-        load_am(1)
         load_scales(am_planes[1], am_scales[1])
+        load_am(1)
         load_am(2)
         load_am(3)
         nc.sync.dma_start(out=bm_codes[:].bitcast(I32), in_=bm_rows)
         load_scales(bm_plane, bm_scales[0])
-        load_am(4)
         for q in range(4):
-            load_mom(q)
+            nc.sync.dma_start(out=momentum[q][:], in_=pair_rows(mom, q))
 
         g_codes = [alloc("g_codes%d" % a, [P, L], U32) for a in range(2)]
         g_planes = [alloc("g_plane%d" % a, [P, L], U8) for a in range(2)]
+        g_grouped = [[alloc("g_grouped%d%d" % (a, w), [P, 2, P, PACK], BF16) for w in range(2)] for a in range(2)]
 
         def columns(j):
             return slice(P * j, P * (j + 1))
 
-        g_grouped = [[alloc("g_grouped%d%d" % (a, w), [P, 2, P, PACK], BF16) for w in range(2)] for a in range(2)]
-
-        def round_half(a, raw, rows, w, split):
+        def round_g(a, raw, rows, w, split):
             source = raw[:].rearrange("p j (c t) -> p c j t", t=PACK)
             target = g_grouped[a][w][:, :, :, rows].rearrange("p t c j -> p c j t")
             nc.vector.tensor_copy(out=target[:, :split], in_=source[:, :split, :, 2 * w:2 * w + 2])
             nc.scalar.copy(out=target[:, split:], in_=source[:, split:, :, 2 * w:2 * w + 2])
 
-        def round_g(a, raw, rows, splits):
-            for w, split in enumerate(splits):
-                round_half(a, raw, rows, w, split)
-
         def quantise_g(a, t):
             nc.vector.quantize_mx(out=g_codes[a][:, columns(t)].bitcast(E5M2), scales=g_planes[a][:, columns(t)],
                                   in_=g_grouped[a][t // 2][:, t % 2].rearrange("p c j -> p (c j)"))
 
-        h_acc = [ps.tile([P, 2, PAIR], F32, name="h%d" % i, tag="bank%d" % i) for i in range(8)]
+        narrow = [ps.tile([P, PACK, P], F32, name="h%d" % b, tag="bank%d" % b) for b in range(NARROW_BANKS)]
+        wide = {b: ps.tile([P, 2, PAIR], F32, name="h%d" % b, tag="bank%d" % b) for b in range(NARROW_BANKS, 8)}
 
-        def h_passes(a, pairs, slots=range(PACK)):
-            for t in slots:
-                for q in pairs:
-                    nc.tensor.matmul_mx(out=h_acc[2 * q + t // 2][:, t % 2, :], lhsT=g_codes[a][:, columns(t)].bitcast(E5M2),
-                                        lhsT_scale=g_planes[a][:, columns(t)],
-                                        rhs=am_columns(a, q), rhs_scale=am_planes[a][:, PAIR * q:PAIR * (q + 1)],
-                                        start=(a == 0 and t % 2 == 0), stop=(a == 1 and t % 2 == 1))
+        def h_pass(target, a, t, first, width, start, stop):
+            n = [a == b and lo <= first < lo + count for b, lo, count in AM_LOADS].index(True)
+            offset = first - AM_LOADS[n][1]
+            nc.tensor.matmul_mx(out=target, lhsT=g_codes[a][:, columns(t)].bitcast(E5M2), lhsT_scale=g_planes[a][:, columns(t)],
+                                rhs=am_parts[n][:, offset:offset + width].bitcast(E4M3),
+                                rhs_scale=am_planes[a][:, first:first + width], start=start, stop=stop)
+
+        def narrow_passes(a, banks):
+            for t in range(PACK):
+                for b in banks:
+                    h_pass(narrow[b][:, t], a, t, P * b, P, a == 0 and t == 0, a == 1 and t == PACK - 1)
+
+        def wide_passes(a, banks):
+            for b in banks:
+                for e in range(2):
+                    h_pass(wide[b][:, e], a, 2 * (b % 2) + e, PAIR * (b // 2), PAIR, a == 0 and e == 0, a == 1 and e == 1)
 
         h_grouped = [alloc("h_grouped%d" % q, [P, 2, P, PACK], BF16) for q in range(4)]
         h_codes = [alloc("h_codes%d" % i, [P, P], U32) for i in range(8)]
         h_planes = [alloc("h_plane%d" % i, [P, P], U8) for i in range(8)]
         y_acc = {}
 
-        def round_h(copy, q, w, tiles=slice(0, 2)):
-            copy(out=h_grouped[q][:, tiles, :, 2 * w:2 * w + 2].rearrange("p u c t -> p c u t"),
-                 in_=h_acc[2 * q + w][:].rearrange("p t (c u) -> p c u t", u=2)[:, :, tiles])
+        def round_narrow(copy, b, part=slice(0, P // 2)):
+            copy(out=h_grouped[b // 2][:, b % 2].rearrange("p (c e) t -> p c t e", e=2)[:, part],
+                 in_=narrow[b][:].rearrange("p t (c e) -> p c t e", e=2)[:, part])
+
+        def round_wide(copy, b, part=slice(0, PAIR)):
+            q, w = divmod(b, 2)
+            words = h_grouped[q][:, :, :, 2 * w:2 * w + 2]
+            if q in NATURAL:
+                copy(out=words.rearrange("p u c t -> p (u c) t")[:, part], in_=wide[b][:].rearrange("p t m -> p m t")[:, part])
+            else:
+                rows = slice(part.start // 2, part.stop // 2)
+                copy(out=words.rearrange("p u c t -> p c u t")[:, rows],
+                     in_=wide[b][:].rearrange("p t (c u) -> p c u t", u=2)[:, rows])
 
         def quantise_h(i):
             nc.vector.quantize_mx(out=h_codes[i][:].bitcast(E5M2), scales=h_planes[i][:],
@@ -135,54 +144,59 @@ def tile_mix_kfac_ema_kernel(tc, g, am_words, am_scales, bm_words, bm_scales, mo
                                 rhs=bm_codes[:].bitcast(E4M3), rhs_scale=bm_plane[:], start=True, stop=True)
 
         def finish(i):
-            nc.vector.scalar_tensor_tensor(out=results[i // 2][:, i % 2], in0=momentum[i // 2][:, i % 2], scalar=DECAY,
+            nc.vector.scalar_tensor_tensor(out=results[i][:], in0=momentum[i // 2][:, i % 2], scalar=DECAY,
                                            in1=y_acc[i][:], op0=ALU.mult, op1=ALU.add)
-            if i == 1:
-                nc.sync.dma_start(out=out_rows[:, 0], in_=results[0][:])
-            elif i > 1:
-                nc.sync.dma_start(out=out_rows[:, i // 2, i % 2], in_=results[i // 2][:, i % 2])
+            nc.sync.dma_start(out=pair_rows(out, i // 2)[:, i % 2], in_=results[i][:])
 
         def multiply(i):
             quantise_h(i)
             y_pass(i)
 
+        V = nc.vector.tensor_copy
+        S = nc.scalar.copy
         for w in range(2):
-            round_half(0, g_first, slice(0, PACK), w, SPLITS[w])
+            round_g(0, g_first, slice(0, PACK), w, WHOLE_SPLIT)
             quantise_g(0, 2 * w)
             quantise_g(0, 2 * w + 1)
-        h_passes(0, (0, 1))
+        narrow_passes(0, range(4))
         for v in range(2):
-            round_g(1, g_second[v], slice(2 * v, 2 * v + 2), ROW_PAIR_SPLITS[v])
+            for w in range(2):
+                round_g(1, g_second[v], slice(2 * v, 2 * v + 2), w, ROW_PAIR_SPLIT)
         for t in range(PACK):
             quantise_g(1, t)
-        h_passes(0, (2,), (0, 1))
-        h_passes(1, (0,))
-        for u in range(2):
-            round_h(nc.scalar.copy, 0, 0, slice(u, u + 1))
-            round_h(nc.vector.tensor_copy, 0, 1, slice(u, u + 1))
-        h_passes(0, (2,), (2, 3))
-        h_passes(1, (1,))
-        round_h(nc.scalar.copy, 1, 0)
-        h_passes(1, (2,))
-        for w in range(2):
-            round_h(nc.scalar.copy, 2, w)
+        narrow_passes(1, (0, 1))
+        narrow_passes(1, (2, 3))
+        for b in (4, 5):
+            for a in range(2):
+                wide_passes(a, (b,))
+        round_narrow(V, 0)
+        round_narrow(S, 1)
+        round_narrow(S, 3)
+        round_wide(S, 4)
+        round_wide(S, 5)
+        round_narrow(V, 2, slice(0, 32))
         multiply(0)
-        multiply(1)
-        h_passes(0, (3,), (0, 1))
-        round_h(nc.vector.tensor_copy, 1, 1)
-        h_passes(1, (3,), (0, 1))
+        quantise_h(1)
+        round_narrow(V, 2, slice(32, 64))
         for a in range(2):
-            h_passes(a, (3,), (2, 3))
-        for w in range(2):
-            round_h(nc.scalar.copy, 3, w)
-        finish(0)
+            wide_passes(a, (6,))
+        y_pass(1)
+        for a in range(2):
+            wide_passes(a, (7,))
+        for b in (6, 7):
+            round_wide(S, b)
+        quantise_h(3)
         multiply(2)
-        multiply(3)
+        y_pass(3)
+        finish(0)
         finish(1)
-        for q in (2, 3):
-            multiply(2 * q)
-            multiply(2 * q + 1)
-            finish(2 * q - 2)
-            finish(2 * q - 1)
+        multiply(4)
+        multiply(5)
+        finish(2)
+        finish(3)
+        multiply(6)
+        finish(4)
+        multiply(7)
+        finish(5)
         finish(6)
         finish(7)

@@ -18,22 +18,16 @@ P = 128
 PACK = 4
 PAIR = 2 * P
 DECAY = 0.9
-WHOLE_SPLIT = 88
-ROW_PAIR_SPLIT = 84
-NARROW_BANKS = 4
-NATURAL = (0, 1)
-AM_LOADS = ((0, 0, 512), (1, 0, 512), (0, 512, 512), (1, 512, 512))
+SPLITS = (92, 92)
+ROW_PAIR_SPLITS = ((84, 84), (84, 84))
+NATURAL = (0, 1, 2, 3)
+AM_LOADS = ((0, 0, 512), (1, 0, 512))
 
 
 def tile_mix_kfac_ema_kernel(tc, g, am_words, am_scales, bm_words, bm_scales, mom, out):
     nc = tc.nc
     am_rows = am_words.rearrange("a p m i -> p a (m i)").bitcast(I32)
     bm_rows = bm_words.rearrange("a p n i -> p (a n i)").bitcast(I32)
-    g_rows = g.rearrange("(a p j) l -> a p j l", a=2, j=PACK)
-
-    def pair_rows(matrix, q):
-        rows = matrix[PAIR * q:PAIR * (q + 1)]
-        return rows.rearrange("(u p) n -> p u n" if q in NATURAL else "(p u) n -> p u n", u=2)
 
     with ExitStack() as ctx:
         sb = ctx.enter_context(tc.tile_pool(name="sb", bufs=1))
@@ -51,18 +45,35 @@ def tile_mix_kfac_ema_kernel(tc, g, am_words, am_scales, bm_words, bm_scales, mo
         g_first = alloc("g_first", [P, PACK, L], F32)
         g_second = [alloc("g_second%d" % v, [P, 2, L], F32) for v in range(2)]
         am_parts = [alloc("am_part%d" % n, [P, count], U32) for n, (a, first, count) in enumerate(AM_LOADS)]
+        am_late = alloc("am_late", [P, 2, M // 2], U32)
         bm_codes = alloc("bm_codes", [P, N], U32)
-        momentum = [alloc("momentum%d" % q, [P, 2, N], F32) for q in range(4)]
-        results = [alloc("result%d" % i, [P, N], F32) for i in range(8)]
+        first_momentum = [alloc("first_momentum%d" % u, [P, N], F32) for u in range(2)]
+        momentum = {q: alloc("momentum%d" % q, [P, 2, N], F32) for q in range(1, 4)}
+        results = [alloc("result%d" % q, [P, 2, N], F32) for q in range(4)]
+        def pair_rows(matrix, q):
+            rows = matrix[PAIR * q:PAIR * (q + 1)]
+            return rows.rearrange("(u p) n -> p u n" if q in NATURAL else "(p u) n -> p u n", u=2)
+
+        g_rows = g.rearrange("(a p j) l -> a p j l", a=2, j=PACK)
 
         def load_am(n):
             a, first, count = AM_LOADS[n]
             nc.sync.dma_start(out=am_parts[n][:].bitcast(I32), in_=am_rows[:, a, first:first + count])
 
+        def am_columns(a, q):
+            if q >= 2:
+                return am_late[:, a, PAIR * (q - 2):PAIR * (q - 1)].bitcast(E4M3)
+            n = [a == b and first <= PAIR * q < first + count for b, first, count in AM_LOADS].index(True)
+            offset = PAIR * q - AM_LOADS[n][1]
+            return am_parts[n][:, offset:offset + PAIR].bitcast(E4M3)
+
         def load_scales(plane, scales):
             for r in range(4):
                 nc.sync.dma_start(out=plane[r:P:32, :].bitcast(I32),
                                   in_=scales.rearrange("(q r) c -> r q c", r=4)[r].bitcast(I32))
+
+        def load_mom(q):
+            nc.sync.dma_start(out=momentum[q][:], in_=pair_rows(mom, q))
 
         nc.sync.dma_start(out=g_first[:], in_=g_rows[0])
         load_scales(am_planes[0], am_scales[0])
@@ -71,68 +82,70 @@ def tile_mix_kfac_ema_kernel(tc, g, am_words, am_scales, bm_words, bm_scales, mo
             nc.sync.dma_start(out=g_second[v][:], in_=g_rows[1][:, 2 * v:2 * v + 2])
         load_scales(am_planes[1], am_scales[1])
         load_am(1)
-        load_am(2)
-        load_am(3)
+        nc.sync.dma_start(out=am_late[:].bitcast(I32), in_=am_rows[:, :, M // 2:])
         nc.sync.dma_start(out=bm_codes[:].bitcast(I32), in_=bm_rows)
         load_scales(bm_plane, bm_scales[0])
-        for q in range(4):
-            nc.sync.dma_start(out=momentum[q][:], in_=pair_rows(mom, q))
+        for i in range(2):
+            nc.sync.dma_start(out=first_momentum[i][:], in_=pair_rows(mom, i // 2)[:, i % 2])
+        for q in range(1, 4):
+            load_mom(q)
 
         g_codes = [alloc("g_codes%d" % a, [P, L], U32) for a in range(2)]
         g_planes = [alloc("g_plane%d" % a, [P, L], U8) for a in range(2)]
-        g_grouped = [[alloc("g_grouped%d%d" % (a, w), [P, 2, P, PACK], BF16) for w in range(2)] for a in range(2)]
 
         def columns(j):
             return slice(P * j, P * (j + 1))
 
-        def round_g(a, raw, rows, w, split):
+        g_grouped = [[alloc("g_grouped%d%d" % (a, w), [P, 2, P, PACK], BF16) for w in range(2)] for a in range(2)]
+
+        def round_half(a, raw, rows, w, split):
             source = raw[:].rearrange("p j (c t) -> p c j t", t=PACK)
             target = g_grouped[a][w][:, :, :, rows].rearrange("p t c j -> p c j t")
             nc.vector.tensor_copy(out=target[:, :split], in_=source[:, :split, :, 2 * w:2 * w + 2])
             nc.scalar.copy(out=target[:, split:], in_=source[:, split:, :, 2 * w:2 * w + 2])
 
+        def round_g(a, raw, rows, splits):
+            for w, split in enumerate(splits):
+                round_half(a, raw, rows, w, split)
+
         def quantise_g(a, t):
             nc.vector.quantize_mx(out=g_codes[a][:, columns(t)].bitcast(E5M2), scales=g_planes[a][:, columns(t)],
                                   in_=g_grouped[a][t // 2][:, t % 2].rearrange("p c j -> p (c j)"))
 
-        narrow = [ps.tile([P, PACK, P], F32, name="h%d" % b, tag="bank%d" % b) for b in range(NARROW_BANKS)]
-        wide = {b: ps.tile([P, 2, PAIR], F32, name="h%d" % b, tag="bank%d" % b) for b in range(NARROW_BANKS, 8)}
+        h_acc = [ps.tile([P, PACK, P] if i in (4, 5) else [P, 2, PAIR], F32, name="h%d" % i, tag="bank%d" % i) for i in range(8)]
 
-        def h_pass(target, a, t, first, width, start, stop):
-            n = [a == b and lo <= first < lo + count for b, lo, count in AM_LOADS].index(True)
-            offset = first - AM_LOADS[n][1]
-            nc.tensor.matmul_mx(out=target, lhsT=g_codes[a][:, columns(t)].bitcast(E5M2), lhsT_scale=g_planes[a][:, columns(t)],
-                                rhs=am_parts[n][:, offset:offset + width].bitcast(E4M3),
-                                rhs_scale=am_planes[a][:, first:first + width], start=start, stop=stop)
-
-        def narrow_passes(a, banks):
+        def narrow_passes(a, i):
             for t in range(PACK):
-                for b in banks:
-                    h_pass(narrow[b][:, t], a, t, P * b, P, a == 0 and t == 0, a == 1 and t == PACK - 1)
+                nc.tensor.matmul_mx(out=h_acc[i][:, t], lhsT=g_codes[a][:, columns(t)].bitcast(E5M2), lhsT_scale=g_planes[a][:, columns(t)],
+                                    rhs=am_columns(a, i // 2)[:, columns(i % 2)], rhs_scale=am_planes[a][:, columns(i)],
+                                    start=(a == 0 and t == 0), stop=(a == 1 and t == PACK - 1))
 
-        def wide_passes(a, banks):
-            for b in banks:
-                for e in range(2):
-                    h_pass(wide[b][:, e], a, 2 * (b % 2) + e, PAIR * (b // 2), PAIR, a == 0 and e == 0, a == 1 and e == 1)
+        def round_narrow(copy, i):
+            copy(out=h_grouped[i // 2][:, i % 2].rearrange("p (c e) t -> p c t e", e=2),
+                 in_=h_acc[i][:].rearrange("p t (c e) -> p c t e", e=2))
+
+        def h_passes(a, pairs, slots=range(PACK)):
+            for t in slots:
+                for q in pairs:
+                    nc.tensor.matmul_mx(out=h_acc[2 * q + t // 2][:, t % 2, :], lhsT=g_codes[a][:, columns(t)].bitcast(E5M2),
+                                        lhsT_scale=g_planes[a][:, columns(t)],
+                                        rhs=am_columns(a, q), rhs_scale=am_planes[a][:, PAIR * q:PAIR * (q + 1)],
+                                        start=(a == 0 and t % 2 == 0), stop=(a == 1 and t % 2 == 1))
 
         h_grouped = [alloc("h_grouped%d" % q, [P, 2, P, PACK], BF16) for q in range(4)]
         h_codes = [alloc("h_codes%d" % i, [P, P], U32) for i in range(8)]
         h_planes = [alloc("h_plane%d" % i, [P, P], U8) for i in range(8)]
         y_acc = {}
 
-        def round_narrow(copy, b, part=slice(0, P // 2)):
-            copy(out=h_grouped[b // 2][:, b % 2].rearrange("p (c e) t -> p c t e", e=2)[:, part],
-                 in_=narrow[b][:].rearrange("p t (c e) -> p c t e", e=2)[:, part])
-
-        def round_wide(copy, b, part=slice(0, PAIR)):
-            q, w = divmod(b, 2)
+        def round_h(copy, q, w, part=slice(0, PAIR)):
             words = h_grouped[q][:, :, :, 2 * w:2 * w + 2]
+            sums = h_acc[2 * q + w][:]
             if q in NATURAL:
-                copy(out=words.rearrange("p u c t -> p (u c) t")[:, part], in_=wide[b][:].rearrange("p t m -> p m t")[:, part])
+                copy(out=words.rearrange("p u c t -> p (u c) t")[:, part], in_=sums.rearrange("p t m -> p m t")[:, part])
             else:
                 rows = slice(part.start // 2, part.stop // 2)
                 copy(out=words.rearrange("p u c t -> p c u t")[:, rows],
-                     in_=wide[b][:].rearrange("p t (c u) -> p c u t", u=2)[:, rows])
+                     in_=sums.rearrange("p t (c u) -> p c u t", u=2)[:, rows])
 
         def quantise_h(i):
             nc.vector.quantize_mx(out=h_codes[i][:].bitcast(E5M2), scales=h_planes[i][:],
@@ -144,51 +157,52 @@ def tile_mix_kfac_ema_kernel(tc, g, am_words, am_scales, bm_words, bm_scales, mo
                                 rhs=bm_codes[:].bitcast(E4M3), rhs_scale=bm_plane[:], start=True, stop=True)
 
         def finish(i):
-            nc.vector.scalar_tensor_tensor(out=results[i][:], in0=momentum[i // 2][:, i % 2], scalar=DECAY,
+            nc.vector.scalar_tensor_tensor(out=results[i // 2][:, i % 2], in0=momentum[i // 2][:, i % 2] if i > 1 else first_momentum[i][:],
+                                           scalar=DECAY,
                                            in1=y_acc[i][:], op0=ALU.mult, op1=ALU.add)
-            nc.sync.dma_start(out=pair_rows(out, i // 2)[:, i % 2], in_=results[i][:])
+            nc.sync.dma_start(out=pair_rows(out, i // 2)[:, i % 2], in_=results[i // 2][:, i % 2])
 
         def multiply(i):
             quantise_h(i)
             y_pass(i)
 
-        V = nc.vector.tensor_copy
-        S = nc.scalar.copy
         for w in range(2):
-            round_g(0, g_first, slice(0, PACK), w, WHOLE_SPLIT)
+            round_half(0, g_first, slice(0, PACK), w, SPLITS[w])
             quantise_g(0, 2 * w)
             quantise_g(0, 2 * w + 1)
-        narrow_passes(0, range(4))
+        h_passes(0, (0, 1))
         for v in range(2):
-            for w in range(2):
-                round_g(1, g_second[v], slice(2 * v, 2 * v + 2), w, ROW_PAIR_SPLIT)
+            round_g(1, g_second[v], slice(2 * v, 2 * v + 2), ROW_PAIR_SPLITS[v])
         for t in range(PACK):
             quantise_g(1, t)
-        narrow_passes(1, (0, 1))
-        narrow_passes(1, (2, 3))
-        for b in (4, 5):
+        h_passes(1, (0,))
+        h_passes(1, (1,))
+        V = nc.vector.tensor_copy
+        S = nc.scalar.copy
+        round_h(V, 0, 0)
+        round_h(S, 0, 1, columns(0))
+        round_h(S, 0, 1, columns(1))
+        round_h(V, 1, 0, columns(0))
+        for i in (4, 5):
             for a in range(2):
-                wide_passes(a, (b,))
-        round_narrow(V, 0)
-        round_narrow(S, 1)
-        round_narrow(S, 3)
-        round_wide(S, 4)
-        round_wide(S, 5)
-        round_narrow(V, 2, slice(0, 32))
+                narrow_passes(a, i)
         multiply(0)
-        quantise_h(1)
-        round_narrow(V, 2, slice(32, 64))
-        for a in range(2):
-            wide_passes(a, (6,))
-        y_pass(1)
-        for a in range(2):
-            wide_passes(a, (7,))
-        for b in (6, 7):
-            round_wide(S, b)
-        quantise_h(3)
+        round_h(V, 1, 0, columns(1))
+        h_passes(0, (3,), (0, 1))
+        multiply(1)
+        h_passes(1, (3,), (0, 1))
+        h_passes(0, (3,), (2, 3))
+        round_h(S, 1, 1, columns(0))
         multiply(2)
-        y_pass(3)
+        h_passes(1, (3,), (2, 3))
+        round_h(S, 1, 1, columns(1))
+        for i in (4, 5):
+            round_narrow(S, i)
+        round_h(S, 3, 0)
+        for u in range(2):
+            round_h(S, 3, 1, columns(u))
         finish(0)
+        multiply(3)
         finish(1)
         multiply(4)
         multiply(5)

@@ -21,7 +21,8 @@ DECAY = 0.9
 SPLITS = (92, 92)
 ROW_PAIR_SPLITS = ((84, 84), (84, 84))
 NATURAL = (0, 1, 2, 3)
-AM_LOADS = ((0, 0, 512), (1, 0, 512))
+MOM_LOADS = ((0, 1), (1, 2), (3, 2), (5, 3))
+AM_LOADS = ((0, 0, 512), (0, 768, 256), (1, 0, 256), (1, 256, 768), (0, 512, 256))
 
 
 def tile_mix_kfac_ema_kernel(tc, g, am_words, am_scales, bm_words, bm_scales, mom, out):
@@ -45,10 +46,9 @@ def tile_mix_kfac_ema_kernel(tc, g, am_words, am_scales, bm_words, bm_scales, mo
         g_first = alloc("g_first", [P, PACK, L], F32)
         g_second = [alloc("g_second%d" % v, [P, 2, L], F32) for v in range(2)]
         am_parts = [alloc("am_part%d" % n, [P, count], U32) for n, (a, first, count) in enumerate(AM_LOADS)]
-        am_late = alloc("am_late", [P, 2, M // 2], U32)
         bm_codes = alloc("bm_codes", [P, N], U32)
-        first_momentum = [alloc("first_momentum%d" % u, [P, N], F32) for u in range(2)]
-        momentum = {q: alloc("momentum%d" % q, [P, 2, N], F32) for q in range(1, 4)}
+        mom_parts = [alloc("mom_part%d" % n, [P, count, N], F32) for n, (first, count) in enumerate(MOM_LOADS)]
+        momentum = [part[:, j] for part, (first, count) in zip(mom_parts, MOM_LOADS) for j in range(count)]
         results = [alloc("result%d" % q, [P, 2, N], F32) for q in range(4)]
         def pair_rows(matrix, q):
             rows = matrix[PAIR * q:PAIR * (q + 1)]
@@ -61,8 +61,6 @@ def tile_mix_kfac_ema_kernel(tc, g, am_words, am_scales, bm_words, bm_scales, mo
             nc.sync.dma_start(out=am_parts[n][:].bitcast(I32), in_=am_rows[:, a, first:first + count])
 
         def am_columns(a, q):
-            if q >= 2:
-                return am_late[:, a, PAIR * (q - 2):PAIR * (q - 1)].bitcast(E4M3)
             n = [a == b and first <= PAIR * q < first + count for b, first, count in AM_LOADS].index(True)
             offset = PAIR * q - AM_LOADS[n][1]
             return am_parts[n][:, offset:offset + PAIR].bitcast(E4M3)
@@ -72,23 +70,20 @@ def tile_mix_kfac_ema_kernel(tc, g, am_words, am_scales, bm_words, bm_scales, mo
                 nc.sync.dma_start(out=plane[r:P:32, :].bitcast(I32),
                                   in_=scales.rearrange("(q r) c -> r q c", r=4)[r].bitcast(I32))
 
-        def load_mom(q):
-            nc.sync.dma_start(out=momentum[q][:], in_=pair_rows(mom, q))
-
         nc.sync.dma_start(out=g_first[:], in_=g_rows[0])
         load_scales(am_planes[0], am_scales[0])
         load_am(0)
         for v in range(2):
             nc.sync.dma_start(out=g_second[v][:], in_=g_rows[1][:, 2 * v:2 * v + 2])
-        load_scales(am_planes[1], am_scales[1])
         load_am(1)
-        nc.sync.dma_start(out=am_late[:].bitcast(I32), in_=am_rows[:, :, M // 2:])
+        load_scales(am_planes[1], am_scales[1])
+        load_am(2)
+        load_am(3)
+        load_am(4)
         nc.sync.dma_start(out=bm_codes[:].bitcast(I32), in_=bm_rows)
         load_scales(bm_plane, bm_scales[0])
-        for i in range(2):
-            nc.sync.dma_start(out=first_momentum[i][:], in_=pair_rows(mom, i // 2)[:, i % 2])
-        for q in range(1, 4):
-            load_mom(q)
+        for part, (first, count) in zip(mom_parts, MOM_LOADS):
+            nc.sync.dma_start(out=part[:], in_=mom[P * first:P * (first + count)].rearrange("(j p) n -> p j n", p=P))
 
         g_codes = [alloc("g_codes%d" % a, [P, L], U32) for a in range(2)]
         g_planes = [alloc("g_plane%d" % a, [P, L], U8) for a in range(2)]
@@ -157,10 +152,12 @@ def tile_mix_kfac_ema_kernel(tc, g, am_words, am_scales, bm_words, bm_scales, mo
                                 rhs=bm_codes[:].bitcast(E4M3), rhs_scale=bm_plane[:], start=True, stop=True)
 
         def finish(i):
-            nc.vector.scalar_tensor_tensor(out=results[i // 2][:, i % 2], in0=momentum[i // 2][:, i % 2] if i > 1 else first_momentum[i][:],
-                                           scalar=DECAY,
+            nc.vector.scalar_tensor_tensor(out=results[i // 2][:, i % 2], in0=momentum[i], scalar=DECAY,
                                            in1=y_acc[i][:], op0=ALU.mult, op1=ALU.add)
-            nc.sync.dma_start(out=pair_rows(out, i // 2)[:, i % 2], in_=results[i // 2][:, i % 2])
+            if i == 1:
+                nc.sync.dma_start(out=pair_rows(out, 0), in_=results[0][:])
+            elif i > 1:
+                nc.sync.dma_start(out=pair_rows(out, i // 2)[:, i % 2], in_=results[i // 2][:, i % 2])
 
         def multiply(i):
             quantise_h(i)
@@ -175,6 +172,7 @@ def tile_mix_kfac_ema_kernel(tc, g, am_words, am_scales, bm_words, bm_scales, mo
             round_g(1, g_second[v], slice(2 * v, 2 * v + 2), ROW_PAIR_SPLITS[v])
         for t in range(PACK):
             quantise_g(1, t)
+        h_passes(0, (3,), (0, 1))
         h_passes(1, (0,))
         h_passes(1, (1,))
         V = nc.vector.tensor_copy
@@ -183,12 +181,12 @@ def tile_mix_kfac_ema_kernel(tc, g, am_words, am_scales, bm_words, bm_scales, mo
         round_h(S, 0, 1, columns(0))
         round_h(S, 0, 1, columns(1))
         round_h(V, 1, 0, columns(0))
-        for i in (4, 5):
-            for a in range(2):
-                narrow_passes(a, i)
+        for a in range(2):
+            narrow_passes(a, 4)
+        narrow_passes(0, 5)
         multiply(0)
+        narrow_passes(1, 5)
         round_h(V, 1, 0, columns(1))
-        h_passes(0, (3,), (0, 1))
         multiply(1)
         h_passes(1, (3,), (0, 1))
         h_passes(0, (3,), (2, 3))
@@ -201,10 +199,10 @@ def tile_mix_kfac_ema_kernel(tc, g, am_words, am_scales, bm_words, bm_scales, mo
         round_h(S, 3, 0)
         for u in range(2):
             round_h(S, 3, 1, columns(u))
-        finish(0)
         multiply(3)
-        finish(1)
+        finish(0)
         multiply(4)
+        finish(1)
         multiply(5)
         finish(2)
         finish(3)

@@ -20,8 +20,7 @@ PAIR = 2 * P
 DECAY = 0.9
 SPLITS = (92, 92)
 ROW_PAIR_SPLITS = ((84, 84), (84, 84))
-NATURAL = (0, 1, 2, 3)
-MOM_LOADS = ((0, 1), (1, 2), (3, 2), (5, 3))
+NATURAL = (1,)
 AM_LOADS = ((0, 0, 512), (0, 768, 256), (1, 0, 256), (1, 256, 768), (0, 512, 256))
 
 
@@ -47,8 +46,7 @@ def tile_mix_kfac_ema_kernel(tc, g, am_words, am_scales, bm_words, bm_scales, mo
         g_second = [alloc("g_second%d" % v, [P, 2, L], F32) for v in range(2)]
         am_parts = [alloc("am_part%d" % n, [P, count], U32) for n, (a, first, count) in enumerate(AM_LOADS)]
         bm_codes = alloc("bm_codes", [P, N], U32)
-        mom_parts = [alloc("mom_part%d" % n, [P, count, N], F32) for n, (first, count) in enumerate(MOM_LOADS)]
-        momentum = [part[:, j] for part, (first, count) in zip(mom_parts, MOM_LOADS) for j in range(count)]
+        momentum = [alloc("momentum%d" % q, [P, 2, N], F32) for q in range(4)]
         results = [alloc("result%d" % q, [P, 2, N], F32) for q in range(4)]
         def pair_rows(matrix, q):
             rows = matrix[PAIR * q:PAIR * (q + 1)]
@@ -82,8 +80,8 @@ def tile_mix_kfac_ema_kernel(tc, g, am_words, am_scales, bm_words, bm_scales, mo
         load_am(4)
         nc.sync.dma_start(out=bm_codes[:].bitcast(I32), in_=bm_rows)
         load_scales(bm_plane, bm_scales[0])
-        for part, (first, count) in zip(mom_parts, MOM_LOADS):
-            nc.sync.dma_start(out=part[:], in_=mom[P * first:P * (first + count)].rearrange("(j p) n -> p j n", p=P))
+        for q in range(4):
+            nc.sync.dma_start(out=momentum[q][:], in_=pair_rows(mom, q))
 
         g_codes = [alloc("g_codes%d" % a, [P, L], U32) for a in range(2)]
         g_planes = [alloc("g_plane%d" % a, [P, L], U8) for a in range(2)]
@@ -116,8 +114,9 @@ def tile_mix_kfac_ema_kernel(tc, g, am_words, am_scales, bm_words, bm_scales, mo
                                     start=(a == 0 and t == 0), stop=(a == 1 and t == PACK - 1))
 
         def round_narrow(copy, i):
-            copy(out=h_grouped[i // 2][:, i % 2].rearrange("p (c e) t -> p c t e", e=2),
-                 in_=h_acc[i][:].rearrange("p t (c e) -> p c t e", e=2))
+            half = slice(P // 2 * (i % 2), P // 2 * (i % 2 + 1))
+            copy(out=h_grouped[i // 2][:].rearrange("p u c t -> p c u t")[:, half],
+                 in_=h_acc[i][:].rearrange("p t (c u) -> p c u t", u=2))
 
         def h_passes(a, pairs, slots=range(PACK)):
             for t in slots:
@@ -132,15 +131,13 @@ def tile_mix_kfac_ema_kernel(tc, g, am_words, am_scales, bm_words, bm_scales, mo
         h_planes = [alloc("h_plane%d" % i, [P, P], U8) for i in range(8)]
         y_acc = {}
 
-        def round_h(copy, q, w, part=slice(0, PAIR)):
-            words = h_grouped[q][:, :, :, 2 * w:2 * w + 2]
+        def round_h(copy, q, w, tiles=slice(0, 2)):
+            words = h_grouped[q][:, tiles, :, 2 * w:2 * w + 2]
             sums = h_acc[2 * q + w][:]
             if q in NATURAL:
-                copy(out=words.rearrange("p u c t -> p (u c) t")[:, part], in_=sums.rearrange("p t m -> p m t")[:, part])
+                copy(out=words, in_=sums.rearrange("p t (u c) -> p u c t", u=2)[:, tiles])
             else:
-                rows = slice(part.start // 2, part.stop // 2)
-                copy(out=words.rearrange("p u c t -> p c u t")[:, rows],
-                     in_=sums.rearrange("p t (c u) -> p c u t", u=2)[:, rows])
+                copy(out=words.rearrange("p u c t -> p c u t"), in_=sums.rearrange("p t (c u) -> p c u t", u=2)[:, :, tiles])
 
         def quantise_h(i):
             nc.vector.quantize_mx(out=h_codes[i][:].bitcast(E5M2), scales=h_planes[i][:],
@@ -152,7 +149,7 @@ def tile_mix_kfac_ema_kernel(tc, g, am_words, am_scales, bm_words, bm_scales, mo
                                 rhs=bm_codes[:].bitcast(E4M3), rhs_scale=bm_plane[:], start=True, stop=True)
 
         def finish(i):
-            nc.vector.scalar_tensor_tensor(out=results[i // 2][:, i % 2], in0=momentum[i], scalar=DECAY,
+            nc.vector.scalar_tensor_tensor(out=results[i // 2][:, i % 2], in0=momentum[i // 2][:, i % 2], scalar=DECAY,
                                            in1=y_acc[i][:], op0=ALU.mult, op1=ALU.add)
             if i == 1:
                 nc.sync.dma_start(out=pair_rows(out, 0), in_=results[0][:])
@@ -178,31 +175,31 @@ def tile_mix_kfac_ema_kernel(tc, g, am_words, am_scales, bm_words, bm_scales, mo
         V = nc.vector.tensor_copy
         S = nc.scalar.copy
         round_h(V, 0, 0)
-        round_h(S, 0, 1, columns(0))
-        round_h(S, 0, 1, columns(1))
-        round_h(V, 1, 0, columns(0))
+        round_h(S, 0, 1, slice(0, 1))
+        round_h(S, 0, 1, slice(1, 2))
+        round_h(V, 1, 0, slice(0, 1))
         for a in range(2):
             narrow_passes(a, 4)
         narrow_passes(0, 5)
         multiply(0)
         narrow_passes(1, 5)
-        round_h(V, 1, 0, columns(1))
+        round_h(V, 1, 0, slice(1, 2))
         multiply(1)
         h_passes(1, (3,), (0, 1))
         h_passes(0, (3,), (2, 3))
-        round_h(S, 1, 1, columns(0))
+        round_h(S, 1, 1, slice(0, 1))
         multiply(2)
         h_passes(1, (3,), (2, 3))
-        round_h(S, 1, 1, columns(1))
+        round_h(S, 1, 1, slice(1, 2))
         for i in (4, 5):
             round_narrow(S, i)
         round_h(S, 3, 0)
         for u in range(2):
-            round_h(S, 3, 1, columns(u))
+            round_h(S, 3, 1, slice(u, u + 1))
         multiply(3)
         finish(0)
-        multiply(4)
         finish(1)
+        multiply(4)
         multiply(5)
         finish(2)
         finish(3)

from contextlib import ExitStack

import concourse.mybir as mybir

K, L, M, N = 1024, 512, 1024, 512
FLOPS = 2 * K * L * M + 2 * L * M * N

F32 = mybir.dt.float32
BF16 = mybir.dt.bfloat16
I32 = mybir.dt.int32
U32 = mybir.dt.uint32
U8 = mybir.dt.uint8
E4M3 = mybir.dt.float8_e4m3fn_x4
E5M2 = mybir.dt.float8_e5m2_x4
ALU = mybir.AluOpType

P = 128
PACK = 4
PAIR = 2 * P
DECAY = 0.9
SPLITS = (92, 92)
ROW_PAIR_SPLITS = ((84, 84), (84, 84))
NATURAL = (1,)
AM_LOADS = ((0, 0, 512), (0, 768, 256), (1, 0, 256), (1, 256, 768), (0, 512, 256))


def tile_mix_kfac_ema_kernel(tc, g, am_words, am_scales, bm_words, bm_scales, mom, out):
    nc = tc.nc
    am_rows = am_words.rearrange("a p m i -> p a (m i)").bitcast(I32)
    bm_rows = bm_words.rearrange("a p n i -> p (a n i)").bitcast(I32)

    with ExitStack() as ctx:
        sb = ctx.enter_context(tc.tile_pool(name="sb", bufs=1))
        ps = ctx.enter_context(tc.psum_pool(name="ps", bufs=1))
        ctx.enter_context(tc.manual_schedule())

        def alloc(name, shape, dtype):
            return sb.tile(shape, dtype, name=name, align_bytes=64)

        am_planes = [alloc("am_plane%d" % a, [P, M], U8) for a in range(2)]
        bm_plane = alloc("bm_plane", [P, N], U8)
        for plane in am_planes + [bm_plane]:
            nc.vector.memset(plane[:].bitcast(I32), 0)

        g_first = alloc("g_first", [P, PACK, L], F32)
        g_second = [alloc("g_second%d" % v, [P, 2, L], F32) for v in range(2)]
        am_parts = [alloc("am_part%d" % n, [P, count], U32) for n, (a, first, count) in enumerate(AM_LOADS)]
        bm_codes = alloc("bm_codes", [P, N], U32)
        momentum = [alloc("momentum%d" % q, [P, 2, N], F32) for q in range(4)]
        results = [alloc("result%d" % q, [P, 2, N], F32) for q in range(4)]
        def pair_rows(matrix, q):
            rows = matrix[PAIR * q:PAIR * (q + 1)]
            return rows.rearrange("(u p) n -> p u n" if q in NATURAL else "(p u) n -> p u n", u=2)

        g_rows = g.rearrange("(a p j) l -> a p j l", a=2, j=PACK)

        def load_am(n):
            a, first, count = AM_LOADS[n]
            nc.sync.dma_start(out=am_parts[n][:].bitcast(I32), in_=am_rows[:, a, first:first + count])

        def am_columns(a, q):
            n = [a == b and first <= PAIR * q < first + count for b, first, count in AM_LOADS].index(True)
            offset = PAIR * q - AM_LOADS[n][1]
            return am_parts[n][:, offset:offset + PAIR].bitcast(E4M3)

        def load_scales(plane, scales):
            for r in range(4):
                nc.sync.dma_start(out=plane[r:P:32, :].bitcast(I32),
                                  in_=scales.rearrange("(q r) c -> r q c", r=4)[r].bitcast(I32))

        nc.sync.dma_start(out=g_first[:], in_=g_rows[0])
        load_scales(am_planes[0], am_scales[0])
        load_am(0)
        for v in range(2):
            nc.sync.dma_start(out=g_second[v][:], in_=g_rows[1][:, 2 * v:2 * v + 2])
        load_am(1)
        load_scales(am_planes[1], am_scales[1])
        load_am(2)
        load_am(3)
        load_am(4)
        nc.sync.dma_start(out=bm_codes[:].bitcast(I32), in_=bm_rows)
        load_scales(bm_plane, bm_scales[0])
        for q in range(4):
            nc.sync.dma_start(out=momentum[q][:], in_=pair_rows(mom, q))

        g_codes = [alloc("g_codes%d" % a, [P, L], U32) for a in range(2)]
        g_planes = [alloc("g_plane%d" % a, [P, L], U8) for a in range(2)]

        def columns(j):
            return slice(P * j, P * (j + 1))

        g_grouped = [[alloc("g_grouped%d%d" % (a, w), [P, 2, P, PACK], BF16) for w in range(2)] for a in range(2)]

        def round_half(a, raw, rows, w, split):
            source = raw[:].rearrange("p j (c t) -> p c j t", t=PACK)
            target = g_grouped[a][w][:, :, :, rows].rearrange("p t c j -> p c j t")
            nc.vector.tensor_copy(out=target[:, :split], in_=source[:, :split, :, 2 * w:2 * w + 2])
            nc.scalar.copy(out=target[:, split:], in_=source[:, split:, :, 2 * w:2 * w + 2])

        def round_g(a, raw, rows, splits):
            for w, split in enumerate(splits):
                round_half(a, raw, rows, w, split)

        def quantise_g(a, t):
            nc.vector.quantize_mx(out=g_codes[a][:, columns(t)].bitcast(E5M2), scales=g_planes[a][:, columns(t)],
                                  in_=g_grouped[a][t // 2][:, t % 2].rearrange("p c j -> p (c j)"))

        h_acc = [ps.tile([P, PACK, P] if i in (4, 5) else [P, 2, PAIR], F32, name="h%d" % i, tag="bank%d" % i) for i in range(8)]

        def narrow_passes(a, i):
            for t in range(PACK):
                nc.tensor.matmul_mx(out=h_acc[i][:, t], lhsT=g_codes[a][:, columns(t)].bitcast(E5M2), lhsT_scale=g_planes[a][:, columns(t)],
                                    rhs=am_columns(a, i // 2)[:, columns(i % 2)], rhs_scale=am_planes[a][:, columns(i)],
                                    start=(a == 0 and t == 0), stop=(a == 1 and t == PACK - 1))

        def round_narrow(copy, i):
            half = slice(P // 2 * (i % 2), P // 2 * (i % 2 + 1))
            copy(out=h_grouped[i // 2][:].rearrange("p u c t -> p c u t")[:, half],
                 in_=h_acc[i][:].rearrange("p t (c u) -> p c u t", u=2))

        def h_passes(a, pairs, slots=range(PACK)):
            for t in slots:
                for q in pairs:
                    nc.tensor.matmul_mx(out=h_acc[2 * q + t // 2][:, t % 2, :], lhsT=g_codes[a][:, columns(t)].bitcast(E5M2),
                                        lhsT_scale=g_planes[a][:, columns(t)],
                                        rhs=am_columns(a, q), rhs_scale=am_planes[a][:, PAIR * q:PAIR * (q + 1)],
                                        start=(a == 0 and t % 2 == 0), stop=(a == 1 and t % 2 == 1))

        h_grouped = [alloc("h_grouped%d" % q, [P, 2, P, PACK], BF16) for q in range(4)]
        h_codes = [alloc("h_codes%d" % i, [P, P], U32) for i in range(8)]
        h_planes = [alloc("h_plane%d" % i, [P, P], U8) for i in range(8)]
        y_acc = {}

        def round_h(copy, q, w, tiles=slice(0, 2)):
            words = h_grouped[q][:, tiles, :, 2 * w:2 * w + 2]
            sums = h_acc[2 * q + w][:]
            if q in NATURAL:
                copy(out=words, in_=sums.rearrange("p t (u c) -> p u c t", u=2)[:, tiles])
            else:
                copy(out=words.rearrange("p u c t -> p c u t"), in_=sums.rearrange("p t (c u) -> p c u t", u=2)[:, :, tiles])

        def quantise_h(i):
            nc.vector.quantize_mx(out=h_codes[i][:].bitcast(E5M2), scales=h_planes[i][:],
                                  in_=h_grouped[i // 2][:, i % 2].rearrange("p m t -> p (m t)"))

        def y_pass(i):
            y_acc[i] = ps.tile([P, N], F32, name="y%d" % i, tag="bank%d" % i)
            nc.tensor.matmul_mx(out=y_acc[i][:], lhsT=h_codes[i][:].bitcast(E5M2), lhsT_scale=h_planes[i][:],
                                rhs=bm_codes[:].bitcast(E4M3), rhs_scale=bm_plane[:], start=True, stop=True)

        def finish(i):
            nc.vector.scalar_tensor_tensor(out=results[i // 2][:, i % 2], in0=momentum[i // 2][:, i % 2], scalar=DECAY,
                                           in1=y_acc[i][:], op0=ALU.mult, op1=ALU.add)
            if i == 1:
                nc.sync.dma_start(out=pair_rows(out, 0), in_=results[0][:])
            elif i > 1:
                nc.sync.dma_start(out=pair_rows(out, i // 2)[:, i % 2], in_=results[i // 2][:, i % 2])

        def multiply(i):
            quantise_h(i)
            y_pass(i)

        for w in range(2):
            round_half(0, g_first, slice(0, PACK), w, SPLITS[w])
            quantise_g(0, 2 * w)
            quantise_g(0, 2 * w + 1)
        h_passes(0, (0, 1))
        for v in range(2):
            round_g(1, g_second[v], slice(2 * v, 2 * v + 2), ROW_PAIR_SPLITS[v])
        for t in range(PACK):
            quantise_g(1, t)
        h_passes(0, (3,), (0, 1))
        h_passes(1, (0,))
        h_passes(1, (1,))
        V = nc.vector.tensor_copy
        S = nc.scalar.copy
        round_h(V, 0, 0)
        round_h(S, 0, 1, slice(0, 1))
        round_h(S, 0, 1, slice(1, 2))
        round_h(V, 1, 0, slice(0, 1))
        for a in range(2):
            narrow_passes(a, 4)
        narrow_passes(0, 5)
        multiply(0)
        narrow_passes(1, 5)
        round_h(V, 1, 0, slice(1, 2))
        multiply(1)
        h_passes(1, (3,), (0, 1))
        h_passes(0, (3,), (2, 3))
        round_h(S, 1, 1, slice(0, 1))
        multiply(2)
        h_passes(1, (3,), (2, 3))
        round_h(S, 1, 1, slice(1, 2))
        for i in (4, 5):
            round_narrow(S, i)
        round_h(S, 3, 0)
        for u in range(2):
            round_h(S, 3, 1, slice(u, u + 1))
        multiply(3)
        finish(0)
        finish(1)
        multiply(4)
        multiply(5)
        finish(2)
        finish(3)
        multiply(6)
        finish(4)
        multiply(7)
        finish(5)
        finish(6)
        finish(7)
